import numpy as np
import ml_dtypes


def mxq(x, axis, fmt="e4m3"):
    dtype, down = {"e4m3": (ml_dtypes.float8_e4m3fn, 7), "e5m2": (ml_dtypes.float8_e5m2, 14)}[fmt]
    v = np.moveaxis(np.asarray(x, np.float32).astype(ml_dtypes.bfloat16).astype(np.float64), axis, -1)
    blocks = v.reshape(v.shape[:-1] + (-1, 32))
    amax = np.abs(blocks).max(-1, keepdims=True)
    byte = np.maximum(np.where(amax > 0, np.frexp(amax)[1] - 1 + 127, 0) - down, 1)
    scale = np.exp2(byte - 127.0)
    codes = (blocks / scale).astype(np.float32).astype(dtype).astype(np.float64)
    return np.moveaxis((codes * scale).reshape(v.shape), -1, axis)


WIDE = False


def mx_kscale(k):
    if not WIDE:
        return np.ones(k)
    levels = np.array([10, -10, 5, -5, 0])
    if k % 512:
        return np.exp2(np.random.permutation(np.resize(levels, k // 32))).repeat(32)
    a = np.empty((k // 512, 16))
    for p in range(k // 512):
        a[p, :8] = np.random.permutation(np.resize(levels, 8))
        for g in range(8):
            far = levels[np.abs(levels - a[p, g]) >= 10]
            a[p, g + 8] = far[np.random.randint(len(far))]
    return np.exp2(a.ravel()).repeat(32)


def f64(x):
    return np.asarray(x).astype(np.float64)


def striped(idx):
    return np.tile(np.asarray(idx).reshape(-1, 16).T, (8, 1)).astype(np.uint16)


def unstriped(offs):
    return offs[:16].T.reshape(-1).astype(np.int64)


E2M1 = np.array([0.0, 0.5, 1.0, 1.5, 2.0, 3.0, 4.0, 6.0, -0.0, -0.5, -1.0, -1.5, -2.0, -3.0, -4.0, -6.0])


def pack_weight(w, fmt):
    k, n = w.shape
    w = f64(np.asarray(w, np.float32).astype(ml_dtypes.bfloat16)).reshape(k // 32, 32, n)
    amax = np.abs(w).max(1)
    if fmt == "e4m3":
        byte = np.frexp(amax)[1] - 1 + 127 - 7
    else:
        mant, ex = np.frexp(amax / 6.0)
        byte = np.where(mant > 0.5, ex, ex - 1) + 127
    byte = np.clip(np.where(amax > 0, byte, 1), 1, 254)
    scaled = (w * np.exp2(127.0 - byte)[:, None, :]).reshape(k, n).astype(np.float32)
    by_word = np.ascontiguousarray(scaled.reshape(k // 512, 128, 4, n).transpose(0, 1, 3, 2))
    if fmt == "e4m3":
        words = by_word.astype(ml_dtypes.float8_e4m3fn).view(np.uint8)
    else:
        c = by_word.astype(ml_dtypes.float4_e2m1fn).view(np.uint8) & 0xF
        words = (c[..., 0::2] | (c[..., 1::2] << 4)).reshape(k // 512, 128, 2 * n)
    return np.ascontiguousarray(words), np.ascontiguousarray(byte.astype(np.uint8).reshape(k // 512, 16, n))


def unpack_weight(words, scales, fmt):
    g, _, n = scales.shape
    words = np.ascontiguousarray(words).reshape(g, 128, n, -1)
    if fmt == "e4m3":
        vals = words.view(ml_dtypes.float8_e4m3fn).astype(np.float64)
    else:
        nib = np.empty((g, 128, n, 4), np.uint8)
        nib[..., 0::2] = words & 0xF
        nib[..., 1::2] = words >> 4
        vals = E2M1[nib]
    vals = vals * np.repeat(np.exp2(scales.astype(np.float64) - 127.0), 8, axis=1)[..., None]
    return vals.transpose(0, 1, 3, 2).reshape(g * 512, n)


D, T, I, J, E = 512, 2048, 512, 512, 512


def setup_inputs():
    n = np.random.standard_normal
    idx = np.random.permutation(T)[:I]
    idx2 = np.random.permutation(T)[:J]
    fd = mx_kscale(D)
    fj = mx_kscale(J)
    tj = np.ones(T)
    tj[idx2] = fj
    qpoolp = pack_weight(n((D, T)) * 0.5 / np.sqrt(D) * fd[:, None], "e4m3")
    keysp = pack_weight(n((D, T)) / fd[:, None], "e2m1")
    return {
        "qpool_words": qpoolp[0],
        "qpool_scales": qpoolp[1],
        "keys_words": keysp[0],
        "keys_scales": keysp[1],
        "vals": (n((E, T)) / tj).astype(np.float32),
        "mask": (0.5 * n((I, J))).astype(np.float32),
        "size": (np.random.uniform(0.5, 2.0, (1, J)) * fj).astype(np.float32),
        "offs": striped(idx),
        "offs2": striped(idx2),
    }


def reference(qpool_words, qpool_scales, keys_words, keys_scales, vals, mask, size, offs, offs2):
    idx = unstriped(offs)
    idx2 = unstriped(offs2)
    qpoolu = unpack_weight(qpool_words, qpool_scales, "e4m3")
    keysu = unpack_weight(keys_words, keys_scales, "e2m1")
    qpoolidxg = qpoolu[:, idx]
    keysidx2g = keysu[:, idx2]
    a = qpoolidxg.T @ keysidx2g
    s = a + f64(mask)
    p = np.exp(s - np.max(s, axis=1, keepdims=True))
    w = p * f64(size) / np.sum(p, axis=1, keepdims=True)
    wt = w.T
    vt = f64(vals)[:, idx2].T
    vtq = mxq(vt, 0, "e4m3")
    wtq = mxq(wt, 0, "e4m3")
    o = vtq.T @ wtq
    y = np.zeros((E, T))
    y[:, idx] = o
    return y

@@ -1,0 +1,217 @@
+from contextlib import ExitStack
+
+import concourse.mybir as mybir
+from concourse.masks import make_identity
+
+D, T, I, J, E = 512, 2048, 512, 512, 512
+FLOPS = 2 * D * I * J + 2 * J * E * I
+
+F32 = mybir.dt.float32
+BF16 = mybir.dt.bfloat16
+I32 = mybir.dt.int32
+U32 = mybir.dt.uint32
+U16 = mybir.dt.uint16
+U8 = mybir.dt.uint8
+FP8X4 = mybir.dt.float8_e4m3fn_x4
+FP4X4 = mybir.dt.float4_e2m1fn_x4
+ALU = mybir.AluOpType
+ACT = mybir.ActivationFunctionType
+AX = mybir.AxisListType
+
+P = 128
+PACK = 4
+TILES = 4
+HALF = 256
+WINDOWS = 3
+ON_SCALAR = (2, 3)
+
+
+def tile_attend_pickboth_kernel(tc, qpool_words, qpool_scales, keys_words, keys_scales, vals, mask, size, offs, offs2, out):
+    nc = tc.nc
+    with ExitStack() as ctx:
+        sb = ctx.enter_context(tc.tile_pool(name="sb", bufs=1))
+        ps = ctx.enter_context(tc.psum_pool(name="ps", bufs=1))
+
+        q_list = sb.tile([P, I // 16], U16, name="q_list")
+        k_list = sb.tile([P, J // 16], U16, name="k_list")
+        q_words = sb.tile([P, T], U32, name="q_words", tag="q_words", align_bytes=64)
+        k_words = sb.tile([P, T], U16, name="k_words", align_bytes=64)
+        q_bytes = sb.tile([P, T], U8, name="q_bytes", align_bytes=64)
+        k_bytes = sb.tile([P, T], U8, name="k_bytes", align_bytes=64)
+        size_col = sb.tile([P, PACK], F32, name="size_col")
+        mask_sb = [sb.tile([P, 2, J], F32, name="mask%d" % h) for h in range(2)]
+        vals_sb = [sb.tile([P, T], F32, name="vals%d" % e) for e in range(TILES)]
+        windows = [sb.tile([P, T], F32, name="window%d" % w) for w in range(WINDOWS - 1)]
+        ident = sb.tile([P, P], F32, name="ident")
+
+        nc.vector.memset(k_bytes[:].bitcast(I32), 0)
+        nc.vector.memset(q_bytes[:].bitcast(I32), 0)
+
+        def load_scale_rows(queue, plane, rows):
+            for quad in range(4):
+                queue.dma_start(
+                    out=plane[32 * quad : 32 * quad + 4, :].bitcast(I32),
+                    in_=rows[0, 4 * quad : 4 * quad + 4, :].bitcast(I32),
+                )
+
+        nc.sync.dma_start(k_list[:], offs2)
+        nc.sync.dma_start(out=k_words[:].bitcast(I32), in_=keys_words[0].bitcast(I32))
+        nc.sync.dma_start(q_list[:], offs)
+        load_scale_rows(nc.sync, k_bytes, keys_scales)
+        nc.sync.dma_start(out=q_words[:].bitcast(I32), in_=qpool_words[0].rearrange("p n t -> p (n t)").bitcast(I32))
+        load_scale_rows(nc.sync, q_bytes, qpool_scales)
+        nc.sync.dma_start(out=mask_sb[0][:], in_=mask[0:HALF, :].rearrange("(a p) j -> p a j", p=P))
+        nc.sync.dma_start(out=size_col[:], in_=size.rearrange("o (p c) -> p (o c)", c=PACK))
+        nc.sync.dma_start(out=mask_sb[1][:], in_=mask[HALF:I, :].rearrange("(a p) j -> p a j", p=P))
+        for e in range(TILES):
+            nc.sync.dma_start(out=vals_sb[e][:], in_=vals[e * P : (e + 1) * P, :])
+
+        make_identity(nc, ident[:])
+        for window in windows:
+            nc.vector.memset(window[:], 0.0)
+
+        size_ps = ps.tile([P, PACK, P], F32, name="size_ps")
+        for c in range(PACK):
+            nc.tensor.transpose(size_ps[:, c, :], size_col[:, c : c + 1].to_broadcast([P, P]), ident[:])
+
+        k_codes = sb.tile([P, J], U16, name="k_codes", align_bytes=64)
+        k_scale = sb.tile([P, J], U8, name="k_scale", align_bytes=64)
+        q_codes = sb.tile([P, I], U32, name="q_codes", align_bytes=64)
+        q_scale = sb.tile([P, I], U8, name="q_scale", align_bytes=64)
+        nc.vector.tensor_copy(k_codes[:], k_words[:].indirect(k_list[:]))
+        nc.vector.tensor_copy(k_scale[:], k_bytes[:].indirect(k_list[:]))
+
+        scores = [ps.tile([P, J], F32, name="scores%d" % b) for b in range(3)]
+
+        def gather_queries(h):
+            cols = slice(h * HALF, (h + 1) * HALF)
+            entries = q_list[:, h * HALF // 16 : (h + 1) * HALF // 16]
+            nc.vector.tensor_copy(q_codes[:, cols], q_words[:].indirect(entries))
+            nc.vector.tensor_copy(q_scale[:, cols], q_bytes[:].indirect(entries))
+
+        def score(i):
+            cols = slice(i * P, (i + 1) * P)
+            nc.tensor.matmul_mx(
+                out=scores[i % 3][:],
+                lhsT=q_codes[:, cols].bitcast(FP8X4),
+                lhsT_scale=q_scale[:, cols],
+                rhs=k_codes[:].bitcast(FP4X4),
+                rhs_scale=k_scale[:],
+                start=True,
+                stop=True,
+            )
+
+        s_sb = [sb.tile([P, J], F32, name="s%d" % i) for i in range(TILES)]
+        p_sb = [sb.tile([P, J], F32, name="p%d" % i) for i in range(TILES)]
+        w_sb = [sb.tile([P, J], BF16, name="w%d" % i, align_bytes=64) for i in range(TILES)]
+        neg_max = [sb.tile([P, 1], F32, name="neg_max%d" % i) for i in range(TILES)]
+        row_sum = [sb.tile([P, 1], F32, name="row_sum%d" % i) for i in range(TILES)]
+        inv_sum = [sb.tile([P, 1], F32, name="inv_sum%d" % i) for i in range(TILES)]
+        turn_ps = [ps.tile([P, 2, P], F32, name="turn%d" % b) for b in range(2)]
+        o_ps = [ps.tile([P, I], F32, name="o_ps%d" % b) for b in range(2)]
+        w_grouped = sb.tile([P, I * PACK], BF16, name="w_grouped", align_bytes=64)
+        w_codes = sb.tile([P, I], U32, name="w_codes", align_bytes=64)
+        w_scale = sb.tile([P, I], U8, name="w_scale", align_bytes=64)
+
+        def exponentials(i):
+            nc.vector.tensor_tensor(s_sb[i][:], scores[i % 3][:], mask_sb[i // 2][:, i % 2, :], ALU.add)
+            nc.vector.tensor_reduce(neg_max[i][:], s_sb[i][:], AX.X, ALU.max, negate=True)
+            nc.scalar.activation(p_sb[i][:], s_sb[i][:], ACT.Exp, bias=neg_max[i][:], accum_out=row_sum[i][:])
+
+        def turn(rows, bank, grouped):
+            words = rows.bitcast(F32)
+            for u in range(2):
+                nc.tensor.transpose(bank[:, u, :], words[:, u : J // 2 : 2], ident[:])
+            nc.scalar.copy(grouped.bitcast(F32).rearrange("p (r u) -> p r u", u=2), bank[:].rearrange("p u r -> p r u"))
+
+        def weights(i):
+            nc.vector.reciprocal(inv_sum[i][:], row_sum[i][:])
+            nc.vector.scalar_tensor_tensor(
+                w_sb[i][:].rearrange("m (p c) -> m p c", c=PACK),
+                p_sb[i][:].rearrange("m (p c) -> m p c", c=PACK),
+                inv_sum[i][:],
+                size_ps[:].rearrange("m c p -> m p c"),
+                ALU.mult,
+                ALU.mult,
+            )
+            turn(w_sb[i][:], turn_ps[i % 2], w_grouped[:, i * P * PACK : (i + 1) * P * PACK])
+
+        def quantise_weights(h):
+            cols = slice(h * HALF, (h + 1) * HALF)
+            nc.vector.quantize_mx(
+                out=w_codes[:, cols].bitcast(FP8X4),
+                scales=w_scale[:, cols],
+                in_=w_grouped[:, h * HALF * PACK : (h + 1) * HALF * PACK],
+            )
+
+        v_rows = [sb.tile([P, J], BF16, name="v_rows%d" % e, align_bytes=64) for e in range(TILES)]
+        v_grouped = [sb.tile([P, P * PACK], BF16, name="v_grouped%d" % e, align_bytes=64) for e in range(TILES)]
+        v_codes = [sb.tile([P, P], U32, name="v_codes%d" % e, align_bytes=64) for e in range(TILES)]
+        v_scale = [sb.tile([P, P], U8, name="v_scale%d" % e, align_bytes=64) for e in range(TILES)]
+        o_sb = [sb.tile([P, I], F32, name="o_sb%d" % e) for e in range(TILES)]
+
+        def gather_values(e):
+            if e in ON_SCALAR:
+                rounded = sb.tile([P, T], BF16, name="rounded%d" % e)
+                for c in range(4):
+                    cols = slice(c * T // 4, (c + 1) * T // 4)
+                    nc.scalar.activation(rounded[:, cols], vals_sb[e][:, cols], ACT.Copy)
+                nc.scalar.activation(v_rows[e][:], rounded[:].indirect(k_list[:]), ACT.Copy)
+            else:
+                nc.vector.tensor_copy(v_rows[e][:], vals_sb[e][:].indirect(k_list[:]))
+            turn(v_rows[e][:], turn_ps[e % 2], v_grouped[e][:])
+
+        def quantise_values(e):
+            nc.vector.quantize_mx(out=v_codes[e][:].bitcast(FP8X4), scales=v_scale[e][:], in_=v_grouped[e][:])
+
+        def product(e):
+            nc.tensor.matmul_mx(
+                out=o_ps[e % 2][:],
+                lhsT=v_codes[e][:].bitcast(FP8X4),
+                lhsT_scale=v_scale[e][:],
+                rhs=w_codes[:].bitcast(FP8X4),
+                rhs_scale=w_scale[:],
+                start=True,
+                stop=True,
+            )
+            nc.scalar.copy(o_sb[e][:], o_ps[e % 2][:])
+
+        def scatter(e):
+            window = windows[e % WINDOWS]
+            nc.vector.tensor_copy(window[:].indirect(q_list[:]), o_sb[e][:])
+            nc.sync.dma_start(out=out[e * P : (e + 1) * P, :], in_=window[:])
+
+        gather_queries(0)
+        score(0)
+        score(1)
+        gather_queries(1)
+        windows.append(sb.tile([P, T], F32, name="last_window", tag="q_words", align_bytes=64))
+        nc.gpsimd.memset(windows[-1][:], 0.0)
+        score(2)
+        exponentials(0)
+        score(3)
+        exponentials(1)
+        weights(0)
+        exponentials(2)
+        weights(1)
+        exponentials(3)
+        weights(2)
+        gather_values(0)
+        weights(3)
+        quantise_weights(0)
+        quantise_values(0)
+        quantise_weights(1)
+        product(0)
+        gather_values(1)
+        quantise_values(1)
+        product(1)
+        scatter(0)
+        gather_values(2)
+        quantise_values(2)
+        product(2)
+        scatter(1)
+        gather_values(3)
+        quantise_values(3)
+        product(3)
+        scatter(2)
+        scatter(3)

@@ -32,24 +32,29 @@ def tile_attend_pickboth_kernel(tc, qpool_words, qpool_scales, keys_words, keys_
         sb = ctx.enter_context(tc.tile_pool(name="sb", bufs=1))
         ps = ctx.enter_context(tc.psum_pool(name="ps", bufs=1))
 
+        def tile(shape, dtype, name, on=None):
+            return sb.tile(shape, dtype, name=name, tag=on or name, align_bytes=64)
+
         q_list = sb.tile([P, I // 16], U16, name="q_list")
         k_list = sb.tile([P, J // 16], U16, name="k_list")
-        q_words = sb.tile([P, T], U32, name="q_words", tag="q_words", align_bytes=64)
-        k_words = sb.tile([P, T], U16, name="k_words", align_bytes=64)
-        q_bytes = sb.tile([P, T], U8, name="q_bytes", align_bytes=64)
-        k_bytes = sb.tile([P, T], U8, name="k_bytes", align_bytes=64)
-        size_col = sb.tile([P, PACK], F32, name="size_col")
-        mask_sb = [sb.tile([P, 2, J], F32, name="mask%d" % h) for h in range(2)]
-        vals_sb = [sb.tile([P, T], F32, name="vals%d" % e) for e in range(TILES)]
-        windows = [sb.tile([P, T], F32, name="window%d" % w) for w in range(WINDOWS - 1)]
-        ident = sb.tile([P, P], F32, name="ident")
+        q_words = tile([P, T], U32, "q_words")
+        k_words = tile([P, T], U16, "k_words")
+        q_bytes = tile([P, T], U8, "q_bytes")
+        k_bytes = tile([P, T], U8, "k_bytes")
+        size_col = tile([P, PACK], F32, "size_col")
+        mask_sb = [tile([P, 2, J], F32, "mask%d" % h) for h in range(2)]
+        ident = tile([P, P], F32, "ident")
 
         nc.vector.memset(k_bytes[:].bitcast(I32), 0)
         nc.vector.memset(q_bytes[:].bitcast(I32), 0)
+        make_identity(nc, ident[:])
+        nc.gpsimd.dma_start(out=size_col[:], in_=size.rearrange("o (p c) -> p (o c)", c=PACK))
+        windows = [tile([P, T], F32, "window0")]
+        nc.vector.memset(windows[0][:].bitcast(I32), 0)
 
-        def load_scale_rows(queue, plane, rows):
+        def load_scale_rows(plane, rows):
             for quad in range(4):
-                queue.dma_start(
+                nc.sync.dma_start(
                     out=plane[32 * quad : 32 * quad + 4, :].bitcast(I32),
                     in_=rows[0, 4 * quad : 4 * quad + 4, :].bitcast(I32),
                 )
@@ -57,42 +62,49 @@ def tile_attend_pickboth_kernel(tc, qpool_words, qpool_scales, keys_words, keys_
         nc.sync.dma_start(k_list[:], offs2)
         nc.sync.dma_start(out=k_words[:].bitcast(I32), in_=keys_words[0].bitcast(I32))
         nc.sync.dma_start(q_list[:], offs)
-        load_scale_rows(nc.sync, k_bytes, keys_scales)
+        load_scale_rows(k_bytes, keys_scales)
         nc.sync.dma_start(out=q_words[:].bitcast(I32), in_=qpool_words[0].rearrange("p n t -> p (n t)").bitcast(I32))
-        load_scale_rows(nc.sync, q_bytes, qpool_scales)
-        nc.sync.dma_start(out=mask_sb[0][:], in_=mask[0:HALF, :].rearrange("(a p) j -> p a j", p=P))
-        nc.sync.dma_start(out=size_col[:], in_=size.rearrange("o (p c) -> p (o c)", c=PACK))
-        nc.sync.dma_start(out=mask_sb[1][:], in_=mask[HALF:I, :].rearrange("(a p) j -> p a j", p=P))
-        for e in range(TILES):
-            nc.sync.dma_start(out=vals_sb[e][:], in_=vals[e * P : (e + 1) * P, :])
+        load_scale_rows(q_bytes, qpool_scales)
+        for h in range(2):
+            nc.sync.dma_start(out=mask_sb[h][:], in_=mask[h * HALF : (h + 1) * HALF, :].rearrange("(a p) j -> p a j", p=P))
 
-        make_identity(nc, ident[:])
-        for window in windows:
-            nc.vector.memset(window[:], 0.0)
+        vals_sb = []
+
+        def load_values(queue, on):
+            e = len(vals_sb)
+            vals_sb.append(tile([P, T], F32, "vals%d" % e, on))
+            queue.dma_start(out=vals_sb[e][:], in_=vals[e * P : (e + 1) * P, :])
 
         size_ps = ps.tile([P, PACK, P], F32, name="size_ps")
         for c in range(PACK):
             nc.tensor.transpose(size_ps[:, c, :], size_col[:, c : c + 1].to_broadcast([P, P]), ident[:])
 
-        k_codes = sb.tile([P, J], U16, name="k_codes", align_bytes=64)
-        k_scale = sb.tile([P, J], U8, name="k_scale", align_bytes=64)
-        q_codes = sb.tile([P, I], U32, name="q_codes", align_bytes=64)
-        q_scale = sb.tile([P, I], U8, name="q_scale", align_bytes=64)
+        k_codes = tile([P, J], U16, "k_codes")
+        k_scale = tile([P, J], U8, "k_scale")
+        q_codes = tile([P, I], U32, "q_codes")
+        q_scale = tile([P, I], U8, "q_scale")
         nc.vector.tensor_copy(k_codes[:], k_words[:].indirect(k_list[:]))
         nc.vector.tensor_copy(k_scale[:], k_bytes[:].indirect(k_list[:]))
+        for e in range(TILES):
+            if e == 1:
+                load_values(nc.scalar, "k_bytes")
+            else:
+                load_values(nc.sync, None)
 
-        scores = [ps.tile([P, J], F32, name="scores%d" % b) for b in range(3)]
+        scores = [ps.tile([P, J], F32, name="scores%d" % b) for b in range(2)]
+
+        def listed(h):
+            return q_list[:, h * HALF // 16 : (h + 1) * HALF // 16]
 
         def gather_queries(h):
             cols = slice(h * HALF, (h + 1) * HALF)
-            entries = q_list[:, h * HALF // 16 : (h + 1) * HALF // 16]
-            nc.vector.tensor_copy(q_codes[:, cols], q_words[:].indirect(entries))
-            nc.vector.tensor_copy(q_scale[:, cols], q_bytes[:].indirect(entries))
+            nc.vector.tensor_copy(q_scale[:, cols], q_bytes[:].indirect(listed(h)))
+            nc.vector.tensor_copy(q_codes[:, cols], q_words[:].indirect(listed(h)))
 
         def score(i):
             cols = slice(i * P, (i + 1) * P)
             nc.tensor.matmul_mx(
-                out=scores[i % 3][:],
+                out=scores[i % 2][:],
                 lhsT=q_codes[:, cols].bitcast(FP8X4),
                 lhsT_scale=q_scale[:, cols],
                 rhs=k_codes[:].bitcast(FP4X4),
@@ -101,20 +113,23 @@ def tile_attend_pickboth_kernel(tc, qpool_words, qpool_scales, keys_words, keys_
                 stop=True,
             )
 
-        s_sb = [sb.tile([P, J], F32, name="s%d" % i) for i in range(TILES)]
-        p_sb = [sb.tile([P, J], F32, name="p%d" % i) for i in range(TILES)]
-        w_sb = [sb.tile([P, J], BF16, name="w%d" % i, align_bytes=64) for i in range(TILES)]
-        neg_max = [sb.tile([P, 1], F32, name="neg_max%d" % i) for i in range(TILES)]
-        row_sum = [sb.tile([P, 1], F32, name="row_sum%d" % i) for i in range(TILES)]
-        inv_sum = [sb.tile([P, 1], F32, name="inv_sum%d" % i) for i in range(TILES)]
-        turn_ps = [ps.tile([P, 2, P], F32, name="turn%d" % b) for b in range(2)]
-        o_ps = [ps.tile([P, I], F32, name="o_ps%d" % b) for b in range(2)]
-        w_grouped = sb.tile([P, I * PACK], BF16, name="w_grouped", align_bytes=64)
-        w_codes = sb.tile([P, I], U32, name="w_codes", align_bytes=64)
-        w_scale = sb.tile([P, I], U8, name="w_scale", align_bytes=64)
+        s_sb = [tile([P, J], F32, "s%d" % i) for i in range(TILES)]
+        p_sb = [tile([P, J], F32, "p%d" % i) for i in range(TILES)]
+        w_sb = [tile([P, J], BF16, "w%d" % i) for i in range(TILES)]
+        neg_max = [tile([P, 1], F32, "neg_max%d" % i) for i in range(TILES)]
+        row_sum = [tile([P, 1], F32, "row_sum%d" % i) for i in range(TILES)]
+        inv_sum = [tile([P, 1], F32, "inv_sum%d" % i) for i in range(TILES)]
+        w_turn = [ps.tile([P, 2, P], F32, name="w_turn%d" % b) for b in range(2)]
+        v_turn = ps.tile([P, 2, P], F32, name="v_turn")
+        o_ps = [ps.tile([P, HALF], F32, name="o_ps%d" % h) for h in range(2)]
+        w_grouped = tile([P, I * PACK], BF16, "w_grouped")
+        w_codes = tile([P, I], U32, "w_codes")
+        w_scale = tile([P, I], U8, "w_scale")
+
+        def add_mask(i):
+            nc.vector.tensor_tensor(s_sb[i][:], scores[i % 2][:], mask_sb[i // 2][:, i % 2, :], ALU.add)
 
         def exponentials(i):
-            nc.vector.tensor_tensor(s_sb[i][:], scores[i % 3][:], mask_sb[i // 2][:, i % 2, :], ALU.add)
             nc.vector.tensor_reduce(neg_max[i][:], s_sb[i][:], AX.X, ALU.max, negate=True)
             nc.scalar.activation(p_sb[i][:], s_sb[i][:], ACT.Exp, bias=neg_max[i][:], accum_out=row_sum[i][:])
 
@@ -124,8 +139,10 @@ def tile_attend_pickboth_kernel(tc, qpool_words, qpool_scales, keys_words, keys_
                 nc.tensor.transpose(bank[:, u, :], words[:, u : J // 2 : 2], ident[:])
             nc.scalar.copy(grouped.bitcast(F32).rearrange("p (r u) -> p r u", u=2), bank[:].rearrange("p u r -> p r u"))
 
-        def weights(i):
+        def invert(i):
             nc.vector.reciprocal(inv_sum[i][:], row_sum[i][:])
+
+        def weights(i):
             nc.vector.scalar_tensor_tensor(
                 w_sb[i][:].rearrange("m (p c) -> m p c", c=PACK),
                 p_sb[i][:].rearrange("m (p c) -> m p c", c=PACK),
@@ -134,7 +151,7 @@ def tile_attend_pickboth_kernel(tc, qpool_words, qpool_scales, keys_words, keys_
                 ALU.mult,
                 ALU.mult,
             )
-            turn(w_sb[i][:], turn_ps[i % 2], w_grouped[:, i * P * PACK : (i + 1) * P * PACK])
+            turn(w_sb[i][:], w_turn[i % 2], w_grouped[:, i * P * PACK : (i + 1) * P * PACK])
 
         def quantise_weights(h):
             cols = slice(h * HALF, (h + 1) * HALF)
@@ -144,74 +161,73 @@ def tile_attend_pickboth_kernel(tc, qpool_words, qpool_scales, keys_words, keys_
                 in_=w_grouped[:, h * HALF * PACK : (h + 1) * HALF * PACK],
             )
 
-        v_rows = [sb.tile([P, J], BF16, name="v_rows%d" % e, align_bytes=64) for e in range(TILES)]
-        v_grouped = [sb.tile([P, P * PACK], BF16, name="v_grouped%d" % e, align_bytes=64) for e in range(TILES)]
-        v_codes = [sb.tile([P, P], U32, name="v_codes%d" % e, align_bytes=64) for e in range(TILES)]
-        v_scale = [sb.tile([P, P], U8, name="v_scale%d" % e, align_bytes=64) for e in range(TILES)]
-        o_sb = [sb.tile([P, I], F32, name="o_sb%d" % e) for e in range(TILES)]
+        v_codes = [tile([P, P], U32, "v_codes%d" % e) for e in range(TILES)]
+        v_scale = [tile([P, P], U8, "v_scale%d" % e) for e in range(TILES)]
 
-        def gather_values(e):
+        rows_on = ["s0", "s2", "v_rows2", "v_rows3"]
+
+        def values(e):
+            v_rows = tile([P, J], BF16, "v_rows%d" % e, rows_on[e])
             if e in ON_SCALAR:
-                rounded = sb.tile([P, T], BF16, name="rounded%d" % e)
+                rounded = tile([P, T], BF16, "rounded%d" % e, "s3")
                 for c in range(4):
                     cols = slice(c * T // 4, (c + 1) * T // 4)
                     nc.scalar.activation(rounded[:, cols], vals_sb[e][:, cols], ACT.Copy)
-                nc.scalar.activation(v_rows[e][:], rounded[:].indirect(k_list[:]), ACT.Copy)
+                for h in range(2):
+                    entries = k_list[:, h * HALF // 16 : (h + 1) * HALF // 16]
+                    nc.scalar.activation(v_rows[:, h * HALF : (h + 1) * HALF], rounded[:].indirect(entries), ACT.Copy)
             else:
-                nc.vector.tensor_copy(v_rows[e][:], vals_sb[e][:].indirect(k_list[:]))
-            turn(v_rows[e][:], turn_ps[e % 2], v_grouped[e][:])
+                nc.vector.tensor_copy(v_rows[:], vals_sb[e][:].indirect(k_list[:]))
+            v_grouped = tile([P, P * PACK], BF16, "v_grouped%d" % e)
+            turn(v_rows[:], v_turn, v_grouped[:])
+            nc.vector.quantize_mx(out=v_codes[e][:].bitcast(FP8X4), scales=v_scale[e][:], in_=v_grouped[:])
 
-        def quantise_values(e):
-            nc.vector.quantize_mx(out=v_codes[e][:].bitcast(FP8X4), scales=v_scale[e][:], in_=v_grouped[e][:])
-
-        def product(e):
+        def product(e, h, on):
+            cols = slice(h * HALF, (h + 1) * HALF)
             nc.tensor.matmul_mx(
-                out=o_ps[e % 2][:],
+                out=o_ps[h][:],
                 lhsT=v_codes[e][:].bitcast(FP8X4),
                 lhsT_scale=v_scale[e][:],
-                rhs=w_codes[:].bitcast(FP8X4),
-                rhs_scale=w_scale[:],
+                rhs=w_codes[:, cols].bitcast(FP8X4),
+                rhs_scale=w_scale[:, cols],
                 start=True,
                 stop=True,
             )
-            nc.scalar.copy(o_sb[e][:], o_ps[e % 2][:])
-
-        def scatter(e):
-            window = windows[e % WINDOWS]
-            nc.vector.tensor_copy(window[:].indirect(q_list[:]), o_sb[e][:])
-            nc.sync.dma_start(out=out[e * P : (e + 1) * P, :], in_=window[:])
+            o_sb = tile([P, HALF], F32, "o_sb%d_%d" % (e, h), on)
+            nc.scalar.copy(o_sb[:], o_ps[h][:])
+            nc.vector.tensor_copy(windows[e % WINDOWS][:].indirect(listed(h)), o_sb[:])
 
         gather_queries(0)
         score(0)
         score(1)
         gather_queries(1)
-        windows.append(sb.tile([P, T], F32, name="last_window", tag="q_words", align_bytes=64))
-        nc.gpsimd.memset(windows[-1][:], 0.0)
+        for w, on in ((1, "q_words"), (2, "q_bytes")):
+            windows.append(tile([P, T], F32, "window%d" % w, on))
+            nc.gpsimd.memset(windows[w][:], 0.0)
+        add_mask(0)
         score(2)
-        exponentials(0)
+        add_mask(1)
         score(3)
+        exponentials(0)
         exponentials(1)
-        weights(0)
+        add_mask(2)
+        add_mask(3)
+        invert(0)
         exponentials(2)
-        weights(1)
+        weights(0)
+        invert(1)
         exponentials(3)
+        weights(1)
+        values(0)
+        invert(2)
+        invert(3)
         weights(2)
-        gather_values(0)
-        weights(3)
         quantise_weights(0)
-        quantise_values(0)
+        weights(3)
         quantise_weights(1)
-        product(0)
-        gather_values(1)
-        quantise_values(1)
-        product(1)
-        scatter(0)
-        gather_values(2)
-        quantise_values(2)
-        product(2)
-        scatter(1)
-        gather_values(3)
-        quantise_values(3)
-        product(3)
-        scatter(2)
-        scatter(3)
+        for e in range(TILES):
+            product(e, 0, "w3" if e == 0 else None)
+            if e + 1 < TILES:
+                values(e + 1)
+            product(e, 1, rows_on[e + 1] if e + 1 < TILES else None)
+            nc.sync.dma_start(out=out[e * P : (e + 1) * P, :], in_=windows[e % WINDOWS][:])

@@ -48,9 +48,9 @@ def tile_attend_pickboth_kernel(tc, qpool_words, qpool_scales, keys_words, keys_
         nc.vector.memset(k_bytes[:].bitcast(I32), 0)
         nc.vector.memset(q_bytes[:].bitcast(I32), 0)
         make_identity(nc, ident[:])
-        nc.gpsimd.dma_start(out=size_col[:], in_=size.rearrange("o (p c) -> p (o c)", c=PACK))
-        windows = [tile([P, T], F32, "window0")]
-        nc.vector.memset(windows[0][:].bitcast(I32), 0)
+        windows = [tile([P, T], F32, "window%d" % w) for w in range(2)]
+        for window in windows:
+            nc.vector.memset(window[:].bitcast(I32), 0)
 
         def load_scale_rows(plane, rows):
             for quad in range(4):
@@ -65,15 +65,23 @@ def tile_attend_pickboth_kernel(tc, qpool_words, qpool_scales, keys_words, keys_
         load_scale_rows(k_bytes, keys_scales)
         nc.sync.dma_start(out=q_words[:].bitcast(I32), in_=qpool_words[0].rearrange("p n t -> p (n t)").bitcast(I32))
         load_scale_rows(q_bytes, qpool_scales)
-        for h in range(2):
+
+        vals_sb = {}
+
+        def load_values(e, queue, on=None):
+            vals_sb[e] = tile([P, T], F32, "vals%d" % e, on)
+            queue.dma_start(out=vals_sb[e][:], in_=vals[e * P : (e + 1) * P, :])
+
+        def load_mask(h):
             nc.sync.dma_start(out=mask_sb[h][:], in_=mask[h * HALF : (h + 1) * HALF, :].rearrange("(a p) j -> p a j", p=P))
 
-        vals_sb = []
-
-        def load_values(queue, on):
-            e = len(vals_sb)
-            vals_sb.append(tile([P, T], F32, "vals%d" % e, on))
-            queue.dma_start(out=vals_sb[e][:], in_=vals[e * P : (e + 1) * P, :])
+        load_values(0, nc.sync)
+        load_mask(0)
+        nc.sync.dma_start(out=size_col[:], in_=size.rearrange("o (p c) -> p (o c)", c=PACK))
+        load_mask(1)
+        load_values(2, nc.sync)
+        load_values(3, nc.sync)
+        load_values(1, nc.sync)
 
         size_ps = ps.tile([P, PACK, P], F32, name="size_ps")
         for c in range(PACK):
@@ -85,11 +93,6 @@ def tile_attend_pickboth_kernel(tc, qpool_words, qpool_scales, keys_words, keys_
         q_scale = tile([P, I], U8, "q_scale")
         nc.vector.tensor_copy(k_codes[:], k_words[:].indirect(k_list[:]))
         nc.vector.tensor_copy(k_scale[:], k_bytes[:].indirect(k_list[:]))
-        for e in range(TILES):
-            if e == 1:
-                load_values(nc.scalar, "k_bytes")
-            else:
-                load_values(nc.sync, None)
 
         scores = [ps.tile([P, J], F32, name="scores%d" % b) for b in range(2)]
 
@@ -115,13 +118,12 @@ def tile_attend_pickboth_kernel(tc, qpool_words, qpool_scales, keys_words, keys_
 
         s_sb = [tile([P, J], F32, "s%d" % i) for i in range(TILES)]
         p_sb = [tile([P, J], F32, "p%d" % i) for i in range(TILES)]
-        w_sb = [tile([P, J], BF16, "w%d" % i) for i in range(TILES)]
         neg_max = [tile([P, 1], F32, "neg_max%d" % i) for i in range(TILES)]
         row_sum = [tile([P, 1], F32, "row_sum%d" % i) for i in range(TILES)]
         inv_sum = [tile([P, 1], F32, "inv_sum%d" % i) for i in range(TILES)]
         w_turn = [ps.tile([P, 2, P], F32, name="w_turn%d" % b) for b in range(2)]
         v_turn = ps.tile([P, 2, P], F32, name="v_turn")
-        o_ps = [ps.tile([P, HALF], F32, name="o_ps%d" % h) for h in range(2)]
+        o_ps = [ps.tile([P, I], F32, name="o_ps%d" % h) for h in range(2)]
         w_grouped = tile([P, I * PACK], BF16, "w_grouped")
         w_codes = tile([P, I], U32, "w_codes")
         w_scale = tile([P, I], U8, "w_scale")
@@ -143,15 +145,16 @@ def tile_attend_pickboth_kernel(tc, qpool_words, qpool_scales, keys_words, keys_
             nc.vector.reciprocal(inv_sum[i][:], row_sum[i][:])
 
         def weights(i):
+            w_rows = tile([P, J], BF16, "w%d" % i, None)
             nc.vector.scalar_tensor_tensor(
-                w_sb[i][:].rearrange("m (p c) -> m p c", c=PACK),
+                w_rows[:].rearrange("m (p c) -> m p c", c=PACK),
                 p_sb[i][:].rearrange("m (p c) -> m p c", c=PACK),
                 inv_sum[i][:],
                 size_ps[:].rearrange("m c p -> m p c"),
                 ALU.mult,
                 ALU.mult,
             )
-            turn(w_sb[i][:], w_turn[i % 2], w_grouped[:, i * P * PACK : (i + 1) * P * PACK])
+            turn(w_rows[:], w_turn[i % 2], w_grouped[:, i * P * PACK : (i + 1) * P * PACK])
 
         def quantise_weights(h):
             cols = slice(h * HALF, (h + 1) * HALF)
@@ -164,28 +167,32 @@ def tile_attend_pickboth_kernel(tc, qpool_words, qpool_scales, keys_words, keys_
         v_codes = [tile([P, P], U32, "v_codes%d" % e) for e in range(TILES)]
         v_scale = [tile([P, P], U8, "v_scale%d" % e) for e in range(TILES)]
 
-        rows_on = ["s0", "s2", "v_rows2", "v_rows3"]
+        rows_on = ["v_rows0", "v_rows1", "v_rows2", "v_rows3"]
 
-        def values(e):
-            v_rows = tile([P, J], BF16, "v_rows%d" % e, rows_on[e])
+        v_rows = {}
+
+        def gather_values(e):
+            v_rows[e] = tile([P, J], BF16, "v_rows%d" % e, rows_on[e])
             if e in ON_SCALAR:
-                rounded = tile([P, T], BF16, "rounded%d" % e, "s3")
-                for c in range(4):
-                    cols = slice(c * T // 4, (c + 1) * T // 4)
+                rounded = tile([P, T], BF16, "rounded%d" % e, "rounded")
+                for c in range(2):
+                    cols = slice(c * T // 2, (c + 1) * T // 2)
                     nc.scalar.activation(rounded[:, cols], vals_sb[e][:, cols], ACT.Copy)
                 for h in range(2):
                     entries = k_list[:, h * HALF // 16 : (h + 1) * HALF // 16]
-                    nc.scalar.activation(v_rows[:, h * HALF : (h + 1) * HALF], rounded[:].indirect(entries), ACT.Copy)
+                    nc.scalar.activation(v_rows[e][:, h * HALF : (h + 1) * HALF], rounded[:].indirect(entries), ACT.Copy)
             else:
-                nc.vector.tensor_copy(v_rows[:], vals_sb[e][:].indirect(k_list[:]))
-            v_grouped = tile([P, P * PACK], BF16, "v_grouped%d" % e)
-            turn(v_rows[:], v_turn, v_grouped[:])
+                nc.vector.tensor_copy(v_rows[e][:], vals_sb[e][:].indirect(k_list[:]))
+
+        def values(e):
+            v_grouped = tile([P, P * PACK], BF16, "v_grouped%d" % e, "s0" if e == 0 else None)
+            turn(v_rows[e][:], v_turn, v_grouped[:])
             nc.vector.quantize_mx(out=v_codes[e][:].bitcast(FP8X4), scales=v_scale[e][:], in_=v_grouped[:])
 
-        def product(e, h, on):
-            cols = slice(h * HALF, (h + 1) * HALF)
+        def product(e, first, last, bank, on):
+            cols = slice(first, last)
             nc.tensor.matmul_mx(
-                out=o_ps[h][:],
+                out=o_ps[bank][:, cols],
                 lhsT=v_codes[e][:].bitcast(FP8X4),
                 lhsT_scale=v_scale[e][:],
                 rhs=w_codes[:, cols].bitcast(FP8X4),
@@ -193,17 +200,16 @@ def tile_attend_pickboth_kernel(tc, qpool_words, qpool_scales, keys_words, keys_
                 start=True,
                 stop=True,
             )
-            o_sb = tile([P, HALF], F32, "o_sb%d_%d" % (e, h), on)
-            nc.scalar.copy(o_sb[:], o_ps[h][:])
-            nc.vector.tensor_copy(windows[e % WINDOWS][:].indirect(listed(h)), o_sb[:])
+            o_sb = tile([P, last - first], F32, "o_sb%d_%d" % (e, first), on)
+            nc.scalar.copy(o_sb[:], o_ps[bank][:, cols])
+            nc.vector.tensor_copy(windows[e % WINDOWS][:].indirect(q_list[:, first // 16 : last // 16]), o_sb[:])
 
         gather_queries(0)
         score(0)
         score(1)
         gather_queries(1)
-        for w, on in ((1, "q_words"), (2, "q_bytes")):
-            windows.append(tile([P, T], F32, "window%d" % w, on))
-            nc.gpsimd.memset(windows[w][:], 0.0)
+        windows.append(tile([P, T], F32, "window2", "q_words"))
+        nc.gpsimd.memset(windows[2][:], 0.0)
         add_mask(0)
         score(2)
         add_mask(1)
@@ -218,16 +224,25 @@ def tile_attend_pickboth_kernel(tc, qpool_words, qpool_scales, keys_words, keys_
         invert(1)
         exponentials(3)
         weights(1)
+        gather_values(0)
         values(0)
         invert(2)
         invert(3)
         weights(2)
         quantise_weights(0)
         weights(3)
+        gather_values(1)
         quantise_weights(1)
+        bank = 0
         for e in range(TILES):
-            product(e, 0, "w3" if e == 0 else None)
+            first = 0
+            if e in (0, 2):
+                product(e, 0, HALF, bank, "w3" if e == 0 else None)
+                first, bank = HALF, 1 - bank
+            if 2 <= e + 1 < TILES or e + 1 in ON_SCALAR:
+                gather_values(e + 1)
             if e + 1 < TILES:
                 values(e + 1)
-            product(e, 1, rows_on[e + 1] if e + 1 < TILES else None)
+            product(e, first, I, bank, rows_on[e + 1] if e + 1 < TILES else None)
+            bank = 1 - bank
             nc.sync.dma_start(out=out[e * P : (e + 1) * P, :], in_=windows[e % WINDOWS][:])

@@ -23,7 +23,7 @@ PACK = 4
 TILES = 4
 HALF = 256
 WINDOWS = 3
-ON_SCALAR = (2, 3)
+ON_SCALAR = ()
 
 
 def tile_attend_pickboth_kernel(tc, qpool_words, qpool_scales, keys_words, keys_scales, vals, mask, size, offs, offs2, out):
@@ -42,7 +42,6 @@ def tile_attend_pickboth_kernel(tc, qpool_words, qpool_scales, keys_words, keys_
         q_bytes = tile([P, T], U8, "q_bytes")
         k_bytes = tile([P, T], U8, "k_bytes")
         size_col = tile([P, PACK], F32, "size_col")
-        mask_sb = [tile([P, 2, J], F32, "mask%d" % h) for h in range(2)]
         ident = tile([P, P], F32, "ident")
 
         nc.vector.memset(k_bytes[:].bitcast(I32), 0)
@@ -72,16 +71,22 @@ def tile_attend_pickboth_kernel(tc, qpool_words, qpool_scales, keys_words, keys_
             vals_sb[e] = tile([P, T], F32, "vals%d" % e, on)
             queue.dma_start(out=vals_sb[e][:], in_=vals[e * P : (e + 1) * P, :])
 
-        def load_mask(h):
-            nc.sync.dma_start(out=mask_sb[h][:], in_=mask[h * HALF : (h + 1) * HALF, :].rearrange("(a p) j -> p a j", p=P))
+        mask_sb = []
+
+        def load_mask(count):
+            first = len(mask_sb)
+            rows = tile([P, count, J], F32, "mask%d" % first)
+            nc.sync.dma_start(out=rows[:], in_=mask[first * P : (first + count) * P, :].rearrange("(a p) j -> p a j", p=P))
+            mask_sb.extend(rows[:, a, :] for a in range(count))
 
         load_values(0, nc.sync)
-        load_mask(0)
-        nc.sync.dma_start(out=size_col[:], in_=size.rearrange("o (p c) -> p (o c)", c=PACK))
         load_mask(1)
+        load_mask(1)
+        load_mask(2)
+        nc.sync.dma_start(out=size_col[:], in_=size.rearrange("o (p c) -> p (o c)", c=PACK))
+        load_values(1, nc.sync)
         load_values(2, nc.sync)
         load_values(3, nc.sync)
-        load_values(1, nc.sync)
 
         size_ps = ps.tile([P, PACK, P], F32, name="size_ps")
         for c in range(PACK):
@@ -129,7 +134,7 @@ def tile_attend_pickboth_kernel(tc, qpool_words, qpool_scales, keys_words, keys_
         w_scale = tile([P, I], U8, "w_scale")
 
         def add_mask(i):
-            nc.vector.tensor_tensor(s_sb[i][:], scores[i % 2][:], mask_sb[i // 2][:, i % 2, :], ALU.add)
+            nc.vector.tensor_tensor(s_sb[i][:], scores[i % 2][:], mask_sb[i], ALU.add)
 
         def exponentials(i):
             nc.vector.tensor_reduce(neg_max[i][:], s_sb[i][:], AX.X, ALU.max, negate=True)
@@ -175,8 +180,8 @@ def tile_attend_pickboth_kernel(tc, qpool_words, qpool_scales, keys_words, keys_
             v_rows[e] = tile([P, J], BF16, "v_rows%d" % e, rows_on[e])
             if e in ON_SCALAR:
                 rounded = tile([P, T], BF16, "rounded%d" % e, "rounded")
-                for c in range(2):
-                    cols = slice(c * T // 2, (c + 1) * T // 2)
+                for c in range(4):
+                    cols = slice(c * T // 4, (c + 1) * T // 4)
                     nc.scalar.activation(rounded[:, cols], vals_sb[e][:, cols], ACT.Copy)
                 for h in range(2):
                     entries = k_list[:, h * HALF // 16 : (h + 1) * HALF // 16]
@@ -185,7 +190,7 @@ def tile_attend_pickboth_kernel(tc, qpool_words, qpool_scales, keys_words, keys_
                 nc.vector.tensor_copy(v_rows[e][:], vals_sb[e][:].indirect(k_list[:]))
 
         def values(e):
-            v_grouped = tile([P, P * PACK], BF16, "v_grouped%d" % e, "s0" if e == 0 else None)
+            v_grouped = tile([P, P * PACK], BF16, "v_grouped%d" % e, "s3" if e == 0 else None)
             turn(v_rows[e][:], v_turn, v_grouped[:])
             nc.vector.quantize_mx(out=v_codes[e][:].bitcast(FP8X4), scales=v_scale[e][:], in_=v_grouped[:])
 
@@ -236,7 +241,7 @@ def tile_attend_pickboth_kernel(tc, qpool_words, qpool_scales, keys_words, keys_
         bank = 0
         for e in range(TILES):
             first = 0
-            if e in (0, 2):
+            if e in (0,):
                 product(e, 0, HALF, bank, "w3" if e == 0 else None)
                 first, bank = HALF, 1 - bank
             if 2 <= e + 1 < TILES or e + 1 in ON_SCALAR:

@@ -23,7 +23,9 @@ PACK = 4
 TILES = 4
 HALF = 256
 WINDOWS = 3
-ON_SCALAR = ()
+ADD_ON_GPSIMD = ()
+CASTS = 4
+ON_SCALAR = (2, 3)
 
 
 def tile_attend_pickboth_kernel(tc, qpool_words, qpool_scales, keys_words, keys_scales, vals, mask, size, offs, offs2, out):
@@ -51,25 +53,30 @@ def tile_attend_pickboth_kernel(tc, qpool_words, qpool_scales, keys_words, keys_
         for window in windows:
             nc.vector.memset(window[:].bitcast(I32), 0)
 
-        def load_scale_rows(plane, rows):
+        def load_scale_rows(plane, rows, queue):
             for quad in range(4):
-                nc.sync.dma_start(
-                    out=plane[32 * quad : 32 * quad + 4, :].bitcast(I32),
-                    in_=rows[0, 4 * quad : 4 * quad + 4, :].bitcast(I32),
+                queue[quad].dma_start(
+                    out=plane[quad:P:32, :].bitcast(I32),
+                    in_=rows[0, quad:16:4, :].bitcast(I32),
                 )
 
         nc.sync.dma_start(k_list[:], offs2)
         nc.sync.dma_start(out=k_words[:].bitcast(I32), in_=keys_words[0].bitcast(I32))
         nc.sync.dma_start(q_list[:], offs)
-        load_scale_rows(k_bytes, keys_scales)
+        load_scale_rows(k_bytes, keys_scales, [nc.sync, nc.sync, nc.scalar, nc.scalar])
         nc.sync.dma_start(out=q_words[:].bitcast(I32), in_=qpool_words[0].rearrange("p n t -> p (n t)").bitcast(I32))
-        load_scale_rows(q_bytes, qpool_scales)
+        load_scale_rows(q_bytes, qpool_scales, [nc.scalar] * 4)
+
+        warm = tile([P, 1], F32, "warm")
+        nc.scalar.activation(warm[:], windows[0][:, 0:1], ACT.Exp)
 
         vals_sb = {}
 
-        def load_values(e, queue, on=None):
-            vals_sb[e] = tile([P, T], F32, "vals%d" % e, on)
-            queue.dma_start(out=vals_sb[e][:], in_=vals[e * P : (e + 1) * P, :])
+        def load_values(e, queue, part=0, parts=1, on=None):
+            if e not in vals_sb:
+                vals_sb[e] = tile([P, T], F32, "vals%d" % e, on)
+            cols = slice(part * T // parts, (part + 1) * T // parts)
+            queue.dma_start(out=vals_sb[e][:, cols], in_=vals[e * P : (e + 1) * P, cols])
 
         mask_sb = []
 
@@ -79,14 +86,16 @@ def tile_attend_pickboth_kernel(tc, qpool_words, qpool_scales, keys_words, keys_
             nc.sync.dma_start(out=rows[:], in_=mask[first * P : (first + count) * P, :].rearrange("(a p) j -> p a j", p=P))
             mask_sb.extend(rows[:, a, :] for a in range(count))
 
+        nc.scalar.dma_start(out=size_col[:], in_=size.rearrange("o (p c) -> p (o c)", c=PACK))
         load_values(0, nc.sync)
         load_mask(1)
         load_mask(1)
         load_mask(2)
-        nc.sync.dma_start(out=size_col[:], in_=size.rearrange("o (p c) -> p (o c)", c=PACK))
+        load_values(2, nc.sync, 0, 2)
+        load_values(2, nc.sync, 1, 2)
         load_values(1, nc.sync)
-        load_values(2, nc.sync)
-        load_values(3, nc.sync)
+        load_values(3, nc.sync, 0, 2)
+        load_values(3, nc.sync, 1, 2)
 
         size_ps = ps.tile([P, PACK, P], F32, name="size_ps")
         for c in range(PACK):
@@ -99,7 +108,7 @@ def tile_attend_pickboth_kernel(tc, qpool_words, qpool_scales, keys_words, keys_
         nc.vector.tensor_copy(k_codes[:], k_words[:].indirect(k_list[:]))
         nc.vector.tensor_copy(k_scale[:], k_bytes[:].indirect(k_list[:]))
 
-        scores = [ps.tile([P, J], F32, name="scores%d" % b) for b in range(2)]
+        scores = [ps.tile([P, J], F32, name="scores%d" % i, tag="bank%d" % i) for i in range(TILES)]
 
         def listed(h):
             return q_list[:, h * HALF // 16 : (h + 1) * HALF // 16]
@@ -112,7 +121,7 @@ def tile_attend_pickboth_kernel(tc, qpool_words, qpool_scales, keys_words, keys_
         def score(i):
             cols = slice(i * P, (i + 1) * P)
             nc.tensor.matmul_mx(
-                out=scores[i % 2][:],
+                out=scores[i][:],
                 lhsT=q_codes[:, cols].bitcast(FP8X4),
                 lhsT_scale=q_scale[:, cols],
                 rhs=k_codes[:].bitcast(FP4X4),
@@ -127,14 +136,17 @@ def tile_attend_pickboth_kernel(tc, qpool_words, qpool_scales, keys_words, keys_
         row_sum = [tile([P, 1], F32, "row_sum%d" % i) for i in range(TILES)]
         inv_sum = [tile([P, 1], F32, "inv_sum%d" % i) for i in range(TILES)]
         w_turn = [ps.tile([P, 2, P], F32, name="w_turn%d" % b) for b in range(2)]
-        v_turn = ps.tile([P, 2, P], F32, name="v_turn")
-        o_ps = [ps.tile([P, I], F32, name="o_ps%d" % h) for h in range(2)]
         w_grouped = tile([P, I * PACK], BF16, "w_grouped")
         w_codes = tile([P, I], U32, "w_codes")
         w_scale = tile([P, I], U8, "w_scale")
 
         def add_mask(i):
-            nc.vector.tensor_tensor(s_sb[i][:], scores[i % 2][:], mask_sb[i], ALU.add)
+            if i in ADD_ON_GPSIMD:
+                a_sb = tile([P, J], F32, "a%d" % i)
+                nc.scalar.activation(a_sb[:], scores[i][:], ACT.Copy)
+                nc.gpsimd.tensor_tensor(s_sb[i][:], a_sb[:], mask_sb[i], ALU.add)
+            else:
+                nc.vector.tensor_tensor(s_sb[i][:], scores[i][:], mask_sb[i], ALU.add)
 
         def exponentials(i):
             nc.vector.tensor_reduce(neg_max[i][:], s_sb[i][:], AX.X, ALU.max, negate=True)
@@ -149,17 +161,19 @@ def tile_attend_pickboth_kernel(tc, qpool_words, qpool_scales, keys_words, keys_
         def invert(i):
             nc.vector.reciprocal(inv_sum[i][:], row_sum[i][:])
 
+        last_rows = tile([P, 2 * J], BF16, "last_rows")
+
         def weights(i):
-            w_rows = tile([P, J], BF16, "w%d" % i, None)
+            w_rows = last_rows[:, HALF : HALF + J] if i == TILES - 1 else tile([P, J], BF16, "w%d" % i)[:]
             nc.vector.scalar_tensor_tensor(
-                w_rows[:].rearrange("m (p c) -> m p c", c=PACK),
+                w_rows.rearrange("m (p c) -> m p c", c=PACK),
                 p_sb[i][:].rearrange("m (p c) -> m p c", c=PACK),
                 inv_sum[i][:],
                 size_ps[:].rearrange("m c p -> m p c"),
                 ALU.mult,
                 ALU.mult,
             )
-            turn(w_rows[:], w_turn[i % 2], w_grouped[:, i * P * PACK : (i + 1) * P * PACK])
+            turn(w_rows, w_turn[i % 2], w_grouped[:, i * P * PACK : (i + 1) * P * PACK])
 
         def quantise_weights(h):
             cols = slice(h * HALF, (h + 1) * HALF)
@@ -172,32 +186,39 @@ def tile_attend_pickboth_kernel(tc, qpool_words, qpool_scales, keys_words, keys_
         v_codes = [tile([P, P], U32, "v_codes%d" % e) for e in range(TILES)]
         v_scale = [tile([P, P], U8, "v_scale%d" % e) for e in range(TILES)]
 
-        rows_on = ["v_rows0", "v_rows1", "v_rows2", "v_rows3"]
+        v_rows = {2: last_rows[:, :J]}
 
-        v_rows = {}
+        rounded = {}
 
-        def gather_values(e):
-            v_rows[e] = tile([P, J], BF16, "v_rows%d" % e, rows_on[e])
+        def round_values(e, on=None):
+            rounded[e] = tile([P, T], BF16, "rounded%d" % e, on)
+            for c in range(CASTS):
+                cols = slice(c * T // CASTS, (c + 1) * T // CASTS)
+                nc.scalar.activation(rounded[e][:, cols], vals_sb[e][:, cols], ACT.Copy)
+
+        def gather_values(e, on=None, halves=(0, 1)):
+            if e not in v_rows:
+                v_rows[e] = tile([P, J], BF16, "v_rows%d" % e, on)[:]
             if e in ON_SCALAR:
-                rounded = tile([P, T], BF16, "rounded%d" % e, "rounded")
-                for c in range(4):
-                    cols = slice(c * T // 4, (c + 1) * T // 4)
-                    nc.scalar.activation(rounded[:, cols], vals_sb[e][:, cols], ACT.Copy)
-                for h in range(2):
+                for h in halves:
                     entries = k_list[:, h * HALF // 16 : (h + 1) * HALF // 16]
-                    nc.scalar.activation(v_rows[e][:, h * HALF : (h + 1) * HALF], rounded[:].indirect(entries), ACT.Copy)
+                    nc.scalar.activation(v_rows[e][:, h * HALF : (h + 1) * HALF], rounded[e][:].indirect(entries), ACT.Copy)
             else:
-                nc.vector.tensor_copy(v_rows[e][:], vals_sb[e][:].indirect(k_list[:]))
+                nc.vector.tensor_copy(v_rows[e], vals_sb[e][:].indirect(k_list[:]))
 
-        def values(e):
-            v_grouped = tile([P, P * PACK], BF16, "v_grouped%d" % e, "s3" if e == 0 else None)
-            turn(v_rows[e][:], v_turn, v_grouped[:])
+        def values(e, bank="v_turn", on=None):
+            v_turn = ps.tile([P, 2, P], F32, name="v_turn%d" % e, tag=bank)
+            v_grouped = tile([P, P * PACK], BF16, "v_grouped%d" % e, on)
+            turn(v_rows[e], v_turn, v_grouped[:])
             nc.vector.quantize_mx(out=v_codes[e][:].bitcast(FP8X4), scales=v_scale[e][:], in_=v_grouped[:])
 
-        def product(e, first, last, bank, on):
+        place = [0, 1, 2, 0]
+
+        def product(e, first, last, bank, on, view=None):
             cols = slice(first, last)
+            o_ps = ps.tile([P, last - first], F32, name="o_ps%d_%d" % (e, first), tag="bank%d" % bank)
             nc.tensor.matmul_mx(
-                out=o_ps[bank][:, cols],
+                out=o_ps[:],
                 lhsT=v_codes[e][:].bitcast(FP8X4),
                 lhsT_scale=v_scale[e][:],
                 rhs=w_codes[:, cols].bitcast(FP8X4),
@@ -205,22 +226,27 @@ def tile_attend_pickboth_kernel(tc, qpool_words, qpool_scales, keys_words, keys_
                 start=True,
                 stop=True,
             )
-            o_sb = tile([P, last - first], F32, "o_sb%d_%d" % (e, first), on)
-            nc.scalar.copy(o_sb[:], o_ps[bank][:, cols])
-            nc.vector.tensor_copy(windows[e % WINDOWS][:].indirect(q_list[:, first // 16 : last // 16]), o_sb[:])
+            o_sb = view if view is not None else tile([P, last - first], F32, "o_sb%d_%d" % (e, first), on)[:]
+            nc.scalar.copy(o_sb, o_ps[:])
+            nc.vector.tensor_copy(windows[place[e]][:].indirect(q_list[:, first // 16 : last // 16]), o_sb)
+
+        def store(e):
+            nc.sync.dma_start(out=out[e * P : (e + 1) * P, :], in_=windows[place[e]][:])
 
         gather_queries(0)
         score(0)
         score(1)
         gather_queries(1)
-        windows.append(tile([P, T], F32, "window2", "q_words"))
-        nc.gpsimd.memset(windows[2][:], 0.0)
-        add_mask(0)
         score(2)
-        add_mask(1)
         score(3)
+        windows.append(tile([P, T], F32, "window2", "q_bytes"))
+        nc.gpsimd.memset(windows[2][:], 0.0)
+        gather_values(0)
+        add_mask(0)
+        add_mask(1)
         exponentials(0)
         exponentials(1)
+        values(0)
         add_mask(2)
         add_mask(3)
         invert(0)
@@ -229,25 +255,28 @@ def tile_attend_pickboth_kernel(tc, qpool_words, qpool_scales, keys_words, keys_
         invert(1)
         exponentials(3)
         weights(1)
-        gather_values(0)
-        values(0)
         invert(2)
-        invert(3)
         weights(2)
+        invert(3)
         quantise_weights(0)
         weights(3)
-        gather_values(1)
+        gather_values(1, "p3")
         quantise_weights(1)
-        bank = 0
-        for e in range(TILES):
-            first = 0
-            if e in (0,):
-                product(e, 0, HALF, bank, "w3" if e == 0 else None)
-                first, bank = HALF, 1 - bank
-            if 2 <= e + 1 < TILES or e + 1 in ON_SCALAR:
-                gather_values(e + 1)
-            if e + 1 < TILES:
-                values(e + 1)
-            product(e, first, I, bank, rows_on[e + 1] if e + 1 < TILES else None)
-            bank = 1 - bank
-            nc.sync.dma_start(out=out[e * P : (e + 1) * P, :], in_=windows[e % WINDOWS][:])
+        product(0, 0, HALF, 0, None, last_rows[:, J:].bitcast(F32))
+        values(1, "bank0")
+        product(0, HALF, I, 1, None)
+        store(0)
+        product(1, 0, HALF, 2, None)
+        round_values(2)
+        gather_values(2)
+        values(2, "bank1")
+        product(1, HALF, I, 3, None, last_rows[:, :J].bitcast(F32))
+        store(1)
+        round_values(3, "rounded2")
+        gather_values(3)
+        product(2, 0, HALF, 0, "rounded2")
+        values(3)
+        product(2, HALF, I, 1, "v_rows3")
+        store(2)
+        product(3, 0, I, 2, None)
+        store(3)

@@ -56,16 +56,16 @@ def tile_attend_pickboth_kernel(tc, qpool_words, qpool_scales, keys_words, keys_
         def load_scale_rows(plane, rows, queue):
             for quad in range(4):
                 queue[quad].dma_start(
-                    out=plane[quad:P:32, :].bitcast(I32),
-                    in_=rows[0, quad:16:4, :].bitcast(I32),
+                    out=plane[32 * quad : 32 * quad + 4, :].bitcast(I32),
+                    in_=rows[0, 4 * quad : 4 * quad + 4, :].bitcast(I32),
                 )
 
         nc.sync.dma_start(k_list[:], offs2)
         nc.sync.dma_start(out=k_words[:].bitcast(I32), in_=keys_words[0].bitcast(I32))
         nc.sync.dma_start(q_list[:], offs)
-        load_scale_rows(k_bytes, keys_scales, [nc.sync, nc.sync, nc.scalar, nc.scalar])
+        load_scale_rows(k_bytes, keys_scales, [nc.sync] * 4)
         nc.sync.dma_start(out=q_words[:].bitcast(I32), in_=qpool_words[0].rearrange("p n t -> p (n t)").bitcast(I32))
-        load_scale_rows(q_bytes, qpool_scales, [nc.scalar] * 4)
+        load_scale_rows(q_bytes, qpool_scales, [nc.sync] * 4)
 
         warm = tile([P, 1], F32, "warm")
         nc.scalar.activation(warm[:], windows[0][:, 0:1], ACT.Exp)
@@ -86,11 +86,11 @@ def tile_attend_pickboth_kernel(tc, qpool_words, qpool_scales, keys_words, keys_
             nc.sync.dma_start(out=rows[:], in_=mask[first * P : (first + count) * P, :].rearrange("(a p) j -> p a j", p=P))
             mask_sb.extend(rows[:, a, :] for a in range(count))
 
-        nc.scalar.dma_start(out=size_col[:], in_=size.rearrange("o (p c) -> p (o c)", c=PACK))
         load_values(0, nc.sync)
         load_mask(1)
         load_mask(1)
         load_mask(2)
+        nc.sync.dma_start(out=size_col[:], in_=size.rearrange("o (p c) -> p (o c)", c=PACK))
         load_values(2, nc.sync, 0, 2)
         load_values(2, nc.sync, 1, 2)
         load_values(1, nc.sync)
@@ -239,7 +239,7 @@ def tile_attend_pickboth_kernel(tc, qpool_words, qpool_scales, keys_words, keys_
         gather_queries(1)
         score(2)
         score(3)
-        windows.append(tile([P, T], F32, "window2", "q_bytes"))
+        windows.append(tile([P, T], F32, "window2", "q_words"))
         nc.gpsimd.memset(windows[2][:], 0.0)
         gather_values(0)
         add_mask(0)

@@ -25,7 +25,7 @@ HALF = 256
 WINDOWS = 3
 ADD_ON_GPSIMD = ()
 CASTS = 4
-ON_SCALAR = (2, 3)
+ON_SCALAR = (0, 3)
 
 
 def tile_attend_pickboth_kernel(tc, qpool_words, qpool_scales, keys_words, keys_scales, vals, mask, size, offs, offs2, out):
@@ -49,7 +49,7 @@ def tile_attend_pickboth_kernel(tc, qpool_words, qpool_scales, keys_words, keys_
         nc.vector.memset(k_bytes[:].bitcast(I32), 0)
         nc.vector.memset(q_bytes[:].bitcast(I32), 0)
         make_identity(nc, ident[:])
-        windows = [tile([P, T], F32, "window%d" % w) for w in range(2)]
+        windows = [tile([P, T], F32, "window%d" % w) for w in range(WINDOWS)]
         for window in windows:
             nc.vector.memset(window[:].bitcast(I32), 0)
 
@@ -86,14 +86,13 @@ def tile_attend_pickboth_kernel(tc, qpool_words, qpool_scales, keys_words, keys_
             nc.sync.dma_start(out=rows[:], in_=mask[first * P : (first + count) * P, :].rearrange("(a p) j -> p a j", p=P))
             mask_sb.extend(rows[:, a, :] for a in range(count))
 
-        load_values(0, nc.sync)
-        load_mask(1)
-        load_mask(1)
+        load_values(0, nc.sync, 0, 2)
+        load_mask(2)
+        load_values(0, nc.sync, 1, 2)
         load_mask(2)
         nc.sync.dma_start(out=size_col[:], in_=size.rearrange("o (p c) -> p (o c)", c=PACK))
-        load_values(2, nc.sync, 0, 2)
-        load_values(2, nc.sync, 1, 2)
         load_values(1, nc.sync)
+        load_values(2, nc.sync)
         load_values(3, nc.sync, 0, 2)
         load_values(3, nc.sync, 1, 2)
 
@@ -134,7 +133,7 @@ def tile_attend_pickboth_kernel(tc, qpool_words, qpool_scales, keys_words, keys_
         p_sb = [tile([P, J], F32, "p%d" % i) for i in range(TILES)]
         neg_max = [tile([P, 1], F32, "neg_max%d" % i) for i in range(TILES)]
         row_sum = [tile([P, 1], F32, "row_sum%d" % i) for i in range(TILES)]
-        inv_sum = [tile([P, 1], F32, "inv_sum%d" % i) for i in range(TILES)]
+        inv_sum = [tile([P, 1], F32, "inv_sum%d" % i, "mask2" if i == 0 else None) for i in range(TILES)]
         w_turn = [ps.tile([P, 2, P], F32, name="w_turn%d" % b) for b in range(2)]
         w_grouped = tile([P, I * PACK], BF16, "w_grouped")
         w_codes = tile([P, I], U32, "w_codes")
@@ -161,19 +160,17 @@ def tile_attend_pickboth_kernel(tc, qpool_words, qpool_scales, keys_words, keys_
         def invert(i):
             nc.vector.reciprocal(inv_sum[i][:], row_sum[i][:])
 
-        last_rows = tile([P, 2 * J], BF16, "last_rows")
-
         def weights(i):
-            w_rows = last_rows[:, HALF : HALF + J] if i == TILES - 1 else tile([P, J], BF16, "w%d" % i)[:]
+            w_rows = tile([P, J], BF16, "w%d" % i, None)
             nc.vector.scalar_tensor_tensor(
-                w_rows.rearrange("m (p c) -> m p c", c=PACK),
+                w_rows[:].rearrange("m (p c) -> m p c", c=PACK),
                 p_sb[i][:].rearrange("m (p c) -> m p c", c=PACK),
                 inv_sum[i][:],
                 size_ps[:].rearrange("m c p -> m p c"),
                 ALU.mult,
                 ALU.mult,
             )
-            turn(w_rows, w_turn[i % 2], w_grouped[:, i * P * PACK : (i + 1) * P * PACK])
+            turn(w_rows[:], w_turn[i % 2], w_grouped[:, i * P * PACK : (i + 1) * P * PACK])
 
         def quantise_weights(h):
             cols = slice(h * HALF, (h + 1) * HALF)
@@ -186,7 +183,7 @@ def tile_attend_pickboth_kernel(tc, qpool_words, qpool_scales, keys_words, keys_
         v_codes = [tile([P, P], U32, "v_codes%d" % e) for e in range(TILES)]
         v_scale = [tile([P, P], U8, "v_scale%d" % e) for e in range(TILES)]
 
-        v_rows = {2: last_rows[:, :J]}
+        v_rows = {}
 
         rounded = {}
 
@@ -198,23 +195,23 @@ def tile_attend_pickboth_kernel(tc, qpool_words, qpool_scales, keys_words, keys_
 
         def gather_values(e, on=None, halves=(0, 1)):
             if e not in v_rows:
-                v_rows[e] = tile([P, J], BF16, "v_rows%d" % e, on)[:]
+                v_rows[e] = tile([P, J], BF16, "v_rows%d" % e, on)
             if e in ON_SCALAR:
                 for h in halves:
                     entries = k_list[:, h * HALF // 16 : (h + 1) * HALF // 16]
                     nc.scalar.activation(v_rows[e][:, h * HALF : (h + 1) * HALF], rounded[e][:].indirect(entries), ACT.Copy)
             else:
-                nc.vector.tensor_copy(v_rows[e], vals_sb[e][:].indirect(k_list[:]))
+                nc.vector.tensor_copy(v_rows[e][:], vals_sb[e][:].indirect(k_list[:]))
 
         def values(e, bank="v_turn", on=None):
             v_turn = ps.tile([P, 2, P], F32, name="v_turn%d" % e, tag=bank)
             v_grouped = tile([P, P * PACK], BF16, "v_grouped%d" % e, on)
-            turn(v_rows[e], v_turn, v_grouped[:])
+            turn(v_rows[e][:], v_turn, v_grouped[:])
             nc.vector.quantize_mx(out=v_codes[e][:].bitcast(FP8X4), scales=v_scale[e][:], in_=v_grouped[:])
 
         place = [0, 1, 2, 0]
 
-        def product(e, first, last, bank, on, view=None):
+        def product(e, first, last, bank, on):
             cols = slice(first, last)
             o_ps = ps.tile([P, last - first], F32, name="o_ps%d_%d" % (e, first), tag="bank%d" % bank)
             nc.tensor.matmul_mx(
@@ -226,9 +223,26 @@ def tile_attend_pickboth_kernel(tc, qpool_words, qpool_scales, keys_words, keys_
                 start=True,
                 stop=True,
             )
-            o_sb = view if view is not None else tile([P, last - first], F32, "o_sb%d_%d" % (e, first), on)[:]
-            nc.scalar.copy(o_sb, o_ps[:])
-            nc.vector.tensor_copy(windows[place[e]][:].indirect(q_list[:, first // 16 : last // 16]), o_sb)
+            o_sb = tile([P, last - first], F32, "o_sb%d_%d" % (e, first), on)
+            nc.scalar.copy(o_sb[:], o_ps[:])
+            nc.vector.tensor_copy(windows[place[e]][:].indirect(q_list[:, first // 16 : last // 16]), o_sb[:])
+
+        def product_in_two(e, banks):
+            o_sb = tile([P, I], F32, "o_sb%d" % e)
+            for h in range(2):
+                cols = slice(h * HALF, (h + 1) * HALF)
+                o_ps = ps.tile([P, HALF], F32, name="o_ps%d_%d" % (e, h), tag="bank%d" % banks[h])
+                nc.tensor.matmul_mx(
+                    out=o_ps[:],
+                    lhsT=v_codes[e][:].bitcast(FP8X4),
+                    lhsT_scale=v_scale[e][:],
+                    rhs=w_codes[:, cols].bitcast(FP8X4),
+                    rhs_scale=w_scale[:, cols],
+                    start=True,
+                    stop=True,
+                )
+                nc.scalar.copy(o_sb[:, cols], o_ps[:])
+            nc.vector.tensor_copy(windows[place[e]][:].indirect(q_list[:]), o_sb[:])
 
         def store(e):
             nc.sync.dma_start(out=out[e * P : (e + 1) * P, :], in_=windows[place[e]][:])
@@ -239,44 +253,41 @@ def tile_attend_pickboth_kernel(tc, qpool_words, qpool_scales, keys_words, keys_
         gather_queries(1)
         score(2)
         score(3)
-        windows.append(tile([P, T], F32, "window2", "q_words"))
-        nc.gpsimd.memset(windows[2][:], 0.0)
-        gather_values(0)
         add_mask(0)
         add_mask(1)
         exponentials(0)
         exponentials(1)
-        values(0)
+        round_values(0)
+        gather_values(0, "s1")
         add_mask(2)
         add_mask(3)
-        invert(0)
         exponentials(2)
-        weights(0)
+        invert(0)
         invert(1)
         exponentials(3)
+        gather_values(1)
+        weights(0)
         weights(1)
         invert(2)
-        weights(2)
         invert(3)
-        quantise_weights(0)
+        values(0, "v_turn", "s2")
+        weights(2)
         weights(3)
-        gather_values(1, "p3")
-        quantise_weights(1)
-        product(0, 0, HALF, 0, None, last_rows[:, J:].bitcast(F32))
-        values(1, "bank0")
-        product(0, HALF, I, 1, None)
-        store(0)
-        product(1, 0, HALF, 2, None)
-        round_values(2)
+        quantise_weights(0)
+        values(1)
         gather_values(2)
-        values(2, "bank1")
-        product(1, HALF, I, 3, None, last_rows[:, :J].bitcast(F32))
+        quantise_weights(1)
+        product(0, 0, HALF, 0, "w3")
+        values(2, "bank0")
+        product(0, HALF, I, 1, "v_rows2")
+        store(0)
+        product(1, 0, I, 1, None)
         store(1)
-        round_values(3, "rounded2")
+        product(2, 0, HALF, 2, None)
+        round_values(3, "w2")
         gather_values(3)
-        product(2, 0, HALF, 0, "rounded2")
         values(3)
-        product(2, HALF, I, 1, "v_rows3")
+        product(2, HALF, I, 0, "v_rows3")
         store(2)
-        product(3, 0, I, 2, None)
+        product_in_two(3, (3, 1))
         store(3)

@@ -49,7 +49,7 @@ def tile_attend_pickboth_kernel(tc, qpool_words, qpool_scales, keys_words, keys_
         nc.vector.memset(k_bytes[:].bitcast(I32), 0)
         nc.vector.memset(q_bytes[:].bitcast(I32), 0)
         make_identity(nc, ident[:])
-        windows = [tile([P, T], F32, "window%d" % w) for w in range(WINDOWS)]
+        windows = [tile([P, T], F32, "window%d" % w) for w in range(1)]
         for window in windows:
             nc.vector.memset(window[:].bitcast(I32), 0)
 
@@ -253,6 +253,9 @@ def tile_attend_pickboth_kernel(tc, qpool_words, qpool_scales, keys_words, keys_
         gather_queries(1)
         score(2)
         score(3)
+        for w, on in ((1, "q_words"), (2, "q_bytes")):
+            windows.append(tile([P, T], F32, "window%d" % w, on))
+            nc.gpsimd.memset(windows[w][:], 0.0)
         add_mask(0)
         add_mask(1)
         exponentials(0)

@@ -23,9 +23,7 @@ PACK = 4
 TILES = 4
 HALF = 256
 WINDOWS = 3
-ADD_ON_GPSIMD = ()
-CASTS = 4
-ON_SCALAR = (0, 3)
+PIECES = 4
 
 
 def tile_attend_pickboth_kernel(tc, qpool_words, qpool_scales, keys_words, keys_scales, vals, mask, size, offs, offs2, out):
@@ -36,6 +34,12 @@ def tile_attend_pickboth_kernel(tc, qpool_words, qpool_scales, keys_words, keys_
 
         def tile(shape, dtype, name, on=None):
             return sb.tile(shape, dtype, name=name, tag=on or name, align_bytes=64)
+
+        def half(h):
+            return slice(h * HALF, (h + 1) * HALF)
+
+        def entries(whole, first, last):
+            return whole[:, first // 16 : last // 16]
 
         q_list = sb.tile([P, I // 16], U16, name="q_list")
         k_list = sb.tile([P, J // 16], U16, name="k_list")
@@ -49,52 +53,43 @@ def tile_attend_pickboth_kernel(tc, qpool_words, qpool_scales, keys_words, keys_
         nc.vector.memset(k_bytes[:].bitcast(I32), 0)
         nc.vector.memset(q_bytes[:].bitcast(I32), 0)
         make_identity(nc, ident[:])
-        windows = [tile([P, T], F32, "window%d" % w) for w in range(1)]
-        for window in windows:
-            nc.vector.memset(window[:].bitcast(I32), 0)
+        windows = [tile([P, T], F32, "window0")]
+        nc.vector.memset(windows[0][:].bitcast(I32), 0)
 
-        def load_scale_rows(plane, rows, queue):
+        def load_scale_rows(pool_bytes, rows):
             for quad in range(4):
-                queue[quad].dma_start(
-                    out=plane[32 * quad : 32 * quad + 4, :].bitcast(I32),
+                nc.sync.dma_start(
+                    out=pool_bytes[32 * quad : 32 * quad + 4, :].bitcast(I32),
                     in_=rows[0, 4 * quad : 4 * quad + 4, :].bitcast(I32),
                 )
 
-        nc.sync.dma_start(k_list[:], offs2)
-        nc.sync.dma_start(out=k_words[:].bitcast(I32), in_=keys_words[0].bitcast(I32))
-        nc.sync.dma_start(q_list[:], offs)
-        load_scale_rows(k_bytes, keys_scales, [nc.sync] * 4)
-        nc.sync.dma_start(out=q_words[:].bitcast(I32), in_=qpool_words[0].rearrange("p n t -> p (n t)").bitcast(I32))
-        load_scale_rows(q_bytes, qpool_scales, [nc.sync] * 4)
-
-        warm = tile([P, 1], F32, "warm")
-        nc.scalar.activation(warm[:], windows[0][:, 0:1], ACT.Exp)
-
-        vals_sb = {}
-
-        def load_values(e, queue, part=0, parts=1, on=None):
-            if e not in vals_sb:
-                vals_sb[e] = tile([P, T], F32, "vals%d" % e, on)
-            cols = slice(part * T // parts, (part + 1) * T // parts)
-            queue.dma_start(out=vals_sb[e][:, cols], in_=vals[e * P : (e + 1) * P, cols])
-
+        vals_sb = [tile([P, T], F32, "vals%d" % e) for e in range(TILES)]
         mask_sb = []
 
-        def load_mask(count):
-            first = len(mask_sb)
-            rows = tile([P, count, J], F32, "mask%d" % first)
-            nc.sync.dma_start(out=rows[:], in_=mask[first * P : (first + count) * P, :].rearrange("(a p) j -> p a j", p=P))
-            mask_sb.extend(rows[:, a, :] for a in range(count))
+        def load_values(e, first, last):
+            nc.sync.dma_start(out=vals_sb[e][:, first:last], in_=vals[e * P : (e + 1) * P, first:last])
 
-        load_values(0, nc.sync, 0, 2)
-        load_mask(2)
-        load_values(0, nc.sync, 1, 2)
-        load_mask(2)
+        def load_mask_pair():
+            first = len(mask_sb)
+            rows = tile([P, 2, J], F32, "mask%d" % first)
+            nc.sync.dma_start(out=rows[:], in_=mask[first * P : (first + 2) * P, :].rearrange("(a p) j -> p a j", p=P))
+            mask_sb.extend(rows[:, a, :] for a in range(2))
+
+        nc.sync.dma_start(k_list[:], offs2)
+        nc.sync.dma_start(q_list[:], offs)
+        load_scale_rows(k_bytes, keys_scales)
+        nc.sync.dma_start(out=k_words[:].bitcast(I32), in_=keys_words[0].bitcast(I32))
+        load_scale_rows(q_bytes, qpool_scales)
+        nc.sync.dma_start(out=q_words[:].bitcast(I32), in_=qpool_words[0].rearrange("p n t -> p (n t)").bitcast(I32))
+        load_values(0, 0, T // 2)
+        load_mask_pair()
+        load_values(0, T // 2, T)
+        load_mask_pair()
         nc.sync.dma_start(out=size_col[:], in_=size.rearrange("o (p c) -> p (o c)", c=PACK))
-        load_values(1, nc.sync)
-        load_values(2, nc.sync)
-        load_values(3, nc.sync, 0, 2)
-        load_values(3, nc.sync, 1, 2)
+        load_values(1, 0, T)
+        load_values(2, 0, T)
+        load_values(3, 0, T // 2)
+        load_values(3, T // 2, T)
 
         size_ps = ps.tile([P, PACK, P], F32, name="size_ps")
         for c in range(PACK):
@@ -109,13 +104,10 @@ def tile_attend_pickboth_kernel(tc, qpool_words, qpool_scales, keys_words, keys_
 
         scores = [ps.tile([P, J], F32, name="scores%d" % i, tag="bank%d" % i) for i in range(TILES)]
 
-        def listed(h):
-            return q_list[:, h * HALF // 16 : (h + 1) * HALF // 16]
-
-        def gather_queries(h):
-            cols = slice(h * HALF, (h + 1) * HALF)
-            nc.vector.tensor_copy(q_scale[:, cols], q_bytes[:].indirect(listed(h)))
-            nc.vector.tensor_copy(q_codes[:, cols], q_words[:].indirect(listed(h)))
+        def pick_queries(h):
+            listed = entries(q_list, h * HALF, (h + 1) * HALF)
+            nc.vector.tensor_copy(q_scale[:, half(h)], q_bytes[:].indirect(listed))
+            nc.vector.tensor_copy(q_codes[:, half(h)], q_words[:].indirect(listed))
 
         def score(i):
             cols = slice(i * P, (i + 1) * P)
@@ -133,19 +125,14 @@ def tile_attend_pickboth_kernel(tc, qpool_words, qpool_scales, keys_words, keys_
         p_sb = [tile([P, J], F32, "p%d" % i) for i in range(TILES)]
         neg_max = [tile([P, 1], F32, "neg_max%d" % i) for i in range(TILES)]
         row_sum = [tile([P, 1], F32, "row_sum%d" % i) for i in range(TILES)]
-        inv_sum = [tile([P, 1], F32, "inv_sum%d" % i, "mask2" if i == 0 else None) for i in range(TILES)]
+        inv_sum = [tile([P, 1], F32, "inv_sum0", "mask2")] + [tile([P, 1], F32, "inv_sum%d" % i) for i in range(1, TILES)]
         w_turn = [ps.tile([P, 2, P], F32, name="w_turn%d" % b) for b in range(2)]
         w_grouped = tile([P, I * PACK], BF16, "w_grouped")
         w_codes = tile([P, I], U32, "w_codes")
         w_scale = tile([P, I], U8, "w_scale")
 
         def add_mask(i):
-            if i in ADD_ON_GPSIMD:
-                a_sb = tile([P, J], F32, "a%d" % i)
-                nc.scalar.activation(a_sb[:], scores[i][:], ACT.Copy)
-                nc.gpsimd.tensor_tensor(s_sb[i][:], a_sb[:], mask_sb[i], ALU.add)
-            else:
-                nc.vector.tensor_tensor(s_sb[i][:], scores[i][:], mask_sb[i], ALU.add)
+            nc.vector.tensor_tensor(s_sb[i][:], scores[i][:], mask_sb[i], ALU.add)
 
         def exponentials(i):
             nc.vector.tensor_reduce(neg_max[i][:], s_sb[i][:], AX.X, ALU.max, negate=True)
@@ -161,7 +148,7 @@ def tile_attend_pickboth_kernel(tc, qpool_words, qpool_scales, keys_words, keys_
             nc.vector.reciprocal(inv_sum[i][:], row_sum[i][:])
 
         def weights(i):
-            w_rows = tile([P, J], BF16, "w%d" % i, None)
+            w_rows = tile([P, J], BF16, "w%d" % i)
             nc.vector.scalar_tensor_tensor(
                 w_rows[:].rearrange("m (p c) -> m p c", c=PACK),
                 p_sb[i][:].rearrange("m (p c) -> m p c", c=PACK),
@@ -173,124 +160,104 @@ def tile_attend_pickboth_kernel(tc, qpool_words, qpool_scales, keys_words, keys_
             turn(w_rows[:], w_turn[i % 2], w_grouped[:, i * P * PACK : (i + 1) * P * PACK])
 
         def quantise_weights(h):
-            cols = slice(h * HALF, (h + 1) * HALF)
             nc.vector.quantize_mx(
-                out=w_codes[:, cols].bitcast(FP8X4),
-                scales=w_scale[:, cols],
+                out=w_codes[:, half(h)].bitcast(FP8X4),
+                scales=w_scale[:, half(h)],
                 in_=w_grouped[:, h * HALF * PACK : (h + 1) * HALF * PACK],
             )
 
         v_codes = [tile([P, P], U32, "v_codes%d" % e) for e in range(TILES)]
         v_scale = [tile([P, P], U8, "v_scale%d" % e) for e in range(TILES)]
-
         v_rows = {}
 
-        rounded = {}
+        def pick_values_on_vector(e):
+            v_rows[e] = tile([P, J], BF16, "v_rows%d" % e)
+            nc.vector.tensor_copy(v_rows[e][:], vals_sb[e][:].indirect(k_list[:]))
 
-        def round_values(e, on=None):
-            rounded[e] = tile([P, T], BF16, "rounded%d" % e, on)
-            for c in range(CASTS):
-                cols = slice(c * T // CASTS, (c + 1) * T // CASTS)
-                nc.scalar.activation(rounded[e][:, cols], vals_sb[e][:, cols], ACT.Copy)
+        def pick_values_on_scalar(e, rounded_on, rows_on):
+            rounded = tile([P, T], BF16, "rounded%d" % e, rounded_on)
+            for c in range(PIECES):
+                cols = slice(c * T // PIECES, (c + 1) * T // PIECES)
+                nc.scalar.activation(rounded[:, cols], vals_sb[e][:, cols], ACT.Copy)
+            v_rows[e] = tile([P, J], BF16, "v_rows%d" % e, rows_on)
+            for h in range(2):
+                nc.scalar.activation(v_rows[e][:, half(h)], rounded[:].indirect(entries(k_list, h * HALF, (h + 1) * HALF)), ACT.Copy)
 
-        def gather_values(e, on=None, halves=(0, 1)):
-            if e not in v_rows:
-                v_rows[e] = tile([P, J], BF16, "v_rows%d" % e, on)
-            if e in ON_SCALAR:
-                for h in halves:
-                    entries = k_list[:, h * HALF // 16 : (h + 1) * HALF // 16]
-                    nc.scalar.activation(v_rows[e][:, h * HALF : (h + 1) * HALF], rounded[e][:].indirect(entries), ACT.Copy)
-            else:
-                nc.vector.tensor_copy(v_rows[e][:], vals_sb[e][:].indirect(k_list[:]))
-
-        def values(e, bank="v_turn", on=None):
+        def quantise_values(e, bank="v_turn", grouped_on=None):
             v_turn = ps.tile([P, 2, P], F32, name="v_turn%d" % e, tag=bank)
-            v_grouped = tile([P, P * PACK], BF16, "v_grouped%d" % e, on)
+            v_grouped = tile([P, P * PACK], BF16, "v_grouped%d" % e, grouped_on)
             turn(v_rows[e][:], v_turn, v_grouped[:])
             nc.vector.quantize_mx(out=v_codes[e][:].bitcast(FP8X4), scales=v_scale[e][:], in_=v_grouped[:])
 
-        place = [0, 1, 2, 0]
-
-        def product(e, first, last, bank, on):
-            cols = slice(first, last)
+        def multiply(e, first, last, bank, sums):
             o_ps = ps.tile([P, last - first], F32, name="o_ps%d_%d" % (e, first), tag="bank%d" % bank)
             nc.tensor.matmul_mx(
                 out=o_ps[:],
                 lhsT=v_codes[e][:].bitcast(FP8X4),
                 lhsT_scale=v_scale[e][:],
-                rhs=w_codes[:, cols].bitcast(FP8X4),
-                rhs_scale=w_scale[:, cols],
+                rhs=w_codes[:, first:last].bitcast(FP8X4),
+                rhs_scale=w_scale[:, first:last],
                 start=True,
                 stop=True,
             )
-            o_sb = tile([P, last - first], F32, "o_sb%d_%d" % (e, first), on)
-            nc.scalar.copy(o_sb[:], o_ps[:])
-            nc.vector.tensor_copy(windows[place[e]][:].indirect(q_list[:, first // 16 : last // 16]), o_sb[:])
+            nc.scalar.copy(sums, o_ps[:])
 
-        def product_in_two(e, banks):
-            o_sb = tile([P, I], F32, "o_sb%d" % e)
-            for h in range(2):
-                cols = slice(h * HALF, (h + 1) * HALF)
-                o_ps = ps.tile([P, HALF], F32, name="o_ps%d_%d" % (e, h), tag="bank%d" % banks[h])
-                nc.tensor.matmul_mx(
-                    out=o_ps[:],
-                    lhsT=v_codes[e][:].bitcast(FP8X4),
-                    lhsT_scale=v_scale[e][:],
-                    rhs=w_codes[:, cols].bitcast(FP8X4),
-                    rhs_scale=w_scale[:, cols],
-                    start=True,
-                    stop=True,
-                )
-                nc.scalar.copy(o_sb[:, cols], o_ps[:])
-            nc.vector.tensor_copy(windows[place[e]][:].indirect(q_list[:]), o_sb[:])
+        def scatter(e, first, last, sums):
+            nc.vector.tensor_copy(windows[e % WINDOWS][:].indirect(entries(q_list, first, last)), sums)
+
+        def product(e, first, last, bank, sums_on=None):
+            sums = tile([P, last - first], F32, "sums%d_%d" % (e, first), sums_on)
+            multiply(e, first, last, bank, sums[:])
+            scatter(e, first, last, sums[:])
 
         def store(e):
-            nc.sync.dma_start(out=out[e * P : (e + 1) * P, :], in_=windows[place[e]][:])
+            nc.sync.dma_start(out=out[e * P : (e + 1) * P, :], in_=windows[e % WINDOWS][:])
 
-        gather_queries(0)
-        score(0)
-        score(1)
-        gather_queries(1)
-        score(2)
-        score(3)
+        for h in range(2):
+            pick_queries(h)
+            score(2 * h)
+            score(2 * h + 1)
         for w, on in ((1, "q_words"), (2, "q_bytes")):
             windows.append(tile([P, T], F32, "window%d" % w, on))
             nc.gpsimd.memset(windows[w][:], 0.0)
+
         add_mask(0)
         add_mask(1)
         exponentials(0)
         exponentials(1)
-        round_values(0)
-        gather_values(0, "s1")
+        pick_values_on_scalar(0, None, "s1")
         add_mask(2)
         add_mask(3)
         exponentials(2)
         invert(0)
         invert(1)
         exponentials(3)
-        gather_values(1)
+        pick_values_on_vector(1)
         weights(0)
         weights(1)
         invert(2)
         invert(3)
-        values(0, "v_turn", "s2")
+        quantise_values(0, grouped_on="s2")
         weights(2)
         weights(3)
         quantise_weights(0)
-        values(1)
-        gather_values(2)
+        quantise_values(1)
+        pick_values_on_vector(2)
         quantise_weights(1)
+
         product(0, 0, HALF, 0, "w3")
-        values(2, "bank0")
+        quantise_values(2, "bank0")
         product(0, HALF, I, 1, "v_rows2")
         store(0)
-        product(1, 0, I, 1, None)
+        product(1, 0, I, 1)
         store(1)
-        product(2, 0, HALF, 2, None)
-        round_values(3, "w2")
-        gather_values(3)
-        values(3)
+        product(2, 0, HALF, 2)
+        pick_values_on_scalar(3, "w2", None)
+        quantise_values(3)
         product(2, HALF, I, 0, "v_rows3")
         store(2)
-        product_in_two(3, (3, 1))
+        last_sums = tile([P, I], F32, "sums3")
+        for h, bank in enumerate((3, 1)):
+            multiply(3, h * HALF, (h + 1) * HALF, bank, last_sums[:, half(h)])
+        scatter(3, 0, I, last_sums[:])
         store(3)

@@ -31,9 +31,13 @@ def tile_attend_pickboth_kernel(tc, qpool_words, qpool_scales, keys_words, keys_
     with ExitStack() as ctx:
         sb = ctx.enter_context(tc.tile_pool(name="sb", bufs=1))
         ps = ctx.enter_context(tc.psum_pool(name="ps", bufs=1))
+        shared = ctx.enter_context(tc.tile_pool(name="shared", bufs=1))
 
         def tile(shape, dtype, name, on=None):
             return sb.tile(shape, dtype, name=name, tag=on or name, align_bytes=64)
+
+        def placed(shape, dtype, name, kib):
+            return shared.tile(shape, dtype, name=name, offset=int(1024 * kib), align_bytes=64)
 
         def half(h):
             return slice(h * HALF, (h + 1) * HALF)
@@ -53,8 +57,10 @@ def tile_attend_pickboth_kernel(tc, qpool_words, qpool_scales, keys_words, keys_
         nc.vector.memset(k_bytes[:].bitcast(I32), 0)
         nc.vector.memset(q_bytes[:].bitcast(I32), 0)
         make_identity(nc, ident[:])
-        windows = [tile([P, T], F32, "window0")]
+        windows = [tile([P, T], F32, "window%d" % w) for w in range(WINDOWS)]
         nc.vector.memset(windows[0][:].bitcast(I32), 0)
+        for w in range(1, WINDOWS):
+            nc.gpsimd.memset(windows[w][:], 0.0)
 
         def load_scale_rows(pool_bytes, rows):
             for quad in range(4):
@@ -63,37 +69,47 @@ def tile_attend_pickboth_kernel(tc, qpool_words, qpool_scales, keys_words, keys_
                     in_=rows[0, 4 * quad : 4 * quad + 4, :].bitcast(I32),
                 )
 
-        vals_sb = [tile([P, T], F32, "vals%d" % e) for e in range(TILES)]
+        vals_sb = {0: tile([P, T], F32, "vals0"), 1: placed([P, T], F32, "vals1", 0)}
+        pieces = {}
         mask_sb = []
 
-        def load_values(e, first, last):
-            nc.sync.dma_start(out=vals_sb[e][:, first:last], in_=vals[e * P : (e + 1) * P, first:last])
+        def load_values(e):
+            nc.sync.dma_start(out=vals_sb[e][:], in_=vals[e * P : (e + 1) * P, :])
 
-        def load_mask_pair():
+        def load_piece(e, first, last, piece):
+            pieces[e, first] = piece
+            nc.sync.dma_start(out=piece[:], in_=vals[e * P : (e + 1) * P, first:last])
+
+        def load_mask(count):
             first = len(mask_sb)
-            rows = tile([P, 2, J], F32, "mask%d" % first)
-            nc.sync.dma_start(out=rows[:], in_=mask[first * P : (first + 2) * P, :].rearrange("(a p) j -> p a j", p=P))
-            mask_sb.extend(rows[:, a, :] for a in range(2))
+            rows = tile([P, count, J], F32, "mask%d" % first)
+            nc.sync.dma_start(out=rows[:], in_=mask[first * P : (first + count) * P, :].rearrange("(a p) j -> p a j", p=P))
+            mask_sb.extend(rows[:, a, :] for a in range(count))
 
         nc.sync.dma_start(k_list[:], offs2)
         nc.sync.dma_start(q_list[:], offs)
+        nc.sync.dma_start(out=size_col[:], in_=size.rearrange("o (p c) -> p (o c)", c=PACK))
         load_scale_rows(k_bytes, keys_scales)
         nc.sync.dma_start(out=k_words[:].bitcast(I32), in_=keys_words[0].bitcast(I32))
         load_scale_rows(q_bytes, qpool_scales)
         nc.sync.dma_start(out=q_words[:].bitcast(I32), in_=qpool_words[0].rearrange("p n t -> p (n t)").bitcast(I32))
-        load_values(0, 0, T // 2)
-        load_mask_pair()
-        load_values(0, T // 2, T)
-        load_mask_pair()
-        nc.sync.dma_start(out=size_col[:], in_=size.rearrange("o (p c) -> p (o c)", c=PACK))
-        load_values(1, 0, T)
-        load_values(2, 0, T)
-        load_values(3, 0, T // 2)
-        load_values(3, T // 2, T)
+        load_piece(2, 0, 512, tile([P, 512], F32, "vals2a"))
+        load_mask(2)
+        load_piece(2, 512, 1024, tile([P, 512], F32, "vals2b"))
+        load_mask(1)
+        load_mask(1)
+        load_values(0)
+        load_piece(2, 1024, 1536, placed([P, 512], F32, "vals2c", 11))
+        load_values(1)
+        load_piece(2, 1536, 2048, placed([P, 512], F32, "vals2d", 27))
+        load_piece(3, 0, 1024, tile([P, 1024], F32, "vals3a"))
+        load_piece(3, 1024, 2048, tile([P, 1024], F32, "vals3b"))
 
         size_ps = ps.tile([P, PACK, P], F32, name="size_ps")
         for c in range(PACK):
             nc.tensor.transpose(size_ps[:, c, :], size_col[:, c : c + 1].to_broadcast([P, P]), ident[:])
+        size_sb = tile([P, J], F32, "size_sb")
+        nc.scalar.activation(size_sb[:].rearrange("m (p c) -> m p c", c=PACK), size_ps[:].rearrange("m c p -> m p c"), ACT.Copy)
 
         k_codes = tile([P, J], U16, "k_codes")
         k_scale = tile([P, J], U8, "k_scale")
@@ -121,22 +137,26 @@ def tile_attend_pickboth_kernel(tc, qpool_words, qpool_scales, keys_words, keys_
                 stop=True,
             )
 
-        s_sb = [tile([P, J], F32, "s%d" % i) for i in range(TILES)]
+        s_sb = [tile([P, J], F32, "s%d" % i) for i in range(TILES - 1)] + [placed([P, J], F32, "s3", 24)]
         p_sb = [tile([P, J], F32, "p%d" % i) for i in range(TILES)]
-        neg_max = [tile([P, 1], F32, "neg_max%d" % i) for i in range(TILES)]
         row_sum = [tile([P, 1], F32, "row_sum%d" % i) for i in range(TILES)]
-        inv_sum = [tile([P, 1], F32, "inv_sum0", "mask2")] + [tile([P, 1], F32, "inv_sum%d" % i) for i in range(1, TILES)]
-        w_turn = [ps.tile([P, 2, P], F32, name="w_turn%d" % b) for b in range(2)]
-        w_grouped = tile([P, I * PACK], BF16, "w_grouped")
-        w_codes = tile([P, I], U32, "w_codes")
-        w_scale = tile([P, I], U8, "w_scale")
+        inv_sum = {}
+        w_grouped = [placed([P, HALF * PACK], BF16, "w_grouped0", 10), placed([P, HALF * PACK], BF16, "w_grouped1", 26)]
+        w_scale = [tile([P, HALF], U8, "w_scale%d" % h) for h in range(2)]
+        w_codes = {}
 
         def add_mask(i):
             nc.vector.tensor_tensor(s_sb[i][:], scores[i][:], mask_sb[i], ALU.add)
 
-        def exponentials(i):
-            nc.vector.tensor_reduce(neg_max[i][:], s_sb[i][:], AX.X, ALU.max, negate=True)
-            nc.scalar.activation(p_sb[i][:], s_sb[i][:], ACT.Exp, bias=neg_max[i][:], accum_out=row_sum[i][:])
+        def add_mask_on_gpsimd(i, on=None):
+            raw = tile([P, J], F32, "raw%d" % i, on)
+            nc.scalar.copy(raw[:], scores[i][:])
+            nc.gpsimd.tensor_tensor(s_sb[i][:], raw[:], mask_sb[i], ALU.add)
+
+        def exponentials(i, max_on=None):
+            neg_max = tile([P, 1], F32, "neg_max%d" % i, max_on)
+            nc.vector.tensor_reduce(neg_max[:], s_sb[i][:], AX.X, ALU.max, negate=True)
+            nc.scalar.activation(p_sb[i][:], s_sb[i][:], ACT.Exp, bias=neg_max[:], accum_out=row_sum[i][:])
 
         def turn(rows, bank, grouped):
             words = rows.bitcast(F32)
@@ -145,10 +165,10 @@ def tile_attend_pickboth_kernel(tc, qpool_words, qpool_scales, keys_words, keys_
             nc.scalar.copy(grouped.bitcast(F32).rearrange("p (r u) -> p r u", u=2), bank[:].rearrange("p u r -> p r u"))
 
         def invert(i):
+            inv_sum[i] = placed([P, 1], F32, "inv_sum2", 25) if i == 2 else tile([P, 1], F32, "inv_sum%d" % i)
             nc.vector.reciprocal(inv_sum[i][:], row_sum[i][:])
 
-        def weights(i):
-            w_rows = tile([P, J], BF16, "w%d" % i)
+        def weights(i, w_rows):
             nc.vector.scalar_tensor_tensor(
                 w_rows[:].rearrange("m (p c) -> m p c", c=PACK),
                 p_sb[i][:].rearrange("m (p c) -> m p c", c=PACK),
@@ -157,46 +177,60 @@ def tile_attend_pickboth_kernel(tc, qpool_words, qpool_scales, keys_words, keys_
                 ALU.mult,
                 ALU.mult,
             )
-            turn(w_rows[:], w_turn[i % 2], w_grouped[:, i * P * PACK : (i + 1) * P * PACK])
+            turn(w_rows[:], ps.tile([P, 2, P], F32, name="w_turn%d" % i, tag="bank%d" % i if i > 1 else "w_turn%d" % i), w_grouped[i // 2][:, i % 2 * P * PACK : (i % 2 + 1) * P * PACK])
 
-        def quantise_weights(h):
+        def weights_on_gpsimd(i):
+            sized = tile([P, J], F32, "sized%d" % i)
+            nc.gpsimd.tensor_tensor(sized[:], p_sb[i][:], size_sb[:], ALU.mult)
+            w_rows = tile([P, J], BF16, "w%d" % i)
+            nc.gpsimd.tensor_scalar(w_rows[:], sized[:], inv_sum[i][:], 0.0, ALU.mult, ALU.add)
+            turn(w_rows[:], ps.tile([P, 2, P], F32, name="w_turn%d" % i, tag="bank%d" % i if i > 1 else "w_turn%d" % i), w_grouped[i // 2][:, i % 2 * P * PACK : (i % 2 + 1) * P * PACK])
+
+        def quantise_weights(h, codes):
+            w_codes[h] = codes
             nc.vector.quantize_mx(
-                out=w_codes[:, half(h)].bitcast(FP8X4),
-                scales=w_scale[:, half(h)],
-                in_=w_grouped[:, h * HALF * PACK : (h + 1) * HALF * PACK],
+                out=codes[:].bitcast(FP8X4),
+                scales=w_scale[h][:],
+                in_=w_grouped[h][:],
             )
 
-        v_codes = [tile([P, P], U32, "v_codes%d" % e) for e in range(TILES)]
+        v_codes = {}
         v_scale = [tile([P, P], U8, "v_scale%d" % e) for e in range(TILES)]
         v_rows = {}
+        v_grouped = {}
 
         def pick_values_on_vector(e):
             v_rows[e] = tile([P, J], BF16, "v_rows%d" % e)
             nc.vector.tensor_copy(v_rows[e][:], vals_sb[e][:].indirect(k_list[:]))
 
-        def pick_values_on_scalar(e, rounded_on, rows_on):
-            rounded = tile([P, T], BF16, "rounded%d" % e, rounded_on)
-            for c in range(PIECES):
-                cols = slice(c * T // PIECES, (c + 1) * T // PIECES)
-                nc.scalar.activation(rounded[:, cols], vals_sb[e][:, cols], ACT.Copy)
-            v_rows[e] = tile([P, J], BF16, "v_rows%d" % e, rows_on)
+        def round_values(e, piece, first, last):
+            nc.scalar.activation(rounded[e][:, first:last], pieces[e, piece][:, first - piece : last - piece], ACT.Copy)
+
+        def pick_values_on_scalar(e, rows):
+            v_rows[e] = rows
             for h in range(2):
-                nc.scalar.activation(v_rows[e][:, half(h)], rounded[:].indirect(entries(k_list, h * HALF, (h + 1) * HALF)), ACT.Copy)
+                listed = entries(k_list, h * HALF, (h + 1) * HALF)
+                nc.scalar.activation(rows[:, half(h)], rounded[e][:].indirect(listed), ACT.Copy)
 
-        def quantise_values(e, bank="v_turn", grouped_on=None):
-            v_turn = ps.tile([P, 2, P], F32, name="v_turn%d" % e, tag=bank)
-            v_grouped = tile([P, P * PACK], BF16, "v_grouped%d" % e, grouped_on)
-            turn(v_rows[e][:], v_turn, v_grouped[:])
-            nc.vector.quantize_mx(out=v_codes[e][:].bitcast(FP8X4), scales=v_scale[e][:], in_=v_grouped[:])
+        def turn_values(e, grouped):
+            v_grouped[e] = grouped
+            v_turn = ps.tile([P, 2, P], F32, name="v_turn%d" % e, tag="v_turn")
+            turn(v_rows[e][:], v_turn, grouped[:])
 
-        def multiply(e, first, last, bank, sums):
-            o_ps = ps.tile([P, last - first], F32, name="o_ps%d_%d" % (e, first), tag="bank%d" % bank)
+        def quantise_values(e):
+            if e not in v_grouped:
+                turn_values(e, tile([P, P * PACK], BF16, "v_grouped%d" % e))
+            v_codes[e] = tile([P, P], U32, "v_codes%d" % e)
+            nc.vector.quantize_mx(out=v_codes[e][:].bitcast(FP8X4), scales=v_scale[e][:], in_=v_grouped[e][:])
+
+        def multiply(e, h, bank, sums):
+            o_ps = ps.tile([P, HALF], F32, name="o_ps%d_%d" % (e, h), tag="bank%d" % bank)
             nc.tensor.matmul_mx(
                 out=o_ps[:],
                 lhsT=v_codes[e][:].bitcast(FP8X4),
                 lhsT_scale=v_scale[e][:],
-                rhs=w_codes[:, first:last].bitcast(FP8X4),
-                rhs_scale=w_scale[:, first:last],
+                rhs=w_codes[h][:].bitcast(FP8X4),
+                rhs_scale=w_scale[h][:],
                 start=True,
                 stop=True,
             )
@@ -205,59 +239,65 @@ def tile_attend_pickboth_kernel(tc, qpool_words, qpool_scales, keys_words, keys_
         def scatter(e, first, last, sums):
             nc.vector.tensor_copy(windows[e % WINDOWS][:].indirect(entries(q_list, first, last)), sums)
 
-        def product(e, first, last, bank, sums_on=None):
-            sums = tile([P, last - first], F32, "sums%d_%d" % (e, first), sums_on)
-            multiply(e, first, last, bank, sums[:])
-            scatter(e, first, last, sums[:])
+        def half_product(e, h, bank, sums):
+            multiply(e, h, bank, sums[:])
+            scatter(e, h * HALF, (h + 1) * HALF, sums[:])
+
+        def whole_product(e, banks, sums):
+            for h in range(2):
+                multiply(e, h, banks[h], sums[:, half(h)])
+            scatter(e, 0, I, sums[:])
 
         def store(e):
             nc.sync.dma_start(out=out[e * P : (e + 1) * P, :], in_=windows[e % WINDOWS][:])
 
+        rounded = {2: placed([P, T], BF16, "rounded2", 17)}
         for h in range(2):
             pick_queries(h)
-            score(2 * h)
-            score(2 * h + 1)
-        for w, on in ((1, "q_words"), (2, "q_bytes")):
-            windows.append(tile([P, T], F32, "window%d" % w, on))
-            nc.gpsimd.memset(windows[w][:], 0.0)
+        for i in (0, 1, 3, 2):
+            score(i)
 
+        round_values(2, 0, 0, 512)
+        round_values(2, 512, 512, 1024)
+        add_mask_on_gpsimd(3, "vals2b")
         add_mask(0)
         add_mask(1)
         exponentials(0)
-        exponentials(1)
-        pick_values_on_scalar(0, None, "s1")
         add_mask(2)
-        add_mask(3)
-        exponentials(2)
+        for i in (1, 2, 3):
+            exponentials(i)
         invert(0)
         invert(1)
-        exponentials(3)
-        pick_values_on_vector(1)
-        weights(0)
-        weights(1)
+        pick_values_on_vector(0)
         invert(2)
         invert(3)
-        quantise_values(0, grouped_on="s2")
-        weights(2)
-        weights(3)
-        quantise_weights(0)
+        round_values(2, 1024, 1024, 1536)
+        turn_values(0, placed([P, P * PACK], BF16, "v_grouped0", 12))
+        weights_on_gpsimd(0)
+        weights(1, placed([P, J], BF16, "w1", 24))
+        round_values(2, 1536, 1536, 2048)
+        weights(2, tile([P, J], BF16, "w2", "neg_max3"))
+        weights(3, tile([P, J], BF16, "w3"))
+        quantise_values(0)
+        quantise_weights(0, tile([P, HALF], U32, "w_codes0"))
+        pick_values_on_vector(1)
+        quantise_weights(1, tile([P, HALF], U32, "w_codes1"))
+        half_product(0, 0, 0, placed([P, HALF], F32, "sums0_0", 28))
+        pick_values_on_scalar(2, placed([P, J], BF16, "v_rows2", 7))
+        turn_values(1, placed([P, P * PACK], BF16, "v_grouped1", 20))
         quantise_values(1)
-        pick_values_on_vector(2)
-        quantise_weights(1)
-
-        product(0, 0, HALF, 0, "w3")
-        quantise_values(2, "bank0")
-        product(0, HALF, I, 1, "v_rows2")
+        half_product(0, 1, 1, placed([P, HALF], F32, "sums0_1", 17))
         store(0)
-        product(1, 0, I, 1)
+        quantise_values(2)
+        whole_product(1, (2, 3), placed([P, I], F32, "sums1", 7))
         store(1)
-        product(2, 0, HALF, 2)
-        pick_values_on_scalar(3, "w2", None)
+        rounded[3] = placed([P, T], BF16, "rounded3", 20)
+        for c in range(PIECES):
+            round_values(3, c // 2 * 1024, c * 512, (c + 1) * 512)
+        half_product(2, 0, 0, tile([P, HALF], F32, "sums2_0", "vals3b"))
+        pick_values_on_scalar(3, tile([P, J], BF16, "v_rows3"))
         quantise_values(3)
-        product(2, HALF, I, 0, "v_rows3")
+        half_product(2, 1, 1, tile([P, HALF], F32, "sums2_1", "v_rows3"))
         store(2)
-        last_sums = tile([P, I], F32, "sums3")
-        for h, bank in enumerate((3, 1)):
-            multiply(3, h * HALF, (h + 1) * HALF, bank, last_sums[:, half(h)])
-        scatter(3, 0, I, last_sums[:])
+        whole_product(3, (2, 3), tile([P, I], F32, "sums3"))
         store(3)

@@ -57,10 +57,8 @@ def tile_attend_pickboth_kernel(tc, qpool_words, qpool_scales, keys_words, keys_
         nc.vector.memset(k_bytes[:].bitcast(I32), 0)
         nc.vector.memset(q_bytes[:].bitcast(I32), 0)
         make_identity(nc, ident[:])
-        windows = [tile([P, T], F32, "window%d" % w) for w in range(WINDOWS)]
+        windows = [tile([P, T], F32, "window0")]
         nc.vector.memset(windows[0][:].bitcast(I32), 0)
-        for w in range(1, WINDOWS):
-            nc.gpsimd.memset(windows[w][:], 0.0)
 
         def load_scale_rows(pool_bytes, rows):
             for quad in range(4):
@@ -117,6 +115,9 @@ def tile_attend_pickboth_kernel(tc, qpool_words, qpool_scales, keys_words, keys_
         q_scale = tile([P, I], U8, "q_scale")
         nc.vector.tensor_copy(k_codes[:], k_words[:].indirect(k_list[:]))
         nc.vector.tensor_copy(k_scale[:], k_bytes[:].indirect(k_list[:]))
+        for w, on in ((1, "k_bytes"), (2, "k_words")):
+            windows.append(tile([P, T], F32, "window%d" % w, on))
+            nc.gpsimd.memset(windows[w][:], 0.0)
 
         scores = [ps.tile([P, J], F32, name="scores%d" % i, tag="bank%d" % i) for i in range(TILES)]
 

@@ -86,7 +86,6 @@ def tile_attend_pickboth_kernel(tc, qpool_words, qpool_scales, keys_words, keys_
 
         nc.sync.dma_start(k_list[:], offs2)
         nc.sync.dma_start(q_list[:], offs)
-        nc.sync.dma_start(out=size_col[:], in_=size.rearrange("o (p c) -> p (o c)", c=PACK))
         load_scale_rows(k_bytes, keys_scales)
         nc.sync.dma_start(out=k_words[:].bitcast(I32), in_=keys_words[0].bitcast(I32))
         load_scale_rows(q_bytes, qpool_scales)
@@ -95,19 +94,14 @@ def tile_attend_pickboth_kernel(tc, qpool_words, qpool_scales, keys_words, keys_
         load_mask(2)
         load_piece(2, 512, 1024, tile([P, 512], F32, "vals2b"))
         load_mask(1)
+        nc.sync.dma_start(out=size_col[:], in_=size.rearrange("o (p c) -> p (o c)", c=PACK))
         load_mask(1)
         load_values(0)
         load_piece(2, 1024, 1536, placed([P, 512], F32, "vals2c", 11))
+        load_piece(2, 1536, 2048, tile([P, 512], F32, "vals2d"))
         load_values(1)
-        load_piece(2, 1536, 2048, placed([P, 512], F32, "vals2d", 27))
         load_piece(3, 0, 1024, tile([P, 1024], F32, "vals3a"))
         load_piece(3, 1024, 2048, tile([P, 1024], F32, "vals3b"))
-
-        size_ps = ps.tile([P, PACK, P], F32, name="size_ps")
-        for c in range(PACK):
-            nc.tensor.transpose(size_ps[:, c, :], size_col[:, c : c + 1].to_broadcast([P, P]), ident[:])
-        size_sb = tile([P, J], F32, "size_sb")
-        nc.scalar.activation(size_sb[:].rearrange("m (p c) -> m p c", c=PACK), size_ps[:].rearrange("m c p -> m p c"), ACT.Copy)
 
         k_codes = tile([P, J], U16, "k_codes")
         k_scale = tile([P, J], U8, "k_scale")
@@ -142,9 +136,10 @@ def tile_attend_pickboth_kernel(tc, qpool_words, qpool_scales, keys_words, keys_
         p_sb = [tile([P, J], F32, "p%d" % i) for i in range(TILES)]
         row_sum = [tile([P, 1], F32, "row_sum%d" % i) for i in range(TILES)]
         inv_sum = {}
-        w_grouped = [placed([P, HALF * PACK], BF16, "w_grouped0", 10), placed([P, HALF * PACK], BF16, "w_grouped1", 26)]
+        w_grouped = [placed([P, HALF * PACK], BF16, "w_grouped0", 10)]
         w_scale = [tile([P, HALF], U8, "w_scale%d" % h) for h in range(2)]
         w_codes = {}
+        w_made = {}
 
         def add_mask(i):
             nc.vector.tensor_tensor(s_sb[i][:], scores[i][:], mask_sb[i], ALU.add)
@@ -178,14 +173,18 @@ def tile_attend_pickboth_kernel(tc, qpool_words, qpool_scales, keys_words, keys_
                 ALU.mult,
                 ALU.mult,
             )
-            turn(w_rows[:], ps.tile([P, 2, P], F32, name="w_turn%d" % i, tag="bank%d" % i if i > 1 else "w_turn%d" % i), w_grouped[i // 2][:, i % 2 * P * PACK : (i % 2 + 1) * P * PACK])
+            w_made[i] = w_rows
+
+        def turn_weights(i):
+            bank = ps.tile([P, 2, P], F32, name="w_turn%d" % i, tag="bank%d" % i if i > 1 else "w_turn%d" % i)
+            turn(w_made[i][:], bank, w_grouped[i // 2][:, i % 2 * P * PACK : (i % 2 + 1) * P * PACK])
 
         def weights_on_gpsimd(i):
             sized = tile([P, J], F32, "sized%d" % i)
             nc.gpsimd.tensor_tensor(sized[:], p_sb[i][:], size_sb[:], ALU.mult)
             w_rows = tile([P, J], BF16, "w%d" % i)
             nc.gpsimd.tensor_scalar(w_rows[:], sized[:], inv_sum[i][:], 0.0, ALU.mult, ALU.add)
-            turn(w_rows[:], ps.tile([P, 2, P], F32, name="w_turn%d" % i, tag="bank%d" % i if i > 1 else "w_turn%d" % i), w_grouped[i // 2][:, i % 2 * P * PACK : (i % 2 + 1) * P * PACK])
+            w_made[i] = w_rows
 
         def quantise_weights(h, codes):
             w_codes[h] = codes
@@ -258,6 +257,12 @@ def tile_attend_pickboth_kernel(tc, qpool_words, qpool_scales, keys_words, keys_
         for i in (0, 1, 3, 2):
             score(i)
 
+        size_ps = ps.tile([P, PACK, P], F32, name="size_ps")
+        for c in range(PACK):
+            nc.tensor.transpose(size_ps[:, c, :], size_col[:, c : c + 1].to_broadcast([P, P]), ident[:])
+        size_sb = tile([P, J], F32, "size_sb")
+        nc.scalar.activation(size_sb[:].rearrange("m (p c) -> m p c", c=PACK), size_ps[:].rearrange("m c p -> m p c"), ACT.Copy)
+
         round_values(2, 0, 0, 512)
         round_values(2, 512, 512, 1024)
         add_mask_on_gpsimd(3, "vals2b")
@@ -271,23 +276,28 @@ def tile_attend_pickboth_kernel(tc, qpool_words, qpool_scales, keys_words, keys_
         invert(1)
         pick_values_on_vector(0)
         invert(2)
+        weights(1, placed([P, J], BF16, "w1", 24))
         invert(3)
         round_values(2, 1024, 1024, 1536)
-        turn_values(0, placed([P, P * PACK], BF16, "v_grouped0", 12))
-        weights_on_gpsimd(0)
-        weights(1, placed([P, J], BF16, "w1", 24))
         round_values(2, 1536, 1536, 2048)
+        weights_on_gpsimd(0)
+        turn_weights(0)
+        turn_values(0, placed([P, P * PACK], BF16, "v_grouped0", 12))
+        turn_weights(1)
         weights(2, tile([P, J], BF16, "w2", "neg_max3"))
         weights(3, tile([P, J], BF16, "w3"))
         quantise_values(0)
         quantise_weights(0, tile([P, HALF], U32, "w_codes0"))
+        w_grouped.append(placed([P, HALF * PACK], BF16, "w_grouped1", 9))
+        turn_weights(2)
+        turn_weights(3)
         pick_values_on_vector(1)
         quantise_weights(1, tile([P, HALF], U32, "w_codes1"))
-        half_product(0, 0, 0, placed([P, HALF], F32, "sums0_0", 28))
+        half_product(0, 0, 0, tile([P, HALF], F32, "sums0_0"))
         pick_values_on_scalar(2, placed([P, J], BF16, "v_rows2", 7))
-        turn_values(1, placed([P, P * PACK], BF16, "v_grouped1", 20))
+        turn_values(1, placed([P, P * PACK], BF16, "v_grouped1", 23))
         quantise_values(1)
-        half_product(0, 1, 1, placed([P, HALF], F32, "sums0_1", 17))
+        half_product(0, 1, 1, tile([P, HALF], F32, "sums0_1"))
         store(0)
         quantise_values(2)
         whole_product(1, (2, 3), placed([P, I], F32, "sums1", 7))

@@ -23,7 +23,8 @@ PACK = 4
 TILES = 4
 HALF = 256
 WINDOWS = 3
-PIECES = 4
+QUARTER = T // 4
+KIB = 1024
 
 
 def tile_attend_pickboth_kernel(tc, qpool_words, qpool_scales, keys_words, keys_scales, vals, mask, size, offs, offs2, out):
@@ -31,13 +32,13 @@ def tile_attend_pickboth_kernel(tc, qpool_words, qpool_scales, keys_words, keys_
     with ExitStack() as ctx:
         sb = ctx.enter_context(tc.tile_pool(name="sb", bufs=1))
         ps = ctx.enter_context(tc.psum_pool(name="ps", bufs=1))
-        shared = ctx.enter_context(tc.tile_pool(name="shared", bufs=1))
+        overlap = ctx.enter_context(tc.tile_pool(name="overlap", bufs=1))
 
         def tile(shape, dtype, name, on=None):
             return sb.tile(shape, dtype, name=name, tag=on or name, align_bytes=64)
 
-        def placed(shape, dtype, name, kib):
-            return shared.tile(shape, dtype, name=name, offset=int(1024 * kib), align_bytes=64)
+        def placed(shape, dtype, name, offset):
+            return overlap.tile(shape, dtype, name=name, offset=offset, align_bytes=64)
 
         def half(h):
             return slice(h * HALF, (h + 1) * HALF)
@@ -67,16 +68,12 @@ def tile_attend_pickboth_kernel(tc, qpool_words, qpool_scales, keys_words, keys_
                     in_=rows[0, 4 * quad : 4 * quad + 4, :].bitcast(I32),
                 )
 
-        vals_sb = {0: tile([P, T], F32, "vals0"), 1: placed([P, T], F32, "vals1", 0)}
-        pieces = {}
+        vals_sb = {}
         mask_sb = []
 
-        def load_values(e):
-            nc.sync.dma_start(out=vals_sb[e][:], in_=vals[e * P : (e + 1) * P, :])
-
-        def load_piece(e, first, last, piece):
-            pieces[e, first] = piece
-            nc.sync.dma_start(out=piece[:], in_=vals[e * P : (e + 1) * P, first:last])
+        def load_values(e, first, piece):
+            vals_sb[e, first] = piece
+            nc.sync.dma_start(out=piece[:], in_=vals[e * P : (e + 1) * P, first : first + piece.shape[1]])
 
         def load_mask(count):
             first = len(mask_sb)
@@ -90,18 +87,18 @@ def tile_attend_pickboth_kernel(tc, qpool_words, qpool_scales, keys_words, keys_
         nc.sync.dma_start(out=k_words[:].bitcast(I32), in_=keys_words[0].bitcast(I32))
         load_scale_rows(q_bytes, qpool_scales)
         nc.sync.dma_start(out=q_words[:].bitcast(I32), in_=qpool_words[0].rearrange("p n t -> p (n t)").bitcast(I32))
-        load_piece(2, 0, 512, tile([P, 512], F32, "vals2a"))
+        load_values(2, 0, tile([P, QUARTER], F32, "vals2a"))
         load_mask(2)
-        load_piece(2, 512, 1024, tile([P, 512], F32, "vals2b"))
+        load_values(2, QUARTER, tile([P, QUARTER], F32, "vals2b"))
         load_mask(1)
         nc.sync.dma_start(out=size_col[:], in_=size.rearrange("o (p c) -> p (o c)", c=PACK))
         load_mask(1)
-        load_values(0)
-        load_piece(2, 1024, 1536, placed([P, 512], F32, "vals2c", 11))
-        load_piece(2, 1536, 2048, tile([P, 512], F32, "vals2d"))
-        load_values(1)
-        load_piece(3, 0, 1024, tile([P, 1024], F32, "vals3a"))
-        load_piece(3, 1024, 2048, tile([P, 1024], F32, "vals3b"))
+        load_values(0, 0, tile([P, T], F32, "vals0"))
+        load_values(2, 2 * QUARTER, placed([P, QUARTER], F32, "vals2c", 2 * KIB))
+        load_values(2, 3 * QUARTER, tile([P, QUARTER], F32, "vals2d"))
+        load_values(1, 0, tile([P, T], F32, "vals1"))
+        load_values(3, 0, tile([P, T // 2], F32, "vals3a"))
+        load_values(3, T // 2, tile([P, T // 2], F32, "vals3b"))
 
         k_codes = tile([P, J], U16, "k_codes")
         k_scale = tile([P, J], U8, "k_scale")
@@ -132,27 +129,51 @@ def tile_attend_pickboth_kernel(tc, qpool_words, qpool_scales, keys_words, keys_
                 stop=True,
             )
 
-        s_sb = [tile([P, J], F32, "s%d" % i) for i in range(TILES - 1)] + [placed([P, J], F32, "s3", 24)]
+        s_sb = [tile([P, J], F32, "s%d" % i) for i in range(TILES)]
         p_sb = [tile([P, J], F32, "p%d" % i) for i in range(TILES)]
-        row_sum = [tile([P, 1], F32, "row_sum%d" % i) for i in range(TILES)]
-        inv_sum = {}
-        w_grouped = [placed([P, HALF * PACK], BF16, "w_grouped0", 10)]
+        row_sums = [tile([P, 2], F32, "row_sums%d" % h) for h in range(2)]
+        inv_sums = [tile([P, 2], F32, "inv_sums%d" % h) for h in range(2)]
+        w_rows = {}
+        w_codes = [tile([P, HALF], U32, "w_codes%d" % h) for h in range(2)]
         w_scale = [tile([P, HALF], U8, "w_scale%d" % h) for h in range(2)]
-        w_codes = {}
-        w_made = {}
+        staged = placed([P, J + HALF * PACK], BF16, "staged", 0)
+        w_grouped = [staged[:, HALF : HALF + HALF * PACK], staged[:, J:]]
+
+        def column(pairs, i):
+            return pairs[i // 2][:, i % 2 : i % 2 + 1]
 
         def add_mask(i):
             nc.vector.tensor_tensor(s_sb[i][:], scores[i][:], mask_sb[i], ALU.add)
 
-        def add_mask_on_gpsimd(i, on=None):
+        def add_mask_on_gpsimd(i, on):
             raw = tile([P, J], F32, "raw%d" % i, on)
             nc.scalar.copy(raw[:], scores[i][:])
             nc.gpsimd.tensor_tensor(s_sb[i][:], raw[:], mask_sb[i], ALU.add)
 
-        def exponentials(i, max_on=None):
-            neg_max = tile([P, 1], F32, "neg_max%d" % i, max_on)
+        def exponentials(i):
+            neg_max = tile([P, 1], F32, "neg_max%d" % i)
             nc.vector.tensor_reduce(neg_max[:], s_sb[i][:], AX.X, ALU.max, negate=True)
-            nc.scalar.activation(p_sb[i][:], s_sb[i][:], ACT.Exp, bias=neg_max[:], accum_out=row_sum[i][:])
+            nc.scalar.activation(p_sb[i][:], s_sb[i][:], ACT.Exp, bias=neg_max[:], accum_out=column(row_sums, i))
+
+        def invert(h):
+            nc.vector.reciprocal(inv_sums[h][:], row_sums[h][:])
+
+        def weights(i, on=None):
+            w_rows[i] = tile([P, J], BF16, "w%d" % i, on)
+            nc.vector.scalar_tensor_tensor(
+                w_rows[i][:].rearrange("m (p c) -> m p c", c=PACK),
+                p_sb[i][:].rearrange("m (p c) -> m p c", c=PACK),
+                column(inv_sums, i),
+                size_ps[:].rearrange("m c p -> m p c"),
+                ALU.mult,
+                ALU.mult,
+            )
+
+        def weights_on_gpsimd(i):
+            sized = tile([P, J], F32, "sized%d" % i)
+            nc.gpsimd.tensor_tensor(sized[:], p_sb[i][:], size_sb[:], ALU.mult)
+            w_rows[i] = tile([P, J], BF16, "w%d" % i)
+            nc.gpsimd.tensor_scalar(w_rows[i][:], sized[:], column(inv_sums, i), 0.0, ALU.mult, ALU.add)
 
         def turn(rows, bank, grouped):
             words = rows.bitcast(F32)
@@ -160,51 +181,25 @@ def tile_attend_pickboth_kernel(tc, qpool_words, qpool_scales, keys_words, keys_
                 nc.tensor.transpose(bank[:, u, :], words[:, u : J // 2 : 2], ident[:])
             nc.scalar.copy(grouped.bitcast(F32).rearrange("p (r u) -> p r u", u=2), bank[:].rearrange("p u r -> p r u"))
 
-        def invert(i):
-            inv_sum[i] = placed([P, 1], F32, "inv_sum2", 25) if i == 2 else tile([P, 1], F32, "inv_sum%d" % i)
-            nc.vector.reciprocal(inv_sum[i][:], row_sum[i][:])
+        def turn_weights(i, tag):
+            bank = ps.tile([P, 2, P], F32, name="w_turn%d" % i, tag=tag)
+            turn(w_rows[i][:], bank, w_grouped[i // 2][:, i % 2 * P * PACK : (i % 2 + 1) * P * PACK])
 
-        def weights(i, w_rows):
-            nc.vector.scalar_tensor_tensor(
-                w_rows[:].rearrange("m (p c) -> m p c", c=PACK),
-                p_sb[i][:].rearrange("m (p c) -> m p c", c=PACK),
-                inv_sum[i][:],
-                size_ps[:].rearrange("m c p -> m p c"),
-                ALU.mult,
-                ALU.mult,
-            )
-            w_made[i] = w_rows
+        def quantise_weights(h):
+            nc.vector.quantize_mx(out=w_codes[h][:].bitcast(FP8X4), scales=w_scale[h][:], in_=w_grouped[h])
 
-        def turn_weights(i):
-            bank = ps.tile([P, 2, P], F32, name="w_turn%d" % i, tag="bank%d" % i if i > 1 else "w_turn%d" % i)
-            turn(w_made[i][:], bank, w_grouped[i // 2][:, i % 2 * P * PACK : (i % 2 + 1) * P * PACK])
-
-        def weights_on_gpsimd(i):
-            sized = tile([P, J], F32, "sized%d" % i)
-            nc.gpsimd.tensor_tensor(sized[:], p_sb[i][:], size_sb[:], ALU.mult)
-            w_rows = tile([P, J], BF16, "w%d" % i)
-            nc.gpsimd.tensor_scalar(w_rows[:], sized[:], inv_sum[i][:], 0.0, ALU.mult, ALU.add)
-            w_made[i] = w_rows
-
-        def quantise_weights(h, codes):
-            w_codes[h] = codes
-            nc.vector.quantize_mx(
-                out=codes[:].bitcast(FP8X4),
-                scales=w_scale[h][:],
-                in_=w_grouped[h][:],
-            )
-
-        v_codes = {}
-        v_scale = [tile([P, P], U8, "v_scale%d" % e) for e in range(TILES)]
         v_rows = {}
         v_grouped = {}
+        v_codes = [tile([P, P], U32, "v_codes%d" % e) for e in range(TILES)]
+        v_scale = [tile([P, P], U8, "v_scale%d" % e) for e in range(TILES)]
+        rounded = {2: tile([P, T], BF16, "rounded2")}
 
         def pick_values_on_vector(e):
-            v_rows[e] = tile([P, J], BF16, "v_rows%d" % e)
-            nc.vector.tensor_copy(v_rows[e][:], vals_sb[e][:].indirect(k_list[:]))
+            v_rows[e] = tile([P, J], BF16, "v_rows%d" % e)[:]
+            nc.vector.tensor_copy(v_rows[e], vals_sb[e, 0][:].indirect(k_list[:]))
 
         def round_values(e, piece, first, last):
-            nc.scalar.activation(rounded[e][:, first:last], pieces[e, piece][:, first - piece : last - piece], ACT.Copy)
+            nc.scalar.activation(rounded[e][:, first:last], vals_sb[e, piece][:, first - piece : last - piece], ACT.Copy)
 
         def pick_values_on_scalar(e, rows):
             v_rows[e] = rows
@@ -214,14 +209,14 @@ def tile_attend_pickboth_kernel(tc, qpool_words, qpool_scales, keys_words, keys_
 
         def turn_values(e, grouped):
             v_grouped[e] = grouped
-            v_turn = ps.tile([P, 2, P], F32, name="v_turn%d" % e, tag="v_turn")
-            turn(v_rows[e][:], v_turn, grouped[:])
+            turn(v_rows[e], ps.tile([P, 2, P], F32, name="v_turn%d" % e, tag="v_turn"), grouped[:])
 
         def quantise_values(e):
-            if e not in v_grouped:
-                turn_values(e, tile([P, P * PACK], BF16, "v_grouped%d" % e))
-            v_codes[e] = tile([P, P], U32, "v_codes%d" % e)
             nc.vector.quantize_mx(out=v_codes[e][:].bitcast(FP8X4), scales=v_scale[e][:], in_=v_grouped[e][:])
+
+        def turn_and_quantise_values(e):
+            turn_values(e, tile([P, P * PACK], BF16, "v_grouped%d" % e))
+            quantise_values(e)
 
         def multiply(e, h, bank, sums):
             o_ps = ps.tile([P, HALF], F32, name="o_ps%d_%d" % (e, h), tag="bank%d" % bank)
@@ -239,19 +234,19 @@ def tile_attend_pickboth_kernel(tc, qpool_words, qpool_scales, keys_words, keys_
         def scatter(e, first, last, sums):
             nc.vector.tensor_copy(windows[e % WINDOWS][:].indirect(entries(q_list, first, last)), sums)
 
-        def half_product(e, h, bank, sums):
-            multiply(e, h, bank, sums[:])
+        def half_product(e, h, sums_on=None):
+            sums = tile([P, HALF], F32, "sums%d_%d" % (e, h), sums_on)
+            multiply(e, h, h, sums[:])
             scatter(e, h * HALF, (h + 1) * HALF, sums[:])
 
-        def whole_product(e, banks, sums):
+        def whole_product(e, sums):
             for h in range(2):
-                multiply(e, h, banks[h], sums[:, half(h)])
+                multiply(e, h, 2 + h, sums[:, half(h)])
             scatter(e, 0, I, sums[:])
 
         def store(e):
             nc.sync.dma_start(out=out[e * P : (e + 1) * P, :], in_=windows[e % WINDOWS][:])
 
-        rounded = {2: placed([P, T], BF16, "rounded2", 17)}
         for h in range(2):
             pick_queries(h)
         for i in (0, 1, 3, 2):
@@ -263,8 +258,8 @@ def tile_attend_pickboth_kernel(tc, qpool_words, qpool_scales, keys_words, keys_
         size_sb = tile([P, J], F32, "size_sb")
         nc.scalar.activation(size_sb[:].rearrange("m (p c) -> m p c", c=PACK), size_ps[:].rearrange("m c p -> m p c"), ACT.Copy)
 
-        round_values(2, 0, 0, 512)
-        round_values(2, 512, 512, 1024)
+        round_values(2, 0, 0, QUARTER)
+        round_values(2, QUARTER, QUARTER, 2 * QUARTER)
         add_mask_on_gpsimd(3, "vals2b")
         add_mask(0)
         add_mask(1)
@@ -273,42 +268,40 @@ def tile_attend_pickboth_kernel(tc, qpool_words, qpool_scales, keys_words, keys_
         for i in (1, 2, 3):
             exponentials(i)
         invert(0)
-        invert(1)
         pick_values_on_vector(0)
-        invert(2)
-        weights(1, placed([P, J], BF16, "w1", 24))
-        invert(3)
-        round_values(2, 1024, 1024, 1536)
-        round_values(2, 1536, 1536, 2048)
+        invert(1)
+        weights(1, "s3")
+        round_values(2, 2 * QUARTER, 2 * QUARTER, 3 * QUARTER)
+        round_values(2, 3 * QUARTER, 3 * QUARTER, T)
         weights_on_gpsimd(0)
-        turn_weights(0)
-        turn_values(0, placed([P, P * PACK], BF16, "v_grouped0", 12))
-        turn_weights(1)
-        weights(2, tile([P, J], BF16, "w2", "neg_max3"))
-        weights(3, tile([P, J], BF16, "w3"))
+        turn_weights(0, "w_turn0")
+        turn_values(0, placed([P, P * PACK], BF16, "v_grouped0", 3 * KIB))
+        turn_weights(1, "w_turn1")
+        weights(2)
+        weights(3)
         quantise_values(0)
-        quantise_weights(0, tile([P, HALF], U32, "w_codes0"))
-        w_grouped.append(placed([P, HALF * PACK], BF16, "w_grouped1", 9))
-        turn_weights(2)
-        turn_weights(3)
+        quantise_weights(0)
+        turn_weights(2, "bank2")
+        turn_weights(3, "bank3")
         pick_values_on_vector(1)
-        quantise_weights(1, tile([P, HALF], U32, "w_codes1"))
-        half_product(0, 0, 0, tile([P, HALF], F32, "sums0_0"))
-        pick_values_on_scalar(2, placed([P, J], BF16, "v_rows2", 7))
-        turn_values(1, placed([P, P * PACK], BF16, "v_grouped1", 23))
-        quantise_values(1)
-        half_product(0, 1, 1, tile([P, HALF], F32, "sums0_1"))
+        quantise_weights(1)
+
+        half_product(0, 0)
+        pick_values_on_scalar(2, staged[:, :J])
+        turn_and_quantise_values(1)
+        half_product(0, 1)
         store(0)
-        quantise_values(2)
-        whole_product(1, (2, 3), placed([P, I], F32, "sums1", 7))
+        turn_and_quantise_values(2)
+        whole_product(1, placed([P, I], F32, "sums1", 0))
         store(1)
-        rounded[3] = placed([P, T], BF16, "rounded3", 20)
-        for c in range(PIECES):
-            round_values(3, c // 2 * 1024, c * 512, (c + 1) * 512)
-        half_product(2, 0, 0, tile([P, HALF], F32, "sums2_0", "vals3b"))
-        pick_values_on_scalar(3, tile([P, J], BF16, "v_rows3"))
-        quantise_values(3)
-        half_product(2, 1, 1, tile([P, HALF], F32, "sums2_1", "v_rows3"))
+        rounded[3] = tile([P, T], BF16, "rounded3", "v_codes0")
+        round_values(3, 0, 0, T // 2)
+        round_values(3, T // 2, 2 * QUARTER, 3 * QUARTER)
+        round_values(3, T // 2, 3 * QUARTER, T)
+        half_product(2, 0, "vals3b")
+        pick_values_on_scalar(3, tile([P, J], BF16, "v_rows3")[:])
+        turn_and_quantise_values(3)
+        half_product(2, 1, "v_rows3")
         store(2)
-        whole_product(3, (2, 3), tile([P, I], F32, "sums3"))
+        whole_product(3, tile([P, I], F32, "sums3"))
         store(3)

@@ -22,8 +22,6 @@ P = 128
 PACK = 4
 TILES = 4
 HALF = 256
-WINDOWS = 3
-QUARTER = T // 4
 KIB = 1024
 
 
@@ -71,9 +69,9 @@ def tile_attend_pickboth_kernel(tc, qpool_words, qpool_scales, keys_words, keys_
         vals_sb = {}
         mask_sb = []
 
-        def load_values(e, first, piece):
-            vals_sb[e, first] = piece
-            nc.sync.dma_start(out=piece[:], in_=vals[e * P : (e + 1) * P, first : first + piece.shape[1]])
+        def load_values(e):
+            vals_sb[e] = placed([P, T], F32, "vals2", 0) if e == 2 else tile([P, T], F32, "vals%d" % e)
+            nc.sync.dma_start(out=vals_sb[e][:], in_=vals[e * P : (e + 1) * P, :])
 
         def load_mask(count):
             first = len(mask_sb)
@@ -87,18 +85,11 @@ def tile_attend_pickboth_kernel(tc, qpool_words, qpool_scales, keys_words, keys_
         nc.sync.dma_start(out=k_words[:].bitcast(I32), in_=keys_words[0].bitcast(I32))
         load_scale_rows(q_bytes, qpool_scales)
         nc.sync.dma_start(out=q_words[:].bitcast(I32), in_=qpool_words[0].rearrange("p n t -> p (n t)").bitcast(I32))
-        load_values(2, 0, tile([P, QUARTER], F32, "vals2a"))
         load_mask(2)
-        load_values(2, QUARTER, tile([P, QUARTER], F32, "vals2b"))
-        load_mask(1)
         nc.sync.dma_start(out=size_col[:], in_=size.rearrange("o (p c) -> p (o c)", c=PACK))
-        load_mask(1)
-        load_values(0, 0, tile([P, T], F32, "vals0"))
-        load_values(2, 2 * QUARTER, placed([P, QUARTER], F32, "vals2c", 2 * KIB))
-        load_values(2, 3 * QUARTER, tile([P, QUARTER], F32, "vals2d"))
-        load_values(1, 0, tile([P, T], F32, "vals1"))
-        load_values(3, 0, tile([P, T // 2], F32, "vals3a"))
-        load_values(3, T // 2, tile([P, T // 2], F32, "vals3b"))
+        load_mask(2)
+        for e in (0, 1, 3, 2):
+            load_values(e)
 
         k_codes = tile([P, J], U16, "k_codes")
         k_scale = tile([P, J], U8, "k_scale")
@@ -106,9 +97,13 @@ def tile_attend_pickboth_kernel(tc, qpool_words, qpool_scales, keys_words, keys_
         q_scale = tile([P, I], U8, "q_scale")
         nc.vector.tensor_copy(k_codes[:], k_words[:].indirect(k_list[:]))
         nc.vector.tensor_copy(k_scale[:], k_bytes[:].indirect(k_list[:]))
-        for w, on in ((1, "k_bytes"), (2, "k_words")):
+
+        def zero_window(w, on):
             windows.append(tile([P, T], F32, "window%d" % w, on))
             nc.gpsimd.memset(windows[w][:], 0.0)
+
+        zero_window(1, "k_bytes")
+        zero_window(2, "k_words")
 
         scores = [ps.tile([P, J], F32, name="scores%d" % i, tag="bank%d" % i) for i in range(TILES)]
 
@@ -134,19 +129,15 @@ def tile_attend_pickboth_kernel(tc, qpool_words, qpool_scales, keys_words, keys_
         row_sums = [tile([P, 2], F32, "row_sums%d" % h) for h in range(2)]
         inv_sums = [tile([P, 2], F32, "inv_sums%d" % h) for h in range(2)]
         w_rows = {}
-        w_codes = [tile([P, HALF], U32, "w_codes%d" % h) for h in range(2)]
-        w_scale = [tile([P, HALF], U8, "w_scale%d" % h) for h in range(2)]
-        staged = placed([P, J + HALF * PACK], BF16, "staged", 0)
-        w_grouped = [staged[:, HALF : HALF + HALF * PACK], staged[:, J:]]
-
-        def column(pairs, i):
-            return pairs[i // 2][:, i % 2 : i % 2 + 1]
+        w_grouped = [tile([P, HALF * PACK], BF16, "w_grouped%d" % h) for h in range(2)]
+        w_codes = tile([P, I], U32, "w_codes")
+        w_scale = tile([P, I], U8, "w_scale")
 
         def add_mask(i):
             nc.vector.tensor_tensor(s_sb[i][:], scores[i][:], mask_sb[i], ALU.add)
 
-        def add_mask_on_gpsimd(i, on):
-            raw = tile([P, J], F32, "raw%d" % i, on)
+        def add_mask_on_gpsimd(i):
+            raw = tile([P, J], F32, "raw%d" % i)
             nc.scalar.copy(raw[:], scores[i][:])
             nc.gpsimd.tensor_tensor(s_sb[i][:], raw[:], mask_sb[i], ALU.add)
 
@@ -154,6 +145,9 @@ def tile_attend_pickboth_kernel(tc, qpool_words, qpool_scales, keys_words, keys_
             neg_max = tile([P, 1], F32, "neg_max%d" % i)
             nc.vector.tensor_reduce(neg_max[:], s_sb[i][:], AX.X, ALU.max, negate=True)
             nc.scalar.activation(p_sb[i][:], s_sb[i][:], ACT.Exp, bias=neg_max[:], accum_out=column(row_sums, i))
+
+        def column(pairs, i):
+            return pairs[i // 2][:, i % 2 : i % 2 + 1]
 
         def invert(h):
             nc.vector.reciprocal(inv_sums[h][:], row_sums[h][:])
@@ -175,80 +169,72 @@ def tile_attend_pickboth_kernel(tc, qpool_words, qpool_scales, keys_words, keys_
             w_rows[i] = tile([P, J], BF16, "w%d" % i)
             nc.gpsimd.tensor_scalar(w_rows[i][:], sized[:], column(inv_sums, i), 0.0, ALU.mult, ALU.add)
 
-        def turn(rows, bank, grouped):
+        def copy_out(engine, to, bank):
+            if engine == "vector":
+                nc.vector.tensor_copy(to, bank)
+            else:
+                nc.scalar.copy(to, bank)
+
+        def turn(rows, bank, grouped, engine="scalar"):
             words = rows.bitcast(F32)
             for u in range(2):
                 nc.tensor.transpose(bank[:, u, :], words[:, u : J // 2 : 2], ident[:])
-            nc.scalar.copy(grouped.bitcast(F32).rearrange("p (r u) -> p r u", u=2), bank[:].rearrange("p u r -> p r u"))
+            copy_out(engine, grouped.bitcast(F32).rearrange("p (r u) -> p r u", u=2), bank[:].rearrange("p u r -> p r u"))
 
-        def turn_weights(i, tag):
-            bank = ps.tile([P, 2, P], F32, name="w_turn%d" % i, tag=tag)
+        def turn_weights(i):
+            bank = ps.tile([P, 2, P], F32, name="w_turn%d" % i, tag="bank%d" % i)
             turn(w_rows[i][:], bank, w_grouped[i // 2][:, i % 2 * P * PACK : (i % 2 + 1) * P * PACK])
 
         def quantise_weights(h):
-            nc.vector.quantize_mx(out=w_codes[h][:].bitcast(FP8X4), scales=w_scale[h][:], in_=w_grouped[h])
+            nc.vector.quantize_mx(out=w_codes[:, half(h)].bitcast(FP8X4), scales=w_scale[:, half(h)], in_=w_grouped[h][:])
 
         v_rows = {}
         v_grouped = {}
-        v_codes = [tile([P, P], U32, "v_codes%d" % e) for e in range(TILES)]
+        v_codes = {}
         v_scale = [tile([P, P], U8, "v_scale%d" % e) for e in range(TILES)]
-        rounded = {2: tile([P, T], BF16, "rounded2")}
 
-        def pick_values_on_vector(e):
-            v_rows[e] = tile([P, J], BF16, "v_rows%d" % e)[:]
-            nc.vector.tensor_copy(v_rows[e], vals_sb[e, 0][:].indirect(k_list[:]))
-
-        def round_values(e, piece, first, last):
-            nc.scalar.activation(rounded[e][:, first:last], vals_sb[e, piece][:, first - piece : last - piece], ACT.Copy)
-
-        def pick_values_on_scalar(e, rows):
+        def pick_values(e, engine, rows, first=0, last=J):
             v_rows[e] = rows
-            for h in range(2):
-                listed = entries(k_list, h * HALF, (h + 1) * HALF)
-                nc.scalar.activation(rows[:, half(h)], rounded[e][:].indirect(listed), ACT.Copy)
+            picked = vals_sb[e][:].indirect(entries(k_list, first, last))
+            if engine == "vector":
+                nc.vector.tensor_copy(rows[:, first:last], picked)
+            else:
+                nc.scalar.activation(rows[:, first:last], picked, ACT.Copy)
 
-        def turn_values(e, grouped):
+        def turn_values(e, grouped, engine="scalar"):
             v_grouped[e] = grouped
-            turn(v_rows[e], ps.tile([P, 2, P], F32, name="v_turn%d" % e, tag="v_turn"), grouped[:])
+            turn(v_rows[e], ps.tile([P, 2, P], F32, name="v_turn%d" % e, tag="v_turn"), grouped, engine)
 
-        def quantise_values(e):
-            nc.vector.quantize_mx(out=v_codes[e][:].bitcast(FP8X4), scales=v_scale[e][:], in_=v_grouped[e][:])
+        def quantise_values(e, at=None):
+            v_codes[e] = tile([P, P], U32, "v_codes%d" % e) if at is None else placed([P, P], U32, "v_codes%d" % e, at)
+            nc.vector.quantize_mx(out=v_codes[e][:].bitcast(FP8X4), scales=v_scale[e][:], in_=v_grouped[e])
 
-        def turn_and_quantise_values(e):
-            turn_values(e, tile([P, P * PACK], BF16, "v_grouped%d" % e))
-            quantise_values(e)
-
-        def multiply(e, h, bank, sums):
-            o_ps = ps.tile([P, HALF], F32, name="o_ps%d_%d" % (e, h), tag="bank%d" % bank)
+        def multiply(e, first, last, bank, engine, sums):
+            o_ps = ps.tile([P, last - first], F32, name="o_ps%d_%d" % (e, first), tag=bank)
             nc.tensor.matmul_mx(
                 out=o_ps[:],
                 lhsT=v_codes[e][:].bitcast(FP8X4),
                 lhsT_scale=v_scale[e][:],
-                rhs=w_codes[h][:].bitcast(FP8X4),
-                rhs_scale=w_scale[h][:],
+                rhs=w_codes[:, first:last].bitcast(FP8X4),
+                rhs_scale=w_scale[:, first:last],
                 start=True,
                 stop=True,
             )
-            nc.scalar.copy(sums, o_ps[:])
+            copy_out(engine, sums, o_ps[:])
 
-        def scatter(e, first, last, sums):
-            nc.vector.tensor_copy(windows[e % WINDOWS][:].indirect(entries(q_list, first, last)), sums)
-
-        def half_product(e, h, sums_on=None):
-            sums = tile([P, HALF], F32, "sums%d_%d" % (e, h), sums_on)
-            multiply(e, h, h, sums[:])
-            scatter(e, h * HALF, (h + 1) * HALF, sums[:])
-
-        def whole_product(e, sums):
-            for h in range(2):
-                multiply(e, h, 2 + h, sums[:, half(h)])
-            scatter(e, 0, I, sums[:])
+        def scatter(e, first, last, engine, sums):
+            places = windows[e][:].indirect(entries(q_list, first, last))
+            if engine == "vector":
+                nc.vector.tensor_copy(places, sums)
+            else:
+                nc.scalar.activation(places, sums, ACT.Copy)
 
         def store(e):
-            nc.sync.dma_start(out=out[e * P : (e + 1) * P, :], in_=windows[e % WINDOWS][:])
+            nc.sync.dma_start(out=out[e * P : (e + 1) * P, :], in_=windows[e][:])
 
         for h in range(2):
             pick_queries(h)
+        zero_window(3, "q_bytes")
         for i in (0, 1, 3, 2):
             score(i)
 
@@ -258,9 +244,13 @@ def tile_attend_pickboth_kernel(tc, qpool_words, qpool_scales, keys_words, keys_
         size_sb = tile([P, J], F32, "size_sb")
         nc.scalar.activation(size_sb[:].rearrange("m (p c) -> m p c", c=PACK), size_ps[:].rearrange("m c p -> m p c"), ACT.Copy)
 
-        round_values(2, 0, 0, QUARTER)
-        round_values(2, QUARTER, QUARTER, 2 * QUARTER)
-        add_mask_on_gpsimd(3, "vals2b")
+        def rows_tile(e, on=None):
+            return tile([P, J], BF16, "v_rows%d" % e, on)[:]
+
+        def grouped_tile(e, on=None):
+            return tile([P, P * PACK], BF16, "v_grouped%d" % e, on)[:]
+
+        add_mask_on_gpsimd(3)
         add_mask(0)
         add_mask(1)
         exponentials(0)
@@ -268,40 +258,49 @@ def tile_attend_pickboth_kernel(tc, qpool_words, qpool_scales, keys_words, keys_
         for i in (1, 2, 3):
             exponentials(i)
         invert(0)
-        pick_values_on_vector(0)
+        pick_values(0, "vector", rows_tile(0))
         invert(1)
         weights(1, "s3")
-        round_values(2, 2 * QUARTER, 2 * QUARTER, 3 * QUARTER)
-        round_values(2, 3 * QUARTER, 3 * QUARTER, T)
         weights_on_gpsimd(0)
-        turn_weights(0, "w_turn0")
-        turn_values(0, placed([P, P * PACK], BF16, "v_grouped0", 3 * KIB))
-        turn_weights(1, "w_turn1")
+        staged = tile([P, HALF + P * PACK], BF16, "staged", "neg_max3")
+        pick_values(1, "scalar", staged[:, :J], 0, HALF)
+        turn_weights(0)
+        turn_values(0, staged[:, HALF:])
+        turn_weights(1)
         weights(2)
         weights(3)
         quantise_values(0)
         quantise_weights(0)
-        turn_weights(2, "bank2")
-        turn_weights(3, "bank3")
-        pick_values_on_vector(1)
+        turn_weights(2)
+        turn_weights(3)
+        pick_values(1, "vector", staged[:, :J], HALF, J)
+        sums0a = placed([P, HALF], F32, "sums0a", 8 * KIB)
+        multiply(0, 0, HALF, "o_bank0", "scalar", sums0a[:])
+        scatter(0, 0, HALF, "scalar", sums0a[:])
         quantise_weights(1)
-
-        half_product(0, 0)
-        pick_values_on_scalar(2, staged[:, :J])
-        turn_and_quantise_values(1)
-        half_product(0, 1)
+        turn_values(1, grouped_tile(1), "vector")
+        pick_values(2, "vector", rows_tile(2, "w_grouped1"))
+        quantise_values(1, 0)
+        pick_values(3, "vector", placed([P, J], BF16, "v_rows3", KIB)[:])
+        sums0b = placed([P, HALF], F32, "sums0b", 8 * KIB - KIB // 2)
+        multiply(0, HALF, I, "o_bank1", "scalar", sums0b[:])
+        turn_values(2, grouped_tile(2))
+        quantise_values(2)
+        scatter(0, HALF, I, "vector", sums0b[:])
         store(0)
-        turn_and_quantise_values(2)
-        whole_product(1, placed([P, I], F32, "sums1", 0))
+        sums1 = tile([P, I], F32, "sums1")
+        multiply(1, 0, I, "o_bank0", "scalar", sums1[:])
+        turn_values(3, grouped_tile(3))
+        scatter(1, 0, HALF, "scalar", sums1[:, half(0)])
+        quantise_values(3)
+        scatter(1, HALF, I, "vector", sums1[:, half(1)])
         store(1)
-        rounded[3] = tile([P, T], BF16, "rounded3", "v_codes0")
-        round_values(3, 0, 0, T // 2)
-        round_values(3, T // 2, 2 * QUARTER, 3 * QUARTER)
-        round_values(3, T // 2, 3 * QUARTER, T)
-        half_product(2, 0, "vals3b")
-        pick_values_on_scalar(3, tile([P, J], BF16, "v_rows3")[:])
-        turn_and_quantise_values(3)
-        half_product(2, 1, "v_rows3")
+        sums2 = tile([P, I], F32, "sums2")
+        multiply(2, 0, I, "o_bank1", "scalar", sums2[:])
+        for h in range(2):
+            scatter(2, h * HALF, (h + 1) * HALF, "scalar", sums2[:, half(h)])
         store(2)
-        whole_product(3, tile([P, I], F32, "sums3"))
+        sums3 = tile([P, I], F32, "sums3")
+        multiply(3, 0, I, "o_bank0", "vector", sums3[:])
+        scatter(3, 0, I, "vector", sums3[:])
         store(3)

@@ -109,7 +109,6 @@ def tile_attend_pickboth_kernel(tc, qpool_words, qpool_scales, keys_words, keys_
 
         def pick_queries(h):
             listed = entries(q_list, h * HALF, (h + 1) * HALF)
-            nc.vector.tensor_copy(q_scale[:, half(h)], q_bytes[:].indirect(listed))
             nc.vector.tensor_copy(q_codes[:, half(h)], q_words[:].indirect(listed))
 
         def score(i):
@@ -129,7 +128,7 @@ def tile_attend_pickboth_kernel(tc, qpool_words, qpool_scales, keys_words, keys_
         row_sums = [tile([P, 2], F32, "row_sums%d" % h) for h in range(2)]
         inv_sums = [tile([P, 2], F32, "inv_sums%d" % h) for h in range(2)]
         w_rows = {}
-        w_grouped = [tile([P, HALF * PACK], BF16, "w_grouped%d" % h) for h in range(2)]
+        w_grouped = [tile([P, HALF * PACK], BF16, "w_grouped0"), placed([P, HALF * PACK], BF16, "w_grouped1", 8 * KIB)]
         w_codes = tile([P, I], U32, "w_codes")
         w_scale = tile([P, I], U8, "w_scale")
 
@@ -232,6 +231,7 @@ def tile_attend_pickboth_kernel(tc, qpool_words, qpool_scales, keys_words, keys_
         def store(e):
             nc.sync.dma_start(out=out[e * P : (e + 1) * P, :], in_=windows[e][:])
 
+        nc.vector.tensor_copy(q_scale[:], q_bytes[:].indirect(q_list[:]))
         for h in range(2):
             pick_queries(h)
         zero_window(3, "q_bytes")
@@ -274,33 +274,37 @@ def tile_attend_pickboth_kernel(tc, qpool_words, qpool_scales, keys_words, keys_
         turn_weights(2)
         turn_weights(3)
         pick_values(1, "vector", staged[:, :J], HALF, J)
-        sums0a = placed([P, HALF], F32, "sums0a", 8 * KIB)
+        sums0a = tile([P, HALF], F32, "sums0a")
         multiply(0, 0, HALF, "o_bank0", "scalar", sums0a[:])
         scatter(0, 0, HALF, "scalar", sums0a[:])
         quantise_weights(1)
         turn_values(1, grouped_tile(1), "vector")
-        pick_values(2, "vector", rows_tile(2, "w_grouped1"))
+        pick_values(2, "vector", placed([P, J], BF16, "v_rows2", 9 * KIB)[:])
         quantise_values(1, 0)
         pick_values(3, "vector", placed([P, J], BF16, "v_rows3", KIB)[:])
-        sums0b = placed([P, HALF], F32, "sums0b", 8 * KIB - KIB // 2)
-        multiply(0, HALF, I, "o_bank1", "scalar", sums0b[:])
         turn_values(2, grouped_tile(2))
+        sums0b = placed([P, HALF], F32, "sums0b", 9 * KIB)
+        multiply(0, HALF, I, "o_bank1", "scalar", sums0b[:])
         quantise_values(2)
         scatter(0, HALF, I, "vector", sums0b[:])
         store(0)
-        sums1 = tile([P, I], F32, "sums1")
-        multiply(1, 0, I, "o_bank0", "scalar", sums1[:])
-        turn_values(3, grouped_tile(3))
-        scatter(1, 0, HALF, "scalar", sums1[:, half(0)])
+        sums1a = placed([P, I], F32, "sums1a", 2 * KIB)[:, :HALF]
+        multiply(1, 0, HALF, "o_bank0", "scalar", sums1a)
+        scatter(1, 0, HALF, "scalar", sums1a)
+        turn_values(3, placed([P, P * PACK], BF16, "v_grouped3", 2 * KIB + KIB // 2)[:])
+        sums1b = placed([P, HALF], F32, "sums1b", KIB + KIB // 2)
+        multiply(1, HALF, I, "bank0", "scalar", sums1b[:])
+        sums2a = tile([P, HALF], F32, "sums2a")
+        multiply(2, 0, HALF, "bank1", "vector", sums2a[:])
         quantise_values(3)
-        scatter(1, HALF, I, "vector", sums1[:, half(1)])
+        scatter(1, HALF, I, "vector", sums1b[:])
         store(1)
-        sums2 = tile([P, I], F32, "sums2")
-        multiply(2, 0, I, "o_bank1", "scalar", sums2[:])
-        for h in range(2):
-            scatter(2, h * HALF, (h + 1) * HALF, "scalar", sums2[:, half(h)])
+        sums2b = placed([P, HALF], F32, "sums2b", 3 * KIB + KIB // 2)
+        multiply(2, HALF, I, "bank2", "scalar", sums2b[:])
+        scatter(2, 0, HALF, "scalar", sums2a[:])
+        scatter(2, HALF, I, "scalar", sums2b[:])
         store(2)
         sums3 = tile([P, I], F32, "sums3")
-        multiply(3, 0, I, "o_bank0", "vector", sums3[:])
+        multiply(3, 0, I, "bank3", "vector", sums3[:])
         scatter(3, 0, I, "vector", sums3[:])
         store(3)

@@ -23,6 +23,7 @@ PACK = 4
 TILES = 4
 HALF = 256
 KIB = 1024
+POOL_BYTES = 4 * T
 
 
 def tile_attend_pickboth_kernel(tc, qpool_words, qpool_scales, keys_words, keys_scales, vals, mask, size, offs, offs2, out):
@@ -30,13 +31,16 @@ def tile_attend_pickboth_kernel(tc, qpool_words, qpool_scales, keys_words, keys_
     with ExitStack() as ctx:
         sb = ctx.enter_context(tc.tile_pool(name="sb", bufs=1))
         ps = ctx.enter_context(tc.psum_pool(name="ps", bufs=1))
-        overlap = ctx.enter_context(tc.tile_pool(name="overlap", bufs=1))
+        reuse = ctx.enter_context(tc.tile_pool(name="reuse", bufs=1))
 
         def tile(shape, dtype, name, on=None):
             return sb.tile(shape, dtype, name=name, tag=on or name, align_bytes=64)
 
-        def placed(shape, dtype, name, offset):
-            return overlap.tile(shape, dtype, name=name, offset=offset, align_bytes=64)
+        def on_values(e, kib, shape, dtype, name):
+            return reuse.tile(shape, dtype, name=name, offset=e * POOL_BYTES + kib * KIB, align_bytes=64)
+
+        def bank(b, shape, name):
+            return ps.tile(shape, F32, name=name, tag="bank%d" % b)
 
         def half(h):
             return slice(h * HALF, (h + 1) * HALF)
@@ -52,11 +56,11 @@ def tile_attend_pickboth_kernel(tc, qpool_words, qpool_scales, keys_words, keys_
         k_bytes = tile([P, T], U8, "k_bytes")
         size_col = tile([P, PACK], F32, "size_col")
         ident = tile([P, P], F32, "ident")
+        windows = {0: tile([P, T], F32, "window0")}
 
         nc.vector.memset(k_bytes[:].bitcast(I32), 0)
         nc.vector.memset(q_bytes[:].bitcast(I32), 0)
         make_identity(nc, ident[:])
-        windows = [tile([P, T], F32, "window0")]
         nc.vector.memset(windows[0][:].bitcast(I32), 0)
 
         def load_scale_rows(pool_bytes, rows):
@@ -66,18 +70,12 @@ def tile_attend_pickboth_kernel(tc, qpool_words, qpool_scales, keys_words, keys_
                     in_=rows[0, 4 * quad : 4 * quad + 4, :].bitcast(I32),
                 )
 
-        vals_sb = {}
         mask_sb = []
 
-        def load_values(e):
-            vals_sb[e] = placed([P, T], F32, "vals2", 0) if e == 2 else tile([P, T], F32, "vals%d" % e)
-            nc.sync.dma_start(out=vals_sb[e][:], in_=vals[e * P : (e + 1) * P, :])
-
-        def load_mask(count):
-            first = len(mask_sb)
-            rows = tile([P, count, J], F32, "mask%d" % first)
-            nc.sync.dma_start(out=rows[:], in_=mask[first * P : (first + count) * P, :].rearrange("(a p) j -> p a j", p=P))
-            mask_sb.extend(rows[:, a, :] for a in range(count))
+        def load_mask(h):
+            rows = tile([P, 2, J], F32, "mask%d" % h)
+            nc.sync.dma_start(out=rows[:], in_=mask[half(h), :].rearrange("(a p) j -> p a j", p=P))
+            mask_sb.extend(rows[:, a, :] for a in range(2))
 
         nc.sync.dma_start(k_list[:], offs2)
         nc.sync.dma_start(q_list[:], offs)
@@ -85,34 +83,35 @@ def tile_attend_pickboth_kernel(tc, qpool_words, qpool_scales, keys_words, keys_
         nc.sync.dma_start(out=k_words[:].bitcast(I32), in_=keys_words[0].bitcast(I32))
         load_scale_rows(q_bytes, qpool_scales)
         nc.sync.dma_start(out=q_words[:].bitcast(I32), in_=qpool_words[0].rearrange("p n t -> p (n t)").bitcast(I32))
-        load_mask(2)
+        load_mask(0)
         nc.sync.dma_start(out=size_col[:], in_=size.rearrange("o (p c) -> p (o c)", c=PACK))
-        load_mask(2)
-        for e in (0, 1, 3, 2):
-            load_values(e)
+        load_mask(1)
+        vals_sb = [on_values(e, 0, [P, T], F32, "vals%d" % e) for e in range(TILES)]
+        for e in range(TILES):
+            nc.sync.dma_start(out=vals_sb[e][:], in_=vals[e * P : (e + 1) * P, :])
 
         k_codes = tile([P, J], U16, "k_codes")
         k_scale = tile([P, J], U8, "k_scale")
         q_codes = tile([P, I], U32, "q_codes")
         q_scale = tile([P, I], U8, "q_scale")
-        nc.vector.tensor_copy(k_codes[:], k_words[:].indirect(k_list[:]))
         nc.vector.tensor_copy(k_scale[:], k_bytes[:].indirect(k_list[:]))
+        nc.vector.tensor_copy(k_codes[:], k_words[:].indirect(k_list[:]))
+        nc.vector.tensor_copy(q_scale[:], q_bytes[:].indirect(q_list[:]))
+        for first, last in ((0, P), (P, HALF), (HALF, I)):
+            nc.vector.tensor_copy(q_codes[:, first:last], q_words[:].indirect(entries(q_list, first, last)))
 
-        def zero_window(w, on):
-            windows.append(tile([P, T], F32, "window%d" % w, on))
-            nc.gpsimd.memset(windows[w][:], 0.0)
+        def zero_window(e, on):
+            windows[e] = tile([P, T], F32, "window%d" % e, on)
+            nc.gpsimd.memset(windows[e][:], 0.0)
 
         zero_window(1, "k_bytes")
         zero_window(2, "k_words")
+        zero_window(3, "q_bytes")
 
-        scores = [ps.tile([P, J], F32, name="scores%d" % i, tag="bank%d" % i) for i in range(TILES)]
-
-        def pick_queries(h):
-            listed = entries(q_list, h * HALF, (h + 1) * HALF)
-            nc.vector.tensor_copy(q_codes[:, half(h)], q_words[:].indirect(listed))
-
-        def score(i):
+        scores = {}
+        for i in (0, 1, 3, 2):
             cols = slice(i * P, (i + 1) * P)
+            scores[i] = bank(i, [P, J], "scores%d" % i)
             nc.tensor.matmul_mx(
                 out=scores[i][:],
                 lhsT=q_codes[:, cols].bitcast(FP8X4),
@@ -123,188 +122,186 @@ def tile_attend_pickboth_kernel(tc, qpool_words, qpool_scales, keys_words, keys_
                 stop=True,
             )
 
+        size_ps = bank(4, [P, PACK, P], "size_ps")
+        for c in range(PACK):
+            nc.tensor.transpose(size_ps[:, c, :], size_col[:, c : c + 1].to_broadcast([P, P]), ident[:])
+
         s_sb = [tile([P, J], F32, "s%d" % i) for i in range(TILES)]
-        p_sb = [tile([P, J], F32, "p%d" % i) for i in range(TILES)]
-        row_sums = [tile([P, 2], F32, "row_sums%d" % h) for h in range(2)]
-        inv_sums = [tile([P, 2], F32, "inv_sums%d" % h) for h in range(2)]
-        w_rows = {}
-        w_grouped = [tile([P, HALF * PACK], BF16, "w_grouped0"), placed([P, HALF * PACK], BF16, "w_grouped1", 8 * KIB)]
-        w_codes = tile([P, I], U32, "w_codes")
-        w_scale = tile([P, I], U8, "w_scale")
+        p_sb, inv_sum, neg_max, w_rows = {}, {}, {}, {}
+        first_sums = tile([P, 2], F32, "row_sums01")
+        row_sum = [first_sums[:, :1], first_sums[:, 1:], tile([P, 1], F32, "row_sum2")[:], tile([P, 1], F32, "row_sum3")[:]]
 
         def add_mask(i):
             nc.vector.tensor_tensor(s_sb[i][:], scores[i][:], mask_sb[i], ALU.add)
 
-        def add_mask_on_gpsimd(i):
-            raw = tile([P, J], F32, "raw%d" % i)
-            nc.scalar.copy(raw[:], scores[i][:])
-            nc.gpsimd.tensor_tensor(s_sb[i][:], raw[:], mask_sb[i], ALU.add)
+        def row_max(i, on=None):
+            neg_max[i] = tile([P, 1], F32, "neg_max%d" % i, on)
+            nc.vector.tensor_reduce(neg_max[i][:], s_sb[i][:], AX.X, ALU.max, negate=True)
 
-        def exponentials(i):
-            neg_max = tile([P, 1], F32, "neg_max%d" % i)
-            nc.vector.tensor_reduce(neg_max[:], s_sb[i][:], AX.X, ALU.max, negate=True)
-            nc.scalar.activation(p_sb[i][:], s_sb[i][:], ACT.Exp, bias=neg_max[:], accum_out=column(row_sums, i))
+        def exponentials(i, to):
+            p_sb[i] = to
+            nc.scalar.activation(to[:], s_sb[i][:], ACT.Exp, bias=neg_max[i][:], accum_out=row_sum[i])
 
-        def column(pairs, i):
-            return pairs[i // 2][:, i % 2 : i % 2 + 1]
+        def invert(i):
+            inv_sum[i] = tile([P, 1], F32, "inv_sum%d" % i)[:]
+            nc.vector.reciprocal(inv_sum[i], row_sum[i])
 
-        def invert(h):
-            nc.vector.reciprocal(inv_sums[h][:], row_sums[h][:])
-
-        def weights(i, on=None):
-            w_rows[i] = tile([P, J], BF16, "w%d" % i, on)
+        def weights(i, to):
+            w_rows[i] = to
             nc.vector.scalar_tensor_tensor(
-                w_rows[i][:].rearrange("m (p c) -> m p c", c=PACK),
+                to[:].rearrange("m (p c) -> m p c", c=PACK),
                 p_sb[i][:].rearrange("m (p c) -> m p c", c=PACK),
-                column(inv_sums, i),
+                inv_sum[i],
                 size_ps[:].rearrange("m c p -> m p c"),
                 ALU.mult,
                 ALU.mult,
             )
 
-        def weights_on_gpsimd(i):
-            sized = tile([P, J], F32, "sized%d" % i)
-            nc.gpsimd.tensor_tensor(sized[:], p_sb[i][:], size_sb[:], ALU.mult)
-            w_rows[i] = tile([P, J], BF16, "w%d" % i)
-            nc.gpsimd.tensor_scalar(w_rows[i][:], sized[:], column(inv_sums, i), 0.0, ALU.mult, ALU.add)
-
-        def copy_out(engine, to, bank):
+        def copy_out(engine, to, source):
             if engine == "vector":
-                nc.vector.tensor_copy(to, bank)
+                nc.vector.tensor_copy(to, source)
             else:
-                nc.scalar.copy(to, bank)
+                nc.scalar.copy(to, source)
 
-        def turn(rows, bank, grouped, engine="scalar"):
-            words = rows.bitcast(F32)
+        turned = {}
+
+        def turn(name, rows, b):
+            words = rows[:].bitcast(F32)
+            turned[name] = bank(b, [P, 2, P], "turned_" + name)
             for u in range(2):
-                nc.tensor.transpose(bank[:, u, :], words[:, u : J // 2 : 2], ident[:])
-            copy_out(engine, grouped.bitcast(F32).rearrange("p (r u) -> p r u", u=2), bank[:].rearrange("p u r -> p r u"))
+                nc.tensor.transpose(turned[name][:, u, :], words[:, u : J // 2 : 2], ident[:])
 
-        def turn_weights(i):
-            bank = ps.tile([P, 2, P], F32, name="w_turn%d" % i, tag="bank%d" % i)
-            turn(w_rows[i][:], bank, w_grouped[i // 2][:, i % 2 * P * PACK : (i % 2 + 1) * P * PACK])
+        def group(name, engine, to):
+            copy_out(engine, to.bitcast(F32).rearrange("p (r u) -> p r u", u=2), turned[name][:].rearrange("p u r -> p r u"))
 
-        def quantise_weights(h):
-            nc.vector.quantize_mx(out=w_codes[:, half(h)].bitcast(FP8X4), scales=w_scale[:, half(h)], in_=w_grouped[h][:])
+        def quantise(codes, scale, grouped):
+            nc.vector.quantize_mx(out=codes.bitcast(FP8X4), scales=scale, in_=grouped)
 
-        v_rows = {}
-        v_grouped = {}
-        v_codes = {}
+        v_rows, v_grouped, v_codes, w_codes, sums = {}, {}, {}, {}, {}
         v_scale = [tile([P, P], U8, "v_scale%d" % e) for e in range(TILES)]
+        w_scale = [tile([P, HALF], U8, "w_scale%d" % h) for h in range(2)]
 
-        def pick_values(e, engine, rows, first=0, last=J):
-            v_rows[e] = rows
-            picked = vals_sb[e][:].indirect(entries(k_list, first, last))
+        def pick_values(e, engine):
+            v_rows[e] = tile([P, J], BF16, "v_rows%d" % e)
+            picked = vals_sb[e][:].indirect(k_list[:])
             if engine == "vector":
-                nc.vector.tensor_copy(rows[:, first:last], picked)
+                nc.vector.tensor_copy(v_rows[e][:], picked)
             else:
-                nc.scalar.activation(rows[:, first:last], picked, ACT.Copy)
+                nc.scalar.activation(v_rows[e][:], picked, ACT.Copy)
 
-        def turn_values(e, grouped, engine="scalar"):
-            v_grouped[e] = grouped
-            turn(v_rows[e], ps.tile([P, 2, P], F32, name="v_turn%d" % e, tag="v_turn"), grouped, engine)
+        def group_values(e, engine, to=None):
+            v_grouped[e] = tile([P, P * PACK], BF16, "v_grouped%d" % e) if to is None else to
+            group("v%d" % e, engine, v_grouped[e][:])
 
-        def quantise_values(e, at=None):
-            v_codes[e] = tile([P, P], U32, "v_codes%d" % e) if at is None else placed([P, P], U32, "v_codes%d" % e, at)
-            nc.vector.quantize_mx(out=v_codes[e][:].bitcast(FP8X4), scales=v_scale[e][:], in_=v_grouped[e])
+        def quantise_values(e, to):
+            v_codes[e] = to
+            quantise(to[:], v_scale[e][:], v_grouped[e][:])
 
-        def multiply(e, first, last, bank, engine, sums):
-            o_ps = ps.tile([P, last - first], F32, name="o_ps%d_%d" % (e, first), tag=bank)
+        def product(e, h, o_ps):
             nc.tensor.matmul_mx(
-                out=o_ps[:],
+                out=o_ps,
                 lhsT=v_codes[e][:].bitcast(FP8X4),
                 lhsT_scale=v_scale[e][:],
-                rhs=w_codes[:, first:last].bitcast(FP8X4),
-                rhs_scale=w_scale[:, first:last],
+                rhs=w_codes[h][:].bitcast(FP8X4),
+                rhs_scale=w_scale[h][:],
                 start=True,
                 stop=True,
             )
-            copy_out(engine, sums, o_ps[:])
 
-        def scatter(e, first, last, engine, sums):
-            places = windows[e][:].indirect(entries(q_list, first, last))
+        def multiply(e, h, b, engine, to):
+            o_ps = bank(b, [P, HALF], "o_ps%d_%d" % (e, h))
+            product(e, h, o_ps[:])
+            sums[e, h] = to[:]
+            copy_out(engine, to[:], o_ps[:])
+
+        def scatter(e, h, engine):
+            places = windows[e][:].indirect(entries(q_list, h * HALF, (h + 1) * HALF))
             if engine == "vector":
-                nc.vector.tensor_copy(places, sums)
+                nc.vector.tensor_copy(places, sums[e, h])
             else:
-                nc.scalar.activation(places, sums, ACT.Copy)
+                nc.scalar.activation(places, sums[e, h], ACT.Copy)
 
         def store(e):
             nc.sync.dma_start(out=out[e * P : (e + 1) * P, :], in_=windows[e][:])
 
-        nc.vector.tensor_copy(q_scale[:], q_bytes[:].indirect(q_list[:]))
-        for h in range(2):
-            pick_queries(h)
-        zero_window(3, "q_bytes")
-        for i in (0, 1, 3, 2):
-            score(i)
+        def sums_tile(e, h, on=None):
+            return tile([P, HALF], F32, "sums%d_%d" % (e, h), on)
 
-        size_ps = ps.tile([P, PACK, P], F32, name="size_ps")
-        for c in range(PACK):
-            nc.tensor.transpose(size_ps[:, c, :], size_col[:, c : c + 1].to_broadcast([P, P]), ident[:])
-        size_sb = tile([P, J], F32, "size_sb")
-        nc.scalar.activation(size_sb[:].rearrange("m (p c) -> m p c", c=PACK), size_ps[:].rearrange("m c p -> m p c"), ACT.Copy)
+        raw = tile([P, J], F32, "raw3")
+        nc.scalar.copy(raw[:], scores[3][:])
+        nc.gpsimd.tensor_tensor(s_sb[3][:], raw[:], mask_sb[3], ALU.add)
 
-        def rows_tile(e, on=None):
-            return tile([P, J], BF16, "v_rows%d" % e, on)[:]
-
-        def grouped_tile(e, on=None):
-            return tile([P, P * PACK], BF16, "v_grouped%d" % e, on)[:]
-
-        add_mask_on_gpsimd(3)
         add_mask(0)
         add_mask(1)
-        exponentials(0)
+        row_max(0)
+        exponentials(0, tile([P, J], F32, "p0"))
+        row_max(1)
+        exponentials(1, tile([P, J], F32, "p1"))
         add_mask(2)
-        for i in (1, 2, 3):
-            exponentials(i)
-        invert(0)
-        pick_values(0, "vector", rows_tile(0))
-        invert(1)
-        weights(1, "s3")
-        weights_on_gpsimd(0)
-        staged = tile([P, HALF + P * PACK], BF16, "staged", "neg_max3")
-        pick_values(1, "scalar", staged[:, :J], 0, HALF)
-        turn_weights(0)
-        turn_values(0, staged[:, HALF:])
-        turn_weights(1)
-        weights(2)
-        weights(3)
-        quantise_values(0)
-        quantise_weights(0)
-        turn_weights(2)
-        turn_weights(3)
-        pick_values(1, "vector", staged[:, :J], HALF, J)
-        sums0a = tile([P, HALF], F32, "sums0a")
-        multiply(0, 0, HALF, "o_bank0", "scalar", sums0a[:])
-        scatter(0, 0, HALF, "scalar", sums0a[:])
-        quantise_weights(1)
-        turn_values(1, grouped_tile(1), "vector")
-        pick_values(2, "vector", placed([P, J], BF16, "v_rows2", 9 * KIB)[:])
-        quantise_values(1, 0)
-        pick_values(3, "vector", placed([P, J], BF16, "v_rows3", KIB)[:])
-        turn_values(2, grouped_tile(2))
-        sums0b = placed([P, HALF], F32, "sums0b", 9 * KIB)
-        multiply(0, HALF, I, "o_bank1", "scalar", sums0b[:])
-        quantise_values(2)
-        scatter(0, HALF, I, "vector", sums0b[:])
+        row_max(2)
+        first_inv = tile([P, 2], F32, "inv_sums01")
+        nc.vector.reciprocal(first_inv[:], first_sums[:])
+        inv_sum.update({0: first_inv[:, :1], 1: first_inv[:, 1:]})
+        pick_values(0, "scalar")
+        turn("v0", v_rows[0], 5)
+        exponentials(2, on_values(0, 0, [P, J], F32, "p2"))
+        w_grouped = tile([P, HALF * PACK], BF16, "w_grouped01")
+        for i in range(2):
+            weights(i, tile([P, J], BF16, "w%d" % i))
+            turn("w%d" % i, w_rows[i], i)
+        row_max(3, "p0")
+        invert(2)
+        group("w0", "scalar", w_grouped[:, : P * PACK])
+        exponentials(3, tile([P, J], F32, "p3"))
+        group_values(0, "scalar")
+        group("w1", "scalar", w_grouped[:, P * PACK :])
+        weights(2, tile([P, J], BF16, "w2"))
+        turn("w2", w_rows[2], 2)
+        invert(3)
+        quantise_values(0, tile([P, P], U32, "v_codes0"))
+        w_codes[0] = tile([P, HALF], U32, "w_codes0")
+        quantise(w_codes[0][:], w_scale[0][:], w_grouped[:])
+        weights(3, tile([P, J], BF16, "w3"))
+        turn("w3", w_rows[3], 3)
+
+        pick_values(1, "scalar")
+        w_grouped2 = on_values(1, 0, [P, P * PACK], BF16, "w_grouped2")
+        group("w2", "scalar", w_grouped2[:])
+        multiply(0, 0, 7, "scalar", on_values(1, 1, [P, HALF], F32, "sums0_0"))
+        scatter(0, 0, "scalar")
+        turn("v1", v_rows[1], 4)
+
+        pick_values(2, "vector")
+        turn("v2", v_rows[2], 5)
+        w_grouped3 = on_values(2, 0, [P, P * PACK], BF16, "w_grouped3")
+        group("w3", "vector", w_grouped3[:])
+        w_codes[1] = on_values(2, 1, [P, HALF], U32, "w_codes1")
+        quantise(w_codes[1][:, :P], w_scale[1][:, :P], w_grouped2[:])
+        quantise(w_codes[1][:, P:], w_scale[1][:, P:], w_grouped3[:])
+        group_values(1, "vector", on_values(2, 2, [P, P * PACK], BF16, "v_grouped1"))
+        group_values(2, "scalar")
+        quantise_values(1, tile([P, P], U32, "v_codes1"))
+        multiply(0, 1, 1, "scalar", sums_tile(0, 1))
+        scatter(0, 1, "scalar")
         store(0)
-        sums1a = placed([P, I], F32, "sums1a", 2 * KIB)[:, :HALF]
-        multiply(1, 0, HALF, "o_bank0", "scalar", sums1a)
-        scatter(1, 0, HALF, "scalar", sums1a)
-        turn_values(3, placed([P, P * PACK], BF16, "v_grouped3", 2 * KIB + KIB // 2)[:])
-        sums1b = placed([P, HALF], F32, "sums1b", KIB + KIB // 2)
-        multiply(1, HALF, I, "bank0", "scalar", sums1b[:])
-        sums2a = tile([P, HALF], F32, "sums2a")
-        multiply(2, 0, HALF, "bank1", "vector", sums2a[:])
-        quantise_values(3)
-        scatter(1, HALF, I, "vector", sums1b[:])
+        multiply(1, 1, 1, "scalar", sums_tile(1, 1))
+
+        pick_values(3, "vector")
+        turn("v3", v_rows[3], 6)
+        multiply(1, 0, 0, "vector", on_values(3, 0, [P, HALF], F32, "sums1_0"))
+        quantise_values(2, on_values(3, 1, [P, P], U32, "v_codes2"))
+        scatter(1, 0, "vector")
+        group_values(3, "scalar")
+        scatter(1, 1, "scalar")
         store(1)
-        sums2b = placed([P, HALF], F32, "sums2b", 3 * KIB + KIB // 2)
-        multiply(2, HALF, I, "bank2", "scalar", sums2b[:])
-        scatter(2, 0, HALF, "scalar", sums2a[:])
-        scatter(2, HALF, I, "scalar", sums2b[:])
+        multiply(2, 0, 2, "vector", sums_tile(2, 0))
+        quantise_values(3, tile([P, P], U32, "v_codes3"))
+        scatter(2, 0, "vector")
+        multiply(2, 1, 3, "scalar", sums_tile(2, 1))
+        scatter(2, 1, "scalar")
         store(2)
-        sums3 = tile([P, I], F32, "sums3")
-        multiply(3, 0, I, "bank3", "vector", sums3[:])
-        scatter(3, 0, I, "vector", sums3[:])
+        multiply(3, 0, 4, "vector", sums_tile(3, 0))
+        scatter(3, 0, "vector")
+        multiply(3, 1, 3, "scalar", sums_tile(3, 1))
+        scatter(3, 1, "scalar")
         store(3)

@@ -56,12 +56,13 @@ def tile_attend_pickboth_kernel(tc, qpool_words, qpool_scales, keys_words, keys_
         k_bytes = tile([P, T], U8, "k_bytes")
         size_col = tile([P, PACK], F32, "size_col")
         ident = tile([P, P], F32, "ident")
-        windows = {0: tile([P, T], F32, "window0")}
+        windows = {e: tile([P, T], F32, "window%d" % e) for e in range(2)}
 
         nc.vector.memset(k_bytes[:].bitcast(I32), 0)
         nc.vector.memset(q_bytes[:].bitcast(I32), 0)
         make_identity(nc, ident[:])
-        nc.vector.memset(windows[0][:].bitcast(I32), 0)
+        for e in range(2):
+            nc.vector.memset(windows[e][:].bitcast(I32), 0)
 
         def load_scale_rows(pool_bytes, rows):
             for quad in range(4):
@@ -104,9 +105,7 @@ def tile_attend_pickboth_kernel(tc, qpool_words, qpool_scales, keys_words, keys_
             windows[e] = tile([P, T], F32, "window%d" % e, on)
             nc.gpsimd.memset(windows[e][:], 0.0)
 
-        zero_window(1, "k_bytes")
-        zero_window(2, "k_words")
-        zero_window(3, "q_bytes")
+        zero_window(2, "q_words")
 
         scores = {}
         for i in (0, 1, 3, 2):
@@ -230,6 +229,7 @@ def tile_attend_pickboth_kernel(tc, qpool_words, qpool_scales, keys_words, keys_
         raw = tile([P, J], F32, "raw3")
         nc.scalar.copy(raw[:], scores[3][:])
         nc.gpsimd.tensor_tensor(s_sb[3][:], raw[:], mask_sb[3], ALU.add)
+        zero_window(3, "raw3")
 
         add_mask(0)
         add_mask(1)

@@ -65,7 +65,7 @@ def tile_attend_pickboth_kernel(tc, qpool_words, qpool_scales, keys_words, keys_
             nc.vector.memset(windows[e][:].bitcast(I32), 0)
 
         def load_scale_rows(pool_bytes, rows):
-            for quad in range(4):
+            for quad in (0, 2, 1, 3):
                 nc.sync.dma_start(
                     out=pool_bytes[32 * quad : 32 * quad + 4, :].bitcast(I32),
                     in_=rows[0, 4 * quad : 4 * quad + 4, :].bitcast(I32),
@@ -80,12 +80,12 @@ def tile_attend_pickboth_kernel(tc, qpool_words, qpool_scales, keys_words, keys_
 
         nc.sync.dma_start(k_list[:], offs2)
         nc.sync.dma_start(q_list[:], offs)
+        nc.sync.dma_start(out=size_col[:], in_=size.rearrange("o (p c) -> p (o c)", c=PACK))
         load_scale_rows(k_bytes, keys_scales)
-        nc.sync.dma_start(out=k_words[:].bitcast(I32), in_=keys_words[0].bitcast(I32))
         load_scale_rows(q_bytes, qpool_scales)
+        nc.sync.dma_start(out=k_words[:].bitcast(I32), in_=keys_words[0].bitcast(I32))
         nc.sync.dma_start(out=q_words[:].bitcast(I32), in_=qpool_words[0].rearrange("p n t -> p (n t)").bitcast(I32))
         load_mask(0)
-        nc.sync.dma_start(out=size_col[:], in_=size.rearrange("o (p c) -> p (o c)", c=PACK))
         load_mask(1)
         vals_sb = [on_values(e, 0, [P, T], F32, "vals%d" % e) for e in range(TILES)]
         for e in range(TILES):
@@ -96,8 +96,8 @@ def tile_attend_pickboth_kernel(tc, qpool_words, qpool_scales, keys_words, keys_
         q_codes = tile([P, I], U32, "q_codes")
         q_scale = tile([P, I], U8, "q_scale")
         nc.vector.tensor_copy(k_scale[:], k_bytes[:].indirect(k_list[:]))
-        nc.vector.tensor_copy(k_codes[:], k_words[:].indirect(k_list[:]))
         nc.vector.tensor_copy(q_scale[:], q_bytes[:].indirect(q_list[:]))
+        nc.vector.tensor_copy(k_codes[:], k_words[:].indirect(k_list[:]))
         for first, last in ((0, P), (P, HALF), (HALF, I)):
             nc.vector.tensor_copy(q_codes[:, first:last], q_words[:].indirect(entries(q_list, first, last)))
 

@@ -65,11 +65,8 @@ def tile_attend_pickboth_kernel(tc, qpool_words, qpool_scales, keys_words, keys_
             nc.vector.memset(windows[e][:].bitcast(I32), 0)
 
         def load_scale_rows(pool_bytes, rows):
-            for quad in (0, 2, 1, 3):
-                nc.sync.dma_start(
-                    out=pool_bytes[32 * quad : 32 * quad + 4, :].bitcast(I32),
-                    in_=rows[0, 4 * quad : 4 * quad + 4, :].bitcast(I32),
-                )
+            for r in range(4):
+                nc.sync.dma_start(out=pool_bytes[r:P:32, :].bitcast(I32), in_=rows[0, r:16:4, :].bitcast(I32))
 
         mask_sb = []
 

@@ -124,8 +124,7 @@ def tile_attend_pickboth_kernel(tc, qpool_words, qpool_scales, keys_words, keys_
 
         s_sb = [tile([P, J], F32, "s%d" % i) for i in range(TILES)]
         p_sb, inv_sum, neg_max, w_rows = {}, {}, {}, {}
-        first_sums = tile([P, 2], F32, "row_sums01")
-        row_sum = [first_sums[:, :1], first_sums[:, 1:], tile([P, 1], F32, "row_sum2")[:], tile([P, 1], F32, "row_sum3")[:]]
+        row_sum = [tile([P, 1], F32, "row_sum%d" % i)[:] for i in range(TILES)]
 
         def add_mask(i):
             nc.vector.tensor_tensor(s_sb[i][:], scores[i][:], mask_sb[i], ALU.add)
@@ -235,31 +234,31 @@ def tile_attend_pickboth_kernel(tc, qpool_words, qpool_scales, keys_words, keys_
         row_max(1)
         exponentials(1, tile([P, J], F32, "p1"))
         add_mask(2)
+        invert(0)
         row_max(2)
-        first_inv = tile([P, 2], F32, "inv_sums01")
-        nc.vector.reciprocal(first_inv[:], first_sums[:])
-        inv_sum.update({0: first_inv[:, :1], 1: first_inv[:, 1:]})
         pick_values(0, "scalar")
         turn("v0", v_rows[0], 5)
         exponentials(2, on_values(0, 0, [P, J], F32, "p2"))
         w_grouped = tile([P, HALF * PACK], BF16, "w_grouped01")
-        for i in range(2):
-            weights(i, tile([P, J], BF16, "w%d" % i))
-            turn("w%d" % i, w_rows[i], i)
+        weights(0, tile([P, J], BF16, "w0"))
+        turn("w0", w_rows[0], 0)
+        invert(1)
         row_max(3, "p0")
-        invert(2)
-        group("w0", "scalar", w_grouped[:, : P * PACK])
         exponentials(3, tile([P, J], F32, "p3"))
+        weights(1, tile([P, J], BF16, "w1"))
+        turn("w1", w_rows[1], 1)
         group_values(0, "scalar")
+        group("w0", "scalar", w_grouped[:, : P * PACK])
         group("w1", "scalar", w_grouped[:, P * PACK :])
+        invert(2)
         weights(2, tile([P, J], BF16, "w2"))
         turn("w2", w_rows[2], 2)
         invert(3)
         quantise_values(0, tile([P, P], U32, "v_codes0"))
-        w_codes[0] = tile([P, HALF], U32, "w_codes0")
-        quantise(w_codes[0][:], w_scale[0][:], w_grouped[:])
         weights(3, tile([P, J], BF16, "w3"))
         turn("w3", w_rows[3], 3)
+        w_codes[0] = tile([P, HALF], U32, "w_codes0")
+        quantise(w_codes[0][:], w_scale[0][:], w_grouped[:])
 
         pick_values(1, "scalar")
         w_grouped2 = on_values(1, 0, [P, P * PACK], BF16, "w_grouped2")
@@ -274,8 +273,8 @@ def tile_attend_pickboth_kernel(tc, qpool_words, qpool_scales, keys_words, keys_
         group("w3", "vector", w_grouped3[:])
         w_codes[1] = on_values(2, 1, [P, HALF], U32, "w_codes1")
         quantise(w_codes[1][:, :P], w_scale[1][:, :P], w_grouped2[:])
-        quantise(w_codes[1][:, P:], w_scale[1][:, P:], w_grouped3[:])
         group_values(1, "vector", on_values(2, 2, [P, P * PACK], BF16, "v_grouped1"))
+        quantise(w_codes[1][:, P:], w_scale[1][:, P:], w_grouped3[:])
         group_values(2, "scalar")
         quantise_values(1, tile([P, P], U32, "v_codes1"))
         multiply(0, 1, 1, "scalar", sums_tile(0, 1))

@@ -238,34 +238,35 @@ def tile_attend_pickboth_kernel(tc, qpool_words, qpool_scales, keys_words, keys_
         row_max(2)
         pick_values(0, "scalar")
         turn("v0", v_rows[0], 5)
-        exponentials(2, on_values(0, 0, [P, J], F32, "p2"))
+        exponentials(2, tile([P, J], F32, "p2", "p0"))
         w_grouped = tile([P, HALF * PACK], BF16, "w_grouped01")
         weights(0, tile([P, J], BF16, "w0"))
         turn("w0", w_rows[0], 0)
         invert(1)
-        row_max(3, "p0")
+        row_max(3, "row_sum0")
         exponentials(3, tile([P, J], F32, "p3"))
         weights(1, tile([P, J], BF16, "w1"))
         turn("w1", w_rows[1], 1)
-        group_values(0, "scalar")
         group("w0", "scalar", w_grouped[:, : P * PACK])
         group("w1", "scalar", w_grouped[:, P * PACK :])
         invert(2)
+        group_values(0, "vector")
         weights(2, tile([P, J], BF16, "w2"))
         turn("w2", w_rows[2], 2)
         invert(3)
         quantise_values(0, tile([P, P], U32, "v_codes0"))
-        weights(3, tile([P, J], BF16, "w3"))
-        turn("w3", w_rows[3], 3)
         w_codes[0] = tile([P, HALF], U32, "w_codes0")
         quantise(w_codes[0][:], w_scale[0][:], w_grouped[:])
+        weights(3, tile([P, J], BF16, "w3"))
+        turn("w3", w_rows[3], 3)
 
         pick_values(1, "scalar")
-        w_grouped2 = on_values(1, 0, [P, P * PACK], BF16, "w_grouped2")
+        w_grouped2 = tile([P, P * PACK], BF16, "w_grouped2", "w_grouped01")
         group("w2", "scalar", w_grouped2[:])
-        multiply(0, 0, 7, "scalar", on_values(1, 1, [P, HALF], F32, "sums0_0"))
+        multiply(0, 0, 7, "scalar", sums_tile(0, 0))
+        turn("v1", v_rows[1], 6)
+        group_values(1, "scalar")
         scatter(0, 0, "scalar")
-        turn("v1", v_rows[1], 4)
 
         pick_values(2, "vector")
         turn("v2", v_rows[2], 5)
@@ -273,17 +274,16 @@ def tile_attend_pickboth_kernel(tc, qpool_words, qpool_scales, keys_words, keys_
         group("w3", "vector", w_grouped3[:])
         w_codes[1] = on_values(2, 1, [P, HALF], U32, "w_codes1")
         quantise(w_codes[1][:, :P], w_scale[1][:, :P], w_grouped2[:])
-        group_values(1, "vector", on_values(2, 2, [P, P * PACK], BF16, "v_grouped1"))
         quantise(w_codes[1][:, P:], w_scale[1][:, P:], w_grouped3[:])
         group_values(2, "scalar")
-        quantise_values(1, tile([P, P], U32, "v_codes1"))
+        quantise_values(1, on_values(2, 2, [P, P], U32, "v_codes1"))
         multiply(0, 1, 1, "scalar", sums_tile(0, 1))
         scatter(0, 1, "scalar")
         store(0)
         multiply(1, 1, 1, "scalar", sums_tile(1, 1))
 
         pick_values(3, "vector")
-        turn("v3", v_rows[3], 6)
+        turn("v3", v_rows[3], 4)
         multiply(1, 0, 0, "vector", on_values(3, 0, [P, HALF], F32, "sums1_0"))
         quantise_values(2, on_values(3, 1, [P, P], U32, "v_codes2"))
         scatter(1, 0, "vector")
@@ -296,7 +296,7 @@ def tile_attend_pickboth_kernel(tc, qpool_words, qpool_scales, keys_words, keys_
         multiply(2, 1, 3, "scalar", sums_tile(2, 1))
         scatter(2, 1, "scalar")
         store(2)
-        multiply(3, 0, 4, "vector", sums_tile(3, 0))
+        multiply(3, 0, 6, "vector", sums_tile(3, 0))
         scatter(3, 0, "vector")
         multiply(3, 1, 3, "scalar", sums_tile(3, 1))
         scatter(3, 1, "scalar")

from contextlib import ExitStack

import concourse.mybir as mybir
from concourse.masks import make_identity

D, T, I, J, E = 512, 2048, 512, 512, 512
FLOPS = 2 * D * I * J + 2 * J * E * I

F32 = mybir.dt.float32
BF16 = mybir.dt.bfloat16
I32 = mybir.dt.int32
U32 = mybir.dt.uint32
U16 = mybir.dt.uint16
U8 = mybir.dt.uint8
FP8X4 = mybir.dt.float8_e4m3fn_x4
FP4X4 = mybir.dt.float4_e2m1fn_x4
ALU = mybir.AluOpType
ACT = mybir.ActivationFunctionType
AX = mybir.AxisListType

P = 128
PACK = 4
TILES = 4
HALF = 256
KIB = 1024
POOL_BYTES = 4 * T


def tile_attend_pickboth_kernel(tc, qpool_words, qpool_scales, keys_words, keys_scales, vals, mask, size, offs, offs2, out):
    nc = tc.nc
    with ExitStack() as ctx:
        sb = ctx.enter_context(tc.tile_pool(name="sb", bufs=1))
        ps = ctx.enter_context(tc.psum_pool(name="ps", bufs=1))
        reuse = ctx.enter_context(tc.tile_pool(name="reuse", bufs=1))

        def tile(shape, dtype, name, on=None):
            return sb.tile(shape, dtype, name=name, tag=on or name, align_bytes=64)

        def on_values(e, kib, shape, dtype, name):
            return reuse.tile(shape, dtype, name=name, offset=e * POOL_BYTES + kib * KIB, align_bytes=64)

        def bank(b, shape, name):
            return ps.tile(shape, F32, name=name, tag="bank%d" % b)

        def half(h):
            return slice(h * HALF, (h + 1) * HALF)

        def entries(whole, first, last):
            return whole[:, first // 16 : last // 16]

        q_list = sb.tile([P, I // 16], U16, name="q_list")
        k_list = sb.tile([P, J // 16], U16, name="k_list")
        q_words = tile([P, T], U32, "q_words")
        k_words = tile([P, T], U16, "k_words")
        q_bytes = tile([P, T], U8, "q_bytes")
        k_bytes = tile([P, T], U8, "k_bytes")
        size_col = tile([P, PACK], F32, "size_col")
        ident = tile([P, P], F32, "ident")
        windows = {e: tile([P, T], F32, "window%d" % e) for e in range(2)}

        nc.vector.memset(k_bytes[:].bitcast(I32), 0)
        nc.vector.memset(q_bytes[:].bitcast(I32), 0)
        make_identity(nc, ident[:])
        for e in range(2):
            nc.vector.memset(windows[e][:].bitcast(I32), 0)

        def load_scale_rows(pool_bytes, rows):
            for r in range(4):
                nc.sync.dma_start(out=pool_bytes[r:P:32, :].bitcast(I32), in_=rows[0, r:16:4, :].bitcast(I32))

        mask_sb = []

        def load_mask(h):
            rows = tile([P, 2, J], F32, "mask%d" % h)
            nc.sync.dma_start(out=rows[:], in_=mask[half(h), :].rearrange("(a p) j -> p a j", p=P))
            mask_sb.extend(rows[:, a, :] for a in range(2))

        nc.sync.dma_start(k_list[:], offs2)
        nc.sync.dma_start(q_list[:], offs)
        nc.sync.dma_start(out=size_col[:], in_=size.rearrange("o (p c) -> p (o c)", c=PACK))
        load_scale_rows(k_bytes, keys_scales)
        load_scale_rows(q_bytes, qpool_scales)
        nc.sync.dma_start(out=k_words[:].bitcast(I32), in_=keys_words[0].bitcast(I32))
        nc.sync.dma_start(out=q_words[:].bitcast(I32), in_=qpool_words[0].rearrange("p n t -> p (n t)").bitcast(I32))
        load_mask(0)
        load_mask(1)
        vals_sb = [on_values(e, 0, [P, T], F32, "vals%d" % e) for e in range(TILES)]
        for e in range(TILES):
            nc.sync.dma_start(out=vals_sb[e][:], in_=vals[e * P : (e + 1) * P, :])

        k_codes = tile([P, J], U16, "k_codes")
        k_scale = tile([P, J], U8, "k_scale")
        q_codes = tile([P, I], U32, "q_codes")
        q_scale = tile([P, I], U8, "q_scale")
        nc.vector.tensor_copy(k_scale[:], k_bytes[:].indirect(k_list[:]))
        nc.vector.tensor_copy(q_scale[:], q_bytes[:].indirect(q_list[:]))
        nc.vector.tensor_copy(k_codes[:], k_words[:].indirect(k_list[:]))
        for first, last in ((0, P), (P, HALF), (HALF, I)):
            nc.vector.tensor_copy(q_codes[:, first:last], q_words[:].indirect(entries(q_list, first, last)))

        def zero_window(e, on):
            windows[e] = tile([P, T], F32, "window%d" % e, on)
            nc.gpsimd.memset(windows[e][:], 0.0)

        zero_window(2, "q_words")

        scores = {}
        for i in (0, 1, 3, 2):
            cols = slice(i * P, (i + 1) * P)
            scores[i] = bank(i, [P, J], "scores%d" % i)
            nc.tensor.matmul_mx(
                out=scores[i][:],
                lhsT=q_codes[:, cols].bitcast(FP8X4),
                lhsT_scale=q_scale[:, cols],
                rhs=k_codes[:].bitcast(FP4X4),
                rhs_scale=k_scale[:],
                start=True,
                stop=True,
            )

        size_ps = bank(4, [P, PACK, P], "size_ps")
        for c in range(PACK):
            nc.tensor.transpose(size_ps[:, c, :], size_col[:, c : c + 1].to_broadcast([P, P]), ident[:])

        s_sb = [tile([P, J], F32, "s%d" % i) for i in range(TILES)]
        p_sb, inv_sum, neg_max, w_rows = {}, {}, {}, {}
        row_sum = [tile([P, 1], F32, "row_sum%d" % i)[:] for i in range(TILES)]

        def add_mask(i):
            nc.vector.tensor_tensor(s_sb[i][:], scores[i][:], mask_sb[i], ALU.add)

        def row_max(i, on=None):
            neg_max[i] = tile([P, 1], F32, "neg_max%d" % i, on)
            nc.vector.tensor_reduce(neg_max[i][:], s_sb[i][:], AX.X, ALU.max, negate=True)

        def exponentials(i, to):
            p_sb[i] = to
            nc.scalar.activation(to[:], s_sb[i][:], ACT.Exp, bias=neg_max[i][:], accum_out=row_sum[i])

        def invert(i):
            inv_sum[i] = tile([P, 1], F32, "inv_sum%d" % i)[:]
            nc.vector.reciprocal(inv_sum[i], row_sum[i])

        def weights(i, to):
            w_rows[i] = to
            nc.vector.scalar_tensor_tensor(
                to[:].rearrange("m (p c) -> m p c", c=PACK),
                p_sb[i][:].rearrange("m (p c) -> m p c", c=PACK),
                inv_sum[i],
                size_ps[:].rearrange("m c p -> m p c"),
                ALU.mult,
                ALU.mult,
            )

        def copy_out(engine, to, source):
            if engine == "vector":
                nc.vector.tensor_copy(to, source)
            else:
                nc.scalar.copy(to, source)

        turned = {}

        def turn(name, rows, b):
            words = rows[:].bitcast(F32)
            turned[name] = bank(b, [P, 2, P], "turned_" + name)
            for u in range(2):
                nc.tensor.transpose(turned[name][:, u, :], words[:, u : J // 2 : 2], ident[:])

        def group(name, engine, to):
            copy_out(engine, to.bitcast(F32).rearrange("p (r u) -> p r u", u=2), turned[name][:].rearrange("p u r -> p r u"))

        def quantise(codes, scale, grouped):
            nc.vector.quantize_mx(out=codes.bitcast(FP8X4), scales=scale, in_=grouped)

        v_rows, v_grouped, v_codes, w_codes, sums = {}, {}, {}, {}, {}
        v_scale = [tile([P, P], U8, "v_scale%d" % e) for e in range(TILES)]
        w_scale = [tile([P, HALF], U8, "w_scale%d" % h) for h in range(2)]

        def pick_values(e, engine):
            v_rows[e] = tile([P, J], BF16, "v_rows%d" % e)
            picked = vals_sb[e][:].indirect(k_list[:])
            if engine == "vector":
                nc.vector.tensor_copy(v_rows[e][:], picked)
            else:
                nc.scalar.activation(v_rows[e][:], picked, ACT.Copy)

        def group_values(e, engine, to=None):
            v_grouped[e] = tile([P, P * PACK], BF16, "v_grouped%d" % e) if to is None else to
            group("v%d" % e, engine, v_grouped[e][:])

        def quantise_values(e, to):
            v_codes[e] = to
            quantise(to[:], v_scale[e][:], v_grouped[e][:])

        def product(e, h, o_ps):
            nc.tensor.matmul_mx(
                out=o_ps,
                lhsT=v_codes[e][:].bitcast(FP8X4),
                lhsT_scale=v_scale[e][:],
                rhs=w_codes[h][:].bitcast(FP8X4),
                rhs_scale=w_scale[h][:],
                start=True,
                stop=True,
            )

        def multiply(e, h, b, engine, to):
            o_ps = bank(b, [P, HALF], "o_ps%d_%d" % (e, h))
            product(e, h, o_ps[:])
            sums[e, h] = to[:]
            copy_out(engine, to[:], o_ps[:])

        def scatter(e, h, engine):
            places = windows[e][:].indirect(entries(q_list, h * HALF, (h + 1) * HALF))
            if engine == "vector":
                nc.vector.tensor_copy(places, sums[e, h])
            else:
                nc.scalar.activation(places, sums[e, h], ACT.Copy)

        def store(e):
            nc.sync.dma_start(out=out[e * P : (e + 1) * P, :], in_=windows[e][:])

        def sums_tile(e, h, on=None):
            return tile([P, HALF], F32, "sums%d_%d" % (e, h), on)

        raw = tile([P, J], F32, "raw3")
        nc.scalar.copy(raw[:], scores[3][:])
        nc.gpsimd.tensor_tensor(s_sb[3][:], raw[:], mask_sb[3], ALU.add)
        zero_window(3, "raw3")

        add_mask(0)
        add_mask(1)
        row_max(0)
        exponentials(0, tile([P, J], F32, "p0"))
        row_max(1)
        exponentials(1, tile([P, J], F32, "p1"))
        add_mask(2)
        invert(0)
        row_max(2)
        pick_values(0, "scalar")
        turn("v0", v_rows[0], 5)
        exponentials(2, tile([P, J], F32, "p2", "p0"))
        w_grouped = tile([P, HALF * PACK], BF16, "w_grouped01")
        weights(0, tile([P, J], BF16, "w0"))
        turn("w0", w_rows[0], 0)
        invert(1)
        row_max(3, "row_sum0")
        exponentials(3, tile([P, J], F32, "p3"))
        weights(1, tile([P, J], BF16, "w1"))
        turn("w1", w_rows[1], 1)
        group("w0", "scalar", w_grouped[:, : P * PACK])
        group("w1", "scalar", w_grouped[:, P * PACK :])
        invert(2)
        group_values(0, "vector")
        weights(2, tile([P, J], BF16, "w2"))
        turn("w2", w_rows[2], 2)
        invert(3)
        quantise_values(0, tile([P, P], U32, "v_codes0"))
        w_codes[0] = tile([P, HALF], U32, "w_codes0")
        quantise(w_codes[0][:], w_scale[0][:], w_grouped[:])
        weights(3, tile([P, J], BF16, "w3"))
        turn("w3", w_rows[3], 3)

        pick_values(1, "scalar")
        w_grouped2 = tile([P, P * PACK], BF16, "w_grouped2", "w_grouped01")
        group("w2", "scalar", w_grouped2[:])
        multiply(0, 0, 7, "scalar", sums_tile(0, 0))
        turn("v1", v_rows[1], 6)
        group_values(1, "scalar")
        scatter(0, 0, "scalar")

        pick_values(2, "vector")
        turn("v2", v_rows[2], 5)
        w_grouped3 = on_values(2, 0, [P, P * PACK], BF16, "w_grouped3")
        group("w3", "vector", w_grouped3[:])
        w_codes[1] = on_values(2, 1, [P, HALF], U32, "w_codes1")
        quantise(w_codes[1][:, :P], w_scale[1][:, :P], w_grouped2[:])
        quantise(w_codes[1][:, P:], w_scale[1][:, P:], w_grouped3[:])
        group_values(2, "scalar")
        quantise_values(1, on_values(2, 2, [P, P], U32, "v_codes1"))
        multiply(0, 1, 1, "scalar", sums_tile(0, 1))
        scatter(0, 1, "scalar")
        store(0)
        multiply(1, 1, 1, "scalar", sums_tile(1, 1))

        pick_values(3, "vector")
        turn("v3", v_rows[3], 4)
        multiply(1, 0, 0, "vector", on_values(3, 0, [P, HALF], F32, "sums1_0"))
        quantise_values(2, on_values(3, 1, [P, P], U32, "v_codes2"))
        scatter(1, 0, "vector")
        group_values(3, "scalar")
        scatter(1, 1, "scalar")
        store(1)
        multiply(2, 0, 2, "vector", sums_tile(2, 0))
        quantise_values(3, tile([P, P], U32, "v_codes3"))
        scatter(2, 0, "vector")
        multiply(2, 1, 3, "scalar", sums_tile(2, 1))
        scatter(2, 1, "scalar")
        store(2)
        multiply(3, 0, 6, "vector", sums_tile(3, 0))
        scatter(3, 0, "vector")
        multiply(3, 1, 3, "scalar", sums_tile(3, 1))
        scatter(3, 1, "scalar")
        store(3)
